import numpy as np
import ml_dtypes


def mxq(x, axis, fmt="e4m3"):
    dtype, down = {"e4m3": (ml_dtypes.float8_e4m3fn, 7), "e5m2": (ml_dtypes.float8_e5m2, 14)}[fmt]
    v = np.moveaxis(np.asarray(x, np.float32).astype(ml_dtypes.bfloat16).astype(np.float64), axis, -1)
    blocks = v.reshape(v.shape[:-1] + (-1, 32))
    amax = np.abs(blocks).max(-1, keepdims=True)
    byte = np.maximum(np.where(amax > 0, np.frexp(amax)[1] - 1 + 127, 0) - down, 1)
    scale = np.exp2(byte - 127.0)
    codes = (blocks / scale).astype(np.float32).astype(dtype).astype(np.float64)
    return np.moveaxis((codes * scale).reshape(v.shape), -1, axis)


WIDE = False


def mx_kscale(k):
    if not WIDE:
        return np.ones(k)
    levels = np.array([24, -24, 12, -12, 0])
    if k % 512:
        return np.exp2(np.random.permutation(np.resize(levels, k // 32))).repeat(32)
    a = np.empty((k // 512, 16))
    for p in range(k // 512):
        a[p, :8] = np.random.permutation(np.resize(levels, 8))
        for g in range(8):
            far = levels[np.abs(levels - a[p, g]) >= 10]
            a[p, g + 8] = far[np.random.randint(len(far))]
    return np.exp2(a.ravel()).repeat(32)


def f64(x):
    return np.asarray(x).astype(np.float64)


def striped(idx):
    return np.tile(idx.reshape(-1, 16).T, (8, 1)).astype(np.uint16)


def unstriped(offs):
    return offs[:16].T.reshape(-1).astype(np.int64)


E2M1 = np.array([0.0, 0.5, 1.0, 1.5, 2.0, 3.0, 4.0, 6.0, -0.0, -0.5, -1.0, -1.5, -2.0, -3.0, -4.0, -6.0])


def pack_weight(w, fmt):
    k, n = w.shape
    w = f64(np.asarray(w, np.float32).astype(ml_dtypes.bfloat16)).reshape(k // 32, 32, n)
    amax = np.abs(w).max(1)
    if fmt == "e4m3":
        byte = np.frexp(amax)[1] - 1 + 127 - 7
    else:
        mant, ex = np.frexp(amax / 6.0)
        byte = np.where(mant > 0.5, ex, ex - 1) + 127
    byte = np.clip(np.where(amax > 0, byte, 1), 1, 254)
    scaled = (w * np.exp2(127.0 - byte)[:, None, :]).reshape(k, n).astype(np.float32)
    by_word = np.ascontiguousarray(scaled.reshape(k // 512, 128, 4, n).transpose(0, 1, 3, 2))
    if fmt == "e4m3":
        words = by_word.astype(ml_dtypes.float8_e4m3fn).view(np.uint8)
    else:
        c = by_word.astype(ml_dtypes.float4_e2m1fn).view(np.uint8) & 0xF
        words = (c[..., 0::2] | (c[..., 1::2] << 4)).reshape(k // 512, 128, 2 * n)
    return np.ascontiguousarray(words), np.ascontiguousarray(byte.astype(np.uint8).reshape(k // 512, 16, n))


def unpack_weight(words, scales, fmt):
    g, _, n = scales.shape
    words = np.ascontiguousarray(words).reshape(g, 128, n, -1)
    if fmt == "e4m3":
        vals = words.view(ml_dtypes.float8_e4m3fn).astype(np.float64)
    else:
        nib = np.empty((g, 128, n, 4), np.uint8)
        nib[..., 0::2] = words & 0xF
        nib[..., 1::2] = words >> 4
        vals = E2M1[nib]
    vals = vals * np.repeat(np.exp2(scales.astype(np.float64) - 127.0), 8, axis=1)[..., None]
    return vals.transpose(0, 1, 3, 2).reshape(g * 512, n)


K, R, N, T, J = 512, 1024, 256, 4096, 512


def setup_inputs():
    n = np.random.standard_normal
    s = mx_kscale(K)[:, None]
    u = mx_kscale(R)[:, None]
    wd = n((R, N)) / np.sqrt(R) / u
    p_tab = pack_weight(n((K, T)) * s, "e4m3")
    p_wc = pack_weight(n((K, R)) / np.sqrt(K) / s * u.T, "e2m1")
    p_wd8 = pack_weight(wd[:512], "e4m3")
    p_wd4 = pack_weight(wd[512:], "e2m1")
    return {
        "tab_words": p_tab[0],
        "tab_scales": p_tab[1],
        "c": (n((K, J)) * s).astype(np.float32),
        "w": (n((K, R)) / np.sqrt(K) / s * u.T).astype(np.float32),
        "wc_words": p_wc[0],
        "wc_scales": p_wc[1],
        "wd8_words": p_wd8[0],
        "wd8_scales": p_wd8[1],
        "wd4_words": p_wd4[0],
        "wd4_scales": p_wd4[1],
        "res": (n((N, J))).astype(np.float32),
        "offs": striped(np.concatenate([np.random.permutation(T)[:J] for _ in range(4)])),
    }


def reference(tab_words, tab_scales, c, w, wc_words, wc_scales, wd8_words, wd8_scales, wd4_words, wd4_scales, res, offs):
    idx = unstriped(offs).reshape(4, J)
    tab_ = unpack_weight(tab_words, tab_scales, "e4m3")[:, idx]
    c_ = mxq(f64(c), 0, "e4m3")
    w_ = mxq(f64(w), 0, "e4m3")
    a0 = w_.T @ tab_[:, 0]
    a1 = w_.T @ tab_[:, 1]
    a2 = w_.T @ tab_[:, 2]
    a3 = w_.T @ tab_[:, 3]
    wc_ = unpack_weight(wc_words, wc_scales, "e2m1")
    ac = wc_.T @ c_
    h = np.maximum(np.maximum(np.maximum(np.maximum(a0, a1), a2), a3) + ac, 0.0)
    h_ = mxq(h, 0, "e4m3")
    wd8_ = unpack_weight(wd8_words, wd8_scales, "e4m3")
    wd4_ = unpack_weight(wd4_words, wd4_scales, "e2m1")
    y = wd8_.T @ h_[:512] + wd4_.T @ h_[512:]
    return f64(res) + y

@@ -1,0 +1,346 @@
+from contextlib import ExitStack
+
+import concourse.mybir as mybir
+from concourse.masks import make_identity
+
+K, R, N, T, J, G = 512, 1024, 256, 4096, 512, 4
+FLOPS = 2 * K * R * J * (G + 1) + 2 * R * N * J
+
+F32 = mybir.dt.float32
+BF16 = mybir.dt.bfloat16
+I32 = mybir.dt.int32
+U32 = mybir.dt.uint32
+U16 = mybir.dt.uint16
+U8 = mybir.dt.uint8
+E4 = mybir.dt.float8_e4m3fn_x4
+E2 = mybir.dt.float4_e2m1fn_x4
+ALU = mybir.AluOpType
+ACT = mybir.ActivationFunctionType
+
+P = 128
+HALF = 512
+PE_ADD_UNITS = (3, 4, 6, 7)
+DMA_ORDER = "w0 c0 w1 c1 r w3 w2 x"
+C_ON_G = ()
+SPLIT = ((0, 0), (1, 0), (0, 1), (1, 1), (2, 0), (3, 0))
+ORDER = (
+    ("n", 0, 0),
+    ("n", 1, 0),
+    ("n", 0, 1),
+    ("n", 1, 1),
+    ("n", 3, 0),
+    ("cw", 3),
+    ("cc", 0),
+    ("n", 0, 2),
+    ("n", 2, 0),
+    ("qc", 0),
+    ("cw", 2),
+    ("n", 1, 2),
+    ("o", 0),
+    ("n", 1, 3),
+    ("n", 0, 3),
+    ("o", 1),
+    ("cc", 1),
+    ("qc", 1),
+    ("o", 2),
+    ("qw", 2),
+    ("n", 3, 1),
+    ("qw", 3),
+    ("o", 3),
+    ("n", 2, 1),
+    ("n", 2, 2),
+    ("n", 3, 2),
+    ("a", 1),
+    ("n", 4, 0),
+    ("n", 5, 0),
+    ("n", 2, 3),
+    ("n", 3, 3),
+    ("a", 0),
+    ("o", 4),
+    ("a", 2),
+    ("a", 3),
+    ("o", 5),
+    ("t", 0),
+    ("n", 4, 1),
+    ("n", 5, 1),
+    ("t", 1),
+    ("n", 4, 2),
+    ("n", 5, 2),
+    ("n", 7, 0),
+    ("n", 4, 3),
+    ("o", 7),
+    ("n", 6, 0),
+    ("n", 5, 3),
+    ("q", 1),
+    ("n", 7, 1),
+    ("a", 4),
+    ("n", 6, 1),
+    ("t", 4),
+    ("t", 3),
+    ("t", 2),
+    ("q", 0),
+    ("q", 4),
+    ("a", 5),
+    ("n", 6, 2),
+    ("y", 0),
+    ("n", 6, 3),
+    ("o", 6),
+    ("t", 5),
+    ("n", 7, 2),
+    ("n", 7, 3),
+    ("a", 6),
+    ("t", 6),
+    ("q", 5),
+    ("a", 7),
+    ("q", 2),
+    ("t", 7),
+    ("y", 1),
+    ("q", 7),
+    ("q", 6),
+    ("q", 3),
+    ("y", 2),
+    ("y", 3),
+)
+
+
+def load_scale_rows(queue, plane, rows):
+    for r in range(4):
+        queue.dma_start(out=plane[r:P:32, :].bitcast(I32), in_=rows[r:16:4, :].bitcast(I32))
+
+
+def tile_list_pnet_mix_res_kernel(
+    tc, tab_words, tab_scales, c, w, wc_words, wc_scales, wd8_words, wd8_scales, wd4_words, wd4_scales, res, offs, out
+):
+    nc = tc.nc
+    with ExitStack() as ctx:
+        keep = ctx.enter_context(tc.tile_pool(name="keep", bufs=1))
+        reuse = ctx.enter_context(tc.tile_pool(name="reuse", bufs=1))
+        head = ctx.enter_context(tc.tile_pool(name="head", bufs=1))
+        late = ctx.enter_context(tc.tile_pool(name="late", bufs=1))
+        psum = ctx.enter_context(tc.psum_pool(name="psum", bufs=1))
+
+        w_k = w.rearrange("(p i) r -> p i r", i=4)
+
+        offsets = keep.tile([P, G * J // 16], U16, name="offsets")
+        nc.sync.dma_start(offsets[:], offs)
+
+        table_s = head.tile([P, T], U8, name="table_s", align_bytes=64, offset=0)
+        nc.vector.memset(table_s[:].bitcast(I32), 0)
+        wd = keep.tile([P, 4 * N + 2 * N + 2 * N], U8, name="wd", align_bytes=64)
+        wd8_w, wd4_w = wd[:, 0 : 4 * N], wd[:, 4 * N : 6 * N]
+        wd8_s, wd4_s = wd[:, 6 * N : 7 * N], wd[:, 7 * N : 8 * N]
+        nc.vector.memset(wd[:, 6 * N :].bitcast(I32), 0)
+        wc_s = keep.tile([P, R], U8, name="wc_s", align_bytes=64)
+        nc.gpsimd.memset(wc_s[:].bitcast(I32), 0)
+        load_scale_rows(nc.gpsimd, wc_s, wc_scales[0])
+        wc_w = keep.tile([P, 2 * R], U8, name="wc_w", align_bytes=64)
+        nc.sync.dma_start(out=wc_w[:].bitcast(I32), in_=wc_words[0].bitcast(I32))
+        nc.sync.dma_start(out=wd4_w.bitcast(I32), in_=wd4_words[0].bitcast(I32))
+        load_scale_rows(nc.sync, table_s, tab_scales[0])
+        table_w = late.tile([P, T], I32, name="table_w", align_bytes=64, offset=0)
+        nc.sync.dma_start(out=table_w[:], in_=tab_words[0].rearrange("p t i -> p (t i)").bitcast(I32))
+        c_k = c.rearrange("(p i) j -> p i j", i=4)
+        c_raw = [keep.tile([P, 4, 256], F32, name=f"c_raw{q}", align_bytes=64) for q in range(2)]
+        w_raw = [keep.tile([P, 4, 256], F32, name=f"w_raw{q}", align_bytes=64) for q in range(4)]
+        res_sb = keep.tile([P, 2, J], F32, name="res_sb", align_bytes=64)
+        for step in DMA_ORDER.split():
+            if step[0] == "c":
+                q = int(step[1])
+                nc.sync.dma_start(out=c_raw[q][:], in_=c_k[:, :, 256 * q : 256 * (q + 1)])
+            if step[0] == "w":
+                q = int(step[1])
+                nc.sync.dma_start(out=w_raw[q][:], in_=w_k[:, :, 256 * q : 256 * (q + 1)])
+            if step == "x":
+                nc.sync.dma_start(out=wd8_w.bitcast(I32), in_=wd8_words[0].rearrange("p n i -> p (n i)").bitcast(I32))
+            if step == "r":
+                nc.sync.dma_start(out=res_sb[:], in_=res.rearrange("(a p) j -> p a j", p=P))
+        load_scale_rows(nc.sync, wd8_s, wd8_scales[0])
+        load_scale_rows(nc.sync, wd4_s, wd4_scales[0])
+
+        ident = keep.tile([P, P], F32, name="ident", align_bytes=64)
+        make_identity(nc, ident[:])
+
+        used_banks = []
+
+        def next_bank(shape):
+            used_banks.append(shape)
+            return psum.tile(shape, F32, name="bank", tag=f"bank{len(used_banks) % 8}")
+
+        picked_s = [keep.tile([P, J], U8, name=f"picked_s{g}", align_bytes=64) for g in range(G)]
+
+        def list_of(g):
+            return offsets[:, g * (J // 16) : (g + 1) * (J // 16)]
+
+        def gather_scales(g):
+            nc.vector.tensor_copy(picked_s[g][:], table_s[:].indirect(list_of(g)))
+
+        for g in range(G):
+            gather_scales(g)
+        picked_early = head.tile([P, 2, J], I32, name="picked_early", align_bytes=64, offset=R)
+        picked_w = [picked_early[:, 0, :], picked_early[:, 1, :]]
+
+        def gather_words(g):
+            nc.vector.tensor_copy(picked_w[g][:, :].bitcast(U32), table_w[:].bitcast(U32).indirect(list_of(g)))
+
+        w_codes = [keep.tile([P, HALF], U32, name=f"w_codes{h}", align_bytes=64) for h in range(2)]
+        w_sc = [keep.tile([P, HALF], U8, name=f"w_sc{h}", align_bytes=64) for h in range(2)]
+
+        w_bf = [
+            reuse.tile([P, 4, 64, 4], BF16, name="w_bf0", tag="slot_d", align_bytes=64),
+            reuse.tile([P, 4, 64, 4], BF16, name="w_bf1", tag="slot_e", align_bytes=64),
+            keep.tile([P, 4, 64, 4], BF16, name="w_bf2", align_bytes=64),
+            keep.tile([P, 4, 64, 4], BF16, name="w_bf3", align_bytes=64),
+        ]
+
+        def cast_w(q):
+            nc.scalar.copy(
+                w_bf[q][:].rearrange("p t m i -> p m i t"),
+                w_raw[q][:].rearrange("p i (m t) -> p m i t", t=4),
+            )
+
+        def quantize_w(q):
+            cols = slice(256 * (q % 2), 256 * (q % 2 + 1))
+            nc.vector.quantize_mx(
+                out=w_codes[q // 2][:, cols].bitcast(E4),
+                scales=w_sc[q // 2][:, cols],
+                in_=w_bf[q][:].rearrange("p t m i -> p (t m i)"),
+            )
+
+        gather_words(0)
+        gather_words(1)
+        cast_w(0)
+        quantize_w(0)
+        picked_w.append(reuse.tile([P, J], I32, name="picked_w2", tag="slot_d", align_bytes=64))
+        gather_words(2)
+        cast_w(1)
+        quantize_w(1)
+        picked_w.append(reuse.tile([P, J], I32, name="picked_w3", tag="slot_e", align_bytes=64))
+        gather_words(3)
+
+        c_codes = keep.tile([P, J], U32, name="c_codes", align_bytes=64)
+        c_sc = keep.tile([P, J], U8, name="c_sc", align_bytes=64)
+        c_bf = [
+            late.tile([P, 256, 4], BF16, name=f"c_bf{q}", align_bytes=64, offset=(2048 * q if q in C_ON_G else 4 * T + 2048 * q))
+            for q in range(2)
+        ]
+
+        def cast_c(q):
+            if q not in C_ON_G:
+                nc.scalar.copy(
+                    c_bf[q][:].rearrange("p (a b) i -> p a i b", b=4),
+                    c_raw[q][:].rearrange("p i (a b) -> p a i b", b=4),
+                )
+            else:
+                nc.gpsimd.tensor_scalar(c_bf[q][:], c_raw[q][:].rearrange("p i j -> p j i"), 1.0, 0.0, ALU.mult, ALU.add)
+
+        def quantize_c(q):
+            nc.vector.quantize_mx(
+                out=c_codes[:, 256 * q : 256 * (q + 1)].bitcast(E4),
+                scales=c_sc[:, 256 * q : 256 * (q + 1)],
+                in_=c_bf[q][:].rearrange("p j i -> p (j i)"),
+            )
+
+        best = [keep.tile([P, 4, P], F32, name=f"best{u}", align_bytes=64) for u in range(8)]
+        own = [keep.tile([P, 4, P], F32, name=f"own{u}", align_bytes=64) for u in range(8)]
+        h_bf = [keep.tile([P, P, 4], BF16, name=f"h_bf{u}", align_bytes=64) for u in range(8)]
+        h_codes = [keep.tile([P, P], U32, name=f"h_codes{u}", align_bytes=64) for u in range(8)]
+        h_sc = [keep.tile([P, P], U8, name=f"h_sc{u}", align_bytes=64) for u in range(8)]
+
+        def neighbour(u, g):
+            h, cols = u // 4, slice(u % 4 * P, (u % 4 + 1) * P)
+            bank = next_bank([P, HALF])
+            width = 256 if (u, g) in SPLIT else HALF
+            for r0 in range(0, HALF, width):
+                nc.tensor.matmul_mx(
+                    out=bank[:, r0 : r0 + width],
+                    lhsT=picked_w[g][:, cols].bitcast(E4),
+                    lhsT_scale=picked_s[g][:, cols],
+                    rhs=w_codes[h][:, r0 : r0 + width].bitcast(E4),
+                    rhs_scale=w_sc[h][:, r0 : r0 + width],
+                    start=True,
+                    stop=True,
+                )
+            held = best[u][:].rearrange("j t (q m) -> j q t m", q=2)
+            sums = bank[:].rearrange("j (q t m) -> j q t m", q=2, t=4)
+            if g == 0:
+                nc.scalar.copy(held, sums)
+            else:
+                nc.vector.tensor_tensor(held, sums, held, ALU.max)
+
+        def own_part(u):
+            h, cols = u // 4, slice(u % 4 * P, (u % 4 + 1) * P)
+            bank = next_bank([P, HALF])
+            nc.tensor.matmul_mx(
+                out=bank[:],
+                lhsT=c_codes[:, cols].bitcast(E4),
+                lhsT_scale=c_sc[:, cols],
+                rhs=wc_w[:, 2 * HALF * h : 2 * HALF * (h + 1)].bitcast(E2),
+                rhs_scale=wc_s[:, HALF * h : HALF * (h + 1)],
+                start=True,
+                stop=True,
+            )
+            nc.scalar.copy(own[u][:].rearrange("j t m -> j m t"), bank[:].rearrange("j (m t) -> j m t", t=4))
+
+        def add_own(u):
+            if u not in PE_ADD_UNITS:
+                nc.gpsimd.tensor_tensor(best[u][:], best[u][:], own[u][:], ALU.add)
+
+        def turn(u):
+            turned = next_bank([P, 4, P])
+            if u in PE_ADD_UNITS:
+                for t in range(4):
+                    nc.tensor.matmul(turned[:, t, :], own[u][:, t, :], ident[:], start=(t == 0), stop=False, is_transpose=True)
+                for t in range(4):
+                    nc.tensor.matmul(turned[:, t, :], best[u][:, t, :], ident[:], start=False, stop=(t == 3), is_transpose=True)
+            else:
+                for t in range(4):
+                    nc.tensor.transpose(turned[:, t, :], best[u][:, t, :], ident[:])
+            nc.scalar.activation(h_bf[u][:], turned[:].rearrange("p t j -> p j t"), ACT.Relu)
+
+        def quantize_h(u):
+            nc.vector.quantize_mx(
+                out=h_codes[u][:].bitcast(E4), scales=h_sc[u][:], in_=h_bf[u][:].rearrange("p j t -> p (j t)")
+            )
+
+        out_v = out.rearrange("(a p) j -> p a j", p=P)
+
+        def second_layer(jt):
+            y = next_bank([P, 2, P])
+            for a in range(2):
+                nc.tensor.matmul_mx(
+                    out=y[:, a, :],
+                    lhsT=wd8_w[:, 4 * P * a : 4 * P * (a + 1)].bitcast(E4),
+                    lhsT_scale=wd8_s[:, P * a : P * (a + 1)],
+                    rhs=h_codes[jt][:].bitcast(E4),
+                    rhs_scale=h_sc[jt][:],
+                    start=True,
+                    stop=False,
+                )
+                nc.tensor.matmul_mx(
+                    out=y[:, a, :],
+                    lhsT=wd4_w[:, 2 * P * a : 2 * P * (a + 1)].bitcast(E2),
+                    lhsT_scale=wd4_s[:, P * a : P * (a + 1)],
+                    rhs=h_codes[4 + jt][:].bitcast(E4),
+                    rhs_scale=h_sc[4 + jt][:],
+                    start=False,
+                    stop=True,
+                )
+            cols = slice(jt * P, (jt + 1) * P)
+            o = keep.tile([P, 2, P], F32, name=f"o{jt}", align_bytes=64)
+            nc.vector.tensor_tensor(o[:], y[:], res_sb[:, :, cols], ALU.add)
+            nc.sync.dma_start(out=out_v[:, :, cols], in_=o[:])
+
+        steps = {
+            "n": neighbour,
+            "o": own_part,
+            "a": add_own,
+            "t": turn,
+            "q": quantize_h,
+            "y": second_layer,
+            "cc": cast_c,
+            "qc": quantize_c,
+            "cw": cast_w,
+            "qw": quantize_w,
+        }
+        for step in ORDER:
+            steps[step[0]](*step[1:])

@@ -1,7 +1,6 @@
 from contextlib import ExitStack
 
 import concourse.mybir as mybir
-from concourse.masks import make_identity
 
 K, R, N, T, J, G = 512, 1024, 256, 4096, 512, 4
 FLOPS = 2 * K * R * J * (G + 1) + 2 * R * N * J
@@ -19,87 +18,96 @@ ACT = mybir.ActivationFunctionType
 
 P = 128
 HALF = 512
-PE_ADD_UNITS = (3, 4, 6, 7)
-DMA_ORDER = "w0 c0 w1 c1 r w3 w2 x"
-C_ON_G = ()
-SPLIT = ((0, 0), (1, 0), (0, 1), (1, 1), (2, 0), (3, 0))
+FOLD = 7
+PE_ADD_UNITS = (6, 7)
+DMA_ORDER = "V T W C r x"
+C_ON_G = (0,)
+C_GATE = 1
+Y_EARLY = (3,)
+Y_ON_G = ()
+LATE = 3
+SPLIT = ()
 ORDER = (
-    ("n", 0, 0),
     ("n", 1, 0),
-    ("n", 0, 1),
-    ("n", 1, 1),
-    ("n", 3, 0),
-    ("cw", 3),
     ("cc", 0),
-    ("n", 0, 2),
+    ("n", 0, 0),
+    ("cw", 3),
     ("n", 2, 0),
     ("qc", 0),
+    ("n", 0, 1),
     ("cw", 2),
-    ("n", 1, 2),
-    ("o", 0),
-    ("n", 1, 3),
-    ("n", 0, 3),
-    ("o", 1),
-    ("cc", 1),
-    ("qc", 1),
-    ("o", 2),
-    ("qw", 2),
-    ("n", 3, 1),
     ("qw", 3),
-    ("o", 3),
+    ("cc", 1),
+    ("n", 0, 2),
+    ("n", 3, 0),
     ("n", 2, 1),
+    ("n", 3, 1),
+    ("n", 1, 1),
+    ("qw", 2),
+    ("n", 1, 2),
+    ("qc", 1),
     ("n", 2, 2),
-    ("n", 3, 2),
-    ("a", 1),
     ("n", 4, 0),
-    ("n", 5, 0),
-    ("n", 2, 3),
-    ("n", 3, 3),
-    ("a", 0),
-    ("o", 4),
-    ("a", 2),
-    ("a", 3),
+    ("o", 0),
+    ("n", 0, 3),
+    ("n", 3, 2),
     ("o", 5),
-    ("t", 0),
+    ("a", 0),
+    ("n", 1, 3),
+    ("n", 2, 3),
+    ("o", 2),
+    ("o", 1),
+    ("n", 5, 0),
     ("n", 4, 1),
-    ("n", 5, 1),
-    ("t", 1),
+    ("t", 0),
+    ("n", 3, 3),
     ("n", 4, 2),
-    ("n", 5, 2),
-    ("n", 7, 0),
-    ("n", 4, 3),
-    ("o", 7),
+    ("o", 6),
+    ("o", 3),
+    ("n", 5, 1),
     ("n", 6, 0),
-    ("n", 5, 3),
-    ("q", 1),
-    ("n", 7, 1),
-    ("a", 4),
+    ("n", 5, 2),
+    ("a", 2),
     ("n", 6, 1),
-    ("t", 4),
+    ("n", 4, 3),
+    ("a", 1),
+    ("o", 4),
+    ("n", 7, 0),
+    ("a", 4),
+    ("n", 5, 3),
+    ("a", 3),
+    ("n", 6, 2),
+    ("n", 7, 1),
+    ("n", 6, 3),
+    ("n", 7, 2),
+    ("t", 1),
     ("t", 3),
-    ("t", 2),
+    ("t", 4),
+    ("a", 6),
+    ("q", 3),
+    ("o", 7),
     ("q", 0),
     ("q", 4),
+    ("f", 3),
+    ("q", 1),
+    ("t", 2),
     ("a", 5),
-    ("n", 6, 2),
-    ("y", 0),
-    ("n", 6, 3),
-    ("o", 6),
-    ("t", 5),
-    ("n", 7, 2),
     ("n", 7, 3),
-    ("a", 6),
-    ("t", 6),
+    ("t", 5),
     ("q", 5),
     ("a", 7),
     ("q", 2),
+    ("t", 6),
+    ("f", 0),
     ("t", 7),
-    ("y", 1),
     ("q", 7),
+    ("y", 0),
     ("q", 6),
-    ("q", 3),
-    ("y", 2),
+    ("f", 1),
+    ("f", 2),
+    ("y", 1),
     ("y", 3),
+    ("y", 2),
 )
 
 
@@ -124,41 +132,60 @@ def tile_list_pnet_mix_res_kernel(
         offsets = keep.tile([P, G * J // 16], U16, name="offsets")
         nc.sync.dma_start(offsets[:], offs)
 
+        wc_s = keep.tile([P, R], U8, name="wc_s", align_bytes=64)
+        nc.vector.memset(wc_s[:].bitcast(I32), 0)
         table_s = head.tile([P, T], U8, name="table_s", align_bytes=64, offset=0)
         nc.vector.memset(table_s[:].bitcast(I32), 0)
         wd = keep.tile([P, 4 * N + 2 * N + 2 * N], U8, name="wd", align_bytes=64)
         wd8_w, wd4_w = wd[:, 0 : 4 * N], wd[:, 4 * N : 6 * N]
         wd8_s, wd4_s = wd[:, 6 * N : 7 * N], wd[:, 7 * N : 8 * N]
         nc.vector.memset(wd[:, 6 * N :].bitcast(I32), 0)
-        wc_s = keep.tile([P, R], U8, name="wc_s", align_bytes=64)
-        nc.gpsimd.memset(wc_s[:].bitcast(I32), 0)
-        load_scale_rows(nc.gpsimd, wc_s, wc_scales[0])
         wc_w = keep.tile([P, 2 * R], U8, name="wc_w", align_bytes=64)
         nc.sync.dma_start(out=wc_w[:].bitcast(I32), in_=wc_words[0].bitcast(I32))
-        nc.sync.dma_start(out=wd4_w.bitcast(I32), in_=wd4_words[0].bitcast(I32))
+        load_scale_rows(nc.sync, wc_s, wc_scales[0])
         load_scale_rows(nc.sync, table_s, tab_scales[0])
         table_w = late.tile([P, T], I32, name="table_w", align_bytes=64, offset=0)
-        nc.sync.dma_start(out=table_w[:], in_=tab_words[0].rearrange("p t i -> p (t i)").bitcast(I32))
         c_k = c.rearrange("(p i) j -> p i j", i=4)
-        c_raw = [keep.tile([P, 4, 256], F32, name=f"c_raw{q}", align_bytes=64) for q in range(2)]
-        w_raw = [keep.tile([P, 4, 256], F32, name=f"w_raw{q}", align_bytes=64) for q in range(4)]
+        def halves(name, whole):
+            if whole:
+                both = keep.tile([P, 4, 512], F32, name=name, align_bytes=64)
+                return both, [both[:, :, 0:256], both[:, :, 256:512]]
+            return None, [keep.tile([P, 4, 256], F32, name=f"{name}{q}", align_bytes=64)[:] for q in range(2)]
+
+        c_all, c_raw = halves("c_raw", "C" in DMA_ORDER)
+        w_zero, w_first = halves("w_first", "V" in DMA_ORDER)
+        w_second, w_last = halves("w_second", "W" in DMA_ORDER)
+        w_raw = w_first + w_last
         res_sb = keep.tile([P, 2, J], F32, name="res_sb", align_bytes=64)
         for step in DMA_ORDER.split():
             if step[0] == "c":
                 q = int(step[1])
-                nc.sync.dma_start(out=c_raw[q][:], in_=c_k[:, :, 256 * q : 256 * (q + 1)])
+                nc.sync.dma_start(out=c_raw[q], in_=c_k[:, :, 256 * q : 256 * (q + 1)])
             if step[0] == "w":
                 q = int(step[1])
-                nc.sync.dma_start(out=w_raw[q][:], in_=w_k[:, :, 256 * q : 256 * (q + 1)])
+                nc.sync.dma_start(out=w_raw[q], in_=w_k[:, :, 256 * q : 256 * (q + 1)])
+            if step == "C":
+                nc.sync.dma_start(out=c_all[:], in_=c_k)
+            if step == "W":
+                nc.sync.dma_start(out=w_second[:], in_=w_k[:, :, HALF:R])
+            if step == "T":
+                nc.sync.dma_start(out=table_w[:], in_=tab_words[0].rearrange("p t i -> p (t i)").bitcast(I32))
+            if step == "V":
+                nc.sync.dma_start(out=w_zero[:], in_=w_k[:, :, 0:HALF])
             if step == "x":
+                nc.sync.dma_start(out=wd4_w.bitcast(I32), in_=wd4_words[0].bitcast(I32))
                 nc.sync.dma_start(out=wd8_w.bitcast(I32), in_=wd8_words[0].rearrange("p n i -> p (n i)").bitcast(I32))
             if step == "r":
                 nc.sync.dma_start(out=res_sb[:], in_=res.rearrange("(a p) j -> p a j", p=P))
         load_scale_rows(nc.sync, wd8_s, wd8_scales[0])
         load_scale_rows(nc.sync, wd4_s, wd4_scales[0])
 
-        ident = keep.tile([P, P], F32, name="ident", align_bytes=64)
-        make_identity(nc, ident[:])
+        wcp_w = keep.tile([P, 2 * R], U8, name="wcp_w", align_bytes=64)
+        for h in range(2):
+            nc.vector.tensor_copy(
+                wcp_w[:, 2 * HALF * h : 2 * HALF * (h + 1)].rearrange("p (t m b) -> p m t b", t=4, b=2),
+                wc_w[:, 2 * HALF * h : 2 * HALF * (h + 1)].rearrange("p (m t b) -> p m t b", t=4, b=2),
+            )
 
         used_banks = []
 
@@ -178,6 +205,11 @@ def tile_list_pnet_mix_res_kernel(
             gather_scales(g)
         picked_early = head.tile([P, 2, J], I32, name="picked_early", align_bytes=64, offset=R)
         picked_w = [picked_early[:, 0, :], picked_early[:, 1, :]]
+        wcp_s = keep.tile([P, R], U8, name="wcp_s", align_bytes=64)
+        nc.vector.tensor_copy(
+            wcp_s[:].rearrange("p (h t m) -> p h m t", h=2, t=4),
+            wc_s[:].rearrange("p (h m t) -> p h m t", h=2, t=4),
+        )
 
         def gather_words(g):
             nc.vector.tensor_copy(picked_w[g][:, :].bitcast(U32), table_w[:].bitcast(U32).indirect(list_of(g)))
@@ -186,41 +218,38 @@ def tile_list_pnet_mix_res_kernel(
         w_sc = [keep.tile([P, HALF], U8, name=f"w_sc{h}", align_bytes=64) for h in range(2)]
 
         w_bf = [
-            reuse.tile([P, 4, 64, 4], BF16, name="w_bf0", tag="slot_d", align_bytes=64),
-            reuse.tile([P, 4, 64, 4], BF16, name="w_bf1", tag="slot_e", align_bytes=64),
-            keep.tile([P, 4, 64, 4], BF16, name="w_bf2", align_bytes=64),
-            keep.tile([P, 4, 64, 4], BF16, name="w_bf3", align_bytes=64),
+            reuse.tile([P, 4, P, 4], BF16, name="w_bf0", tag="slot_d", align_bytes=64),
+            keep.tile([P, 4, P, 4], BF16, name="w_bf1", align_bytes=64),
         ]
 
         def cast_w(q):
             nc.scalar.copy(
-                w_bf[q][:].rearrange("p t m i -> p m i t"),
-                w_raw[q][:].rearrange("p i (m t) -> p m i t", t=4),
+                w_bf[q // 2][:, :, 64 * (q % 2) : 64 * (q % 2 + 1), :].rearrange("p t m i -> p m i t"),
+                w_raw[q].rearrange("p i (m t) -> p m i t", t=4),
             )
 
-        def quantize_w(q):
-            cols = slice(256 * (q % 2), 256 * (q % 2 + 1))
+        def quantize_w(h):
             nc.vector.quantize_mx(
-                out=w_codes[q // 2][:, cols].bitcast(E4),
-                scales=w_sc[q // 2][:, cols],
-                in_=w_bf[q][:].rearrange("p t m i -> p (t m i)"),
+                out=w_codes[h][:].bitcast(E4), scales=w_sc[h][:], in_=w_bf[h][:].rearrange("p t m i -> p (t m i)")
             )
 
-        gather_words(0)
-        gather_words(1)
+        for g in range(2, LATE):
+            picked_w.append(keep.tile([P, J], I32, name=f"picked_w{g}", align_bytes=64))
+        for g in range(LATE):
+            gather_words(g)
         cast_w(0)
-        quantize_w(0)
-        picked_w.append(reuse.tile([P, J], I32, name="picked_w2", tag="slot_d", align_bytes=64))
-        gather_words(2)
         cast_w(1)
-        quantize_w(1)
-        picked_w.append(reuse.tile([P, J], I32, name="picked_w3", tag="slot_e", align_bytes=64))
-        gather_words(3)
+        quantize_w(0)
+        if LATE < G:
+            picked_late = reuse.tile([P, G - LATE, J], I32, name="picked_late", tag="slot_d", align_bytes=64)
+            for g in range(LATE, G):
+                picked_w.append(picked_late[:, g - LATE, :])
+                gather_words(g)
 
         c_codes = keep.tile([P, J], U32, name="c_codes", align_bytes=64)
         c_sc = keep.tile([P, J], U8, name="c_sc", align_bytes=64)
         c_bf = [
-            late.tile([P, 256, 4], BF16, name=f"c_bf{q}", align_bytes=64, offset=(2048 * q if q in C_ON_G else 4 * T + 2048 * q))
+            late.tile([P, 256, 4], BF16, name=f"c_bf{q}", align_bytes=64, offset=(2048 * q if (q in C_ON_G and C_GATE) else 4 * T + 2048 * q))
             for q in range(2)
         ]
 
@@ -228,10 +257,10 @@ def tile_list_pnet_mix_res_kernel(
             if q not in C_ON_G:
                 nc.scalar.copy(
                     c_bf[q][:].rearrange("p (a b) i -> p a i b", b=4),
-                    c_raw[q][:].rearrange("p i (a b) -> p a i b", b=4),
+                    c_raw[q].rearrange("p i (a b) -> p a i b", b=4),
                 )
             else:
-                nc.gpsimd.tensor_scalar(c_bf[q][:], c_raw[q][:].rearrange("p i j -> p j i"), 1.0, 0.0, ALU.mult, ALU.add)
+                nc.gpsimd.tensor_scalar(c_bf[q][:], c_raw[q].rearrange("p i j -> p j i"), 1.0, 0.0, ALU.mult, ALU.add)
 
         def quantize_c(q):
             nc.vector.quantize_mx(
@@ -242,60 +271,69 @@ def tile_list_pnet_mix_res_kernel(
 
         best = [keep.tile([P, 4, P], F32, name=f"best{u}", align_bytes=64) for u in range(8)]
         own = [keep.tile([P, 4, P], F32, name=f"own{u}", align_bytes=64) for u in range(8)]
+        pre = [keep.tile([P, 4, P], BF16, name=f"pre{u}", align_bytes=64) for u in range(8)]
         h_bf = [keep.tile([P, P, 4], BF16, name=f"h_bf{u}", align_bytes=64) for u in range(8)]
         h_codes = [keep.tile([P, P], U32, name=f"h_codes{u}", align_bytes=64) for u in range(8)]
         h_sc = [keep.tile([P, P], U8, name=f"h_sc{u}", align_bytes=64) for u in range(8)]
 
-        def neighbour(u, g):
+        def own_pass(bank, u, t, start):
             h, cols = u // 4, slice(u % 4 * P, (u % 4 + 1) * P)
-            bank = next_bank([P, HALF])
-            width = 256 if (u, g) in SPLIT else HALF
-            for r0 in range(0, HALF, width):
-                nc.tensor.matmul_mx(
-                    out=bank[:, r0 : r0 + width],
-                    lhsT=picked_w[g][:, cols].bitcast(E4),
-                    lhsT_scale=picked_s[g][:, cols],
-                    rhs=w_codes[h][:, r0 : r0 + width].bitcast(E4),
-                    rhs_scale=w_sc[h][:, r0 : r0 + width],
-                    start=True,
-                    stop=True,
-                )
-            held = best[u][:].rearrange("j t (q m) -> j q t m", q=2)
-            sums = bank[:].rearrange("j (q t m) -> j q t m", q=2, t=4)
-            if g == 0:
-                nc.scalar.copy(held, sums)
-            else:
-                nc.vector.tensor_tensor(held, sums, held, ALU.max)
-
-        def own_part(u):
-            h, cols = u // 4, slice(u % 4 * P, (u % 4 + 1) * P)
-            bank = next_bank([P, HALF])
+            r0 = HALF * h + P * t
             nc.tensor.matmul_mx(
-                out=bank[:],
-                lhsT=c_codes[:, cols].bitcast(E4),
-                lhsT_scale=c_sc[:, cols],
-                rhs=wc_w[:, 2 * HALF * h : 2 * HALF * (h + 1)].bitcast(E2),
-                rhs_scale=wc_s[:, HALF * h : HALF * (h + 1)],
-                start=True,
+                out=bank[:, t, :],
+                lhsT=wcp_w[:, 2 * r0 : 2 * (r0 + P)].bitcast(E2),
+                lhsT_scale=wcp_s[:, r0 : r0 + P],
+                rhs=c_codes[:, cols].bitcast(E4),
+                rhs_scale=c_sc[:, cols],
+                start=start,
                 stop=True,
             )
-            nc.scalar.copy(own[u][:].rearrange("j t m -> j m t"), bank[:].rearrange("j (m t) -> j m t", t=4))
+
+        def neighbour(u, g):
+            h, cols = u // 4, slice(u % 4 * P, (u % 4 + 1) * P)
+            bank = next_bank([P, 4, P])
+            for t in range(4):
+                nc.tensor.matmul_mx(
+                    out=bank[:, t, :],
+                    lhsT=w_codes[h][:, P * t : P * (t + 1)].bitcast(E4),
+                    lhsT_scale=w_sc[h][:, P * t : P * (t + 1)],
+                    rhs=picked_w[g][:, cols].bitcast(E4),
+                    rhs_scale=picked_s[g][:, cols],
+                    start=True,
+                    stop=u != FOLD,
+                )
+                if u == FOLD:
+                    own_pass(bank, u, t, False)
+            if g == 0 and u == FOLD:
+                nc.scalar.activation(best[u][:], bank[:], ACT.Relu)
+            elif g == 0:
+                nc.scalar.copy(best[u][:], bank[:])
+            elif g == 3 and u == FOLD:
+                nc.vector.tensor_tensor(
+                    h_bf[u][:], bank[:].rearrange("p t j -> p j t"), best[u][:].rearrange("p t j -> p j t"), ALU.max
+                )
+            else:
+                nc.vector.tensor_tensor(best[u][:], bank[:], best[u][:], ALU.max)
+
+        def own_part(u):
+            if u != FOLD and u not in PE_ADD_UNITS:
+                bank = next_bank([P, 4, P])
+                for t in range(4):
+                    own_pass(bank, u, t, True)
+                nc.scalar.copy(own[u][:], bank[:])
 
         def add_own(u):
-            if u not in PE_ADD_UNITS:
-                nc.gpsimd.tensor_tensor(best[u][:], best[u][:], own[u][:], ALU.add)
+            if u != FOLD and u in PE_ADD_UNITS:
+                bank = next_bank([P, 4, P])
+                for t in range(4):
+                    own_pass(bank, u, t, True)
+                nc.vector.tensor_tensor(pre[u][:], bank[:], best[u][:], ALU.add)
+            elif u != FOLD:
+                nc.gpsimd.tensor_tensor(pre[u][:], best[u][:], own[u][:], ALU.add)
 
         def turn(u):
-            turned = next_bank([P, 4, P])
-            if u in PE_ADD_UNITS:
-                for t in range(4):
-                    nc.tensor.matmul(turned[:, t, :], own[u][:, t, :], ident[:], start=(t == 0), stop=False, is_transpose=True)
-                for t in range(4):
-                    nc.tensor.matmul(turned[:, t, :], best[u][:, t, :], ident[:], start=False, stop=(t == 3), is_transpose=True)
-            else:
-                for t in range(4):
-                    nc.tensor.transpose(turned[:, t, :], best[u][:, t, :], ident[:])
-            nc.scalar.activation(h_bf[u][:], turned[:].rearrange("p t j -> p j t"), ACT.Relu)
+            if u != FOLD:
+                nc.scalar.activation(h_bf[u][:], pre[u][:].rearrange("p t j -> p j t"), ACT.Relu)
 
         def quantize_h(u):
             nc.vector.quantize_mx(
@@ -304,30 +342,54 @@ def tile_list_pnet_mix_res_kernel(
 
         out_v = out.rearrange("(a p) j -> p a j", p=P)
 
+        opened = {}
+
+        def first_pass(y, jt, a):
+            nc.tensor.matmul_mx(
+                out=y,
+                lhsT=wd8_w[:, 4 * P * a : 4 * P * (a + 1)].bitcast(E4),
+                lhsT_scale=wd8_s[:, P * a : P * (a + 1)],
+                rhs=h_codes[jt][:].bitcast(E4),
+                rhs_scale=h_sc[jt][:],
+                start=True,
+                stop=False,
+            )
+
+        def second_pass(y, jt, a):
+            nc.tensor.matmul_mx(
+                out=y,
+                lhsT=wd4_w[:, 2 * P * a : 2 * P * (a + 1)].bitcast(E2),
+                lhsT_scale=wd4_s[:, P * a : P * (a + 1)],
+                rhs=h_codes[4 + jt][:].bitcast(E4),
+                rhs_scale=h_sc[4 + jt][:],
+                start=False,
+                stop=True,
+            )
+
+        def open_layer(jt):
+            if jt in Y_EARLY:
+                opened[jt] = [next_bank([P, P]), next_bank([P, P])]
+                for a in range(2):
+                    first_pass(opened[jt][a][:], jt, a)
+
         def second_layer(jt):
-            y = next_bank([P, 2, P])
-            for a in range(2):
-                nc.tensor.matmul_mx(
-                    out=y[:, a, :],
-                    lhsT=wd8_w[:, 4 * P * a : 4 * P * (a + 1)].bitcast(E4),
-                    lhsT_scale=wd8_s[:, P * a : P * (a + 1)],
-                    rhs=h_codes[jt][:].bitcast(E4),
-                    rhs_scale=h_sc[jt][:],
-                    start=True,
-                    stop=False,
-                )
-                nc.tensor.matmul_mx(
-                    out=y[:, a, :],
-                    lhsT=wd4_w[:, 2 * P * a : 2 * P * (a + 1)].bitcast(E2),
-                    lhsT_scale=wd4_s[:, P * a : P * (a + 1)],
-                    rhs=h_codes[4 + jt][:].bitcast(E4),
-                    rhs_scale=h_sc[4 + jt][:],
-                    start=False,
-                    stop=True,
-                )
             cols = slice(jt * P, (jt + 1) * P)
             o = keep.tile([P, 2, P], F32, name=f"o{jt}", align_bytes=64)
-            nc.vector.tensor_tensor(o[:], y[:], res_sb[:, :, cols], ALU.add)
+            if jt in Y_EARLY:
+                for a in range(2):
+                    second_pass(opened[jt][a][:], jt, a)
+                for a in range(2):
+                    nc.vector.tensor_tensor(o[:, a, :], opened[jt][a][:], res_sb[:, a, cols], ALU.add)
+            else:
+                y = next_bank([P, 2, P])
+                for a in range(2):
+                    first_pass(y[:, a, :], jt, a)
+                    second_pass(y[:, a, :], jt, a)
+                if jt in Y_ON_G:
+                    nc.scalar.copy(o[:], y[:])
+                    nc.gpsimd.tensor_tensor(o[:], o[:], res_sb[:, :, cols], ALU.add)
+                else:
+                    nc.vector.tensor_tensor(o[:], y[:], res_sb[:, :, cols], ALU.add)
             nc.sync.dma_start(out=out_v[:, :, cols], in_=o[:])
 
         steps = {
@@ -337,10 +399,11 @@ def tile_list_pnet_mix_res_kernel(
             "t": turn,
             "q": quantize_h,
             "y": second_layer,
+            "f": open_layer,
             "cc": cast_c,
             "qc": quantize_c,
             "cw": cast_w,
-            "qw": quantize_w,
+            "qw": lambda q: quantize_w(1) if q == 3 else None,
         }
         for step in ORDER:
             steps[step[0]](*step[1:])

@@ -20,12 +20,13 @@ P = 128
 HALF = 512
 FOLD = 7
 PE_ADD_UNITS = (6, 7)
-DMA_ORDER = "V T W C r x"
+DMA_ORDER = "V s T W C r x"
 C_ON_G = (0,)
 C_GATE = 1
 Y_EARLY = (3,)
 Y_ON_G = ()
-LATE = 3
+LATE = 4
+FOLD_S = 1
 SPLIT = ()
 ORDER = (
     ("n", 1, 0),
@@ -123,7 +124,6 @@ def tile_list_pnet_mix_res_kernel(
     with ExitStack() as ctx:
         keep = ctx.enter_context(tc.tile_pool(name="keep", bufs=1))
         reuse = ctx.enter_context(tc.tile_pool(name="reuse", bufs=1))
-        head = ctx.enter_context(tc.tile_pool(name="head", bufs=1))
         late = ctx.enter_context(tc.tile_pool(name="late", bufs=1))
         psum = ctx.enter_context(tc.psum_pool(name="psum", bufs=1))
 
@@ -132,17 +132,17 @@ def tile_list_pnet_mix_res_kernel(
         offsets = keep.tile([P, G * J // 16], U16, name="offsets")
         nc.sync.dma_start(offsets[:], offs)
 
+        table_s = keep.tile([P, T], U8, name="table_s", align_bytes=64)
+        nc.vector.memset(table_s[:].bitcast(I32), 0)
         wc_s = keep.tile([P, R], U8, name="wc_s", align_bytes=64)
         nc.vector.memset(wc_s[:].bitcast(I32), 0)
-        table_s = head.tile([P, T], U8, name="table_s", align_bytes=64, offset=0)
-        nc.vector.memset(table_s[:].bitcast(I32), 0)
         wd = keep.tile([P, 4 * N + 2 * N + 2 * N], U8, name="wd", align_bytes=64)
         wd8_w, wd4_w = wd[:, 0 : 4 * N], wd[:, 4 * N : 6 * N]
         wd8_s, wd4_s = wd[:, 6 * N : 7 * N], wd[:, 7 * N : 8 * N]
         nc.vector.memset(wd[:, 6 * N :].bitcast(I32), 0)
         wc_w = keep.tile([P, 2 * R], U8, name="wc_w", align_bytes=64)
-        nc.sync.dma_start(out=wc_w[:].bitcast(I32), in_=wc_words[0].bitcast(I32))
-        load_scale_rows(nc.sync, wc_s, wc_scales[0])
+        for h in range(2):
+            nc.sync.dma_start(out=wc_w[:, R * h : R * (h + 1)].bitcast(I32), in_=wc_words[0][:, R * h : R * (h + 1)].bitcast(I32))
         load_scale_rows(nc.sync, table_s, tab_scales[0])
         table_w = late.tile([P, T], I32, name="table_w", align_bytes=64, offset=0)
         c_k = c.rearrange("(p i) j -> p i j", i=4)
@@ -175,6 +175,8 @@ def tile_list_pnet_mix_res_kernel(
             if step == "x":
                 nc.sync.dma_start(out=wd4_w.bitcast(I32), in_=wd4_words[0].bitcast(I32))
                 nc.sync.dma_start(out=wd8_w.bitcast(I32), in_=wd8_words[0].rearrange("p n i -> p (n i)").bitcast(I32))
+            if step == "s":
+                load_scale_rows(nc.sync, wc_s, wc_scales[0])
             if step == "r":
                 nc.sync.dma_start(out=res_sb[:], in_=res.rearrange("(a p) j -> p a j", p=P))
         load_scale_rows(nc.sync, wd8_s, wd8_scales[0])
@@ -203,7 +205,7 @@ def tile_list_pnet_mix_res_kernel(
 
         for g in range(G):
             gather_scales(g)
-        picked_early = head.tile([P, 2, J], I32, name="picked_early", align_bytes=64, offset=R)
+        picked_early = keep.tile([P, 2, J], I32, name="picked_early", align_bytes=64)
         picked_w = [picked_early[:, 0, :], picked_early[:, 1, :]]
         wcp_s = keep.tile([P, R], U8, name="wcp_s", align_bytes=64)
         nc.vector.tensor_copy(
@@ -272,6 +274,7 @@ def tile_list_pnet_mix_res_kernel(
         best = [keep.tile([P, 4, P], F32, name=f"best{u}", align_bytes=64) for u in range(8)]
         own = [keep.tile([P, 4, P], F32, name=f"own{u}", align_bytes=64) for u in range(8)]
         pre = [keep.tile([P, 4, P], BF16, name=f"pre{u}", align_bytes=64) for u in range(8)]
+        folded = keep.tile([P, 4, P, 4], BF16, name="folded", align_bytes=64)
         h_bf = [keep.tile([P, P, 4], BF16, name=f"h_bf{u}", align_bytes=64) for u in range(8)]
         h_codes = [keep.tile([P, P], U32, name=f"h_codes{u}", align_bytes=64) for u in range(8)]
         h_sc = [keep.tile([P, P], U8, name=f"h_sc{u}", align_bytes=64) for u in range(8)]
@@ -304,16 +307,30 @@ def tile_list_pnet_mix_res_kernel(
                 )
                 if u == FOLD:
                     own_pass(bank, u, t, False)
-            if g == 0 and u == FOLD:
+            woven = bank[:].rearrange("p t j -> p j t")
+            if u == FOLD and FOLD_S > 1 and g < FOLD_S:
+                nc.scalar.activation(folded[:, g, :, :], woven, ACT.Relu)
+                if g == 3:
+                    nc.vector.tensor_tensor(folded[:, 0:2, :, :], folded[:, 0:2, :, :], folded[:, 2:4, :, :], ALU.max)
+                    nc.vector.tensor_tensor(h_bf[u][:], folded[:, 0, :, :], folded[:, 1, :, :], ALU.max)
+            elif u == FOLD and FOLD_S > 1:
+                k = g - FOLD_S if FOLD_S == 2 else 2
+                nc.vector.tensor_tensor(folded[:, k, :, :], folded[:, k, :, :], woven, ALU.max)
+                if g == 3 and FOLD_S == 2:
+                    nc.vector.tensor_tensor(h_bf[u][:], folded[:, 0, :, :], folded[:, 1, :, :], ALU.max)
+                elif g == 3:
+                    nc.vector.tensor_tensor(folded[:, 0, :, :], folded[:, 0, :, :], folded[:, 1, :, :], ALU.max)
+                    nc.vector.tensor_tensor(h_bf[u][:], folded[:, 0, :, :], folded[:, 2, :, :], ALU.max)
+            elif g == 0 and u == FOLD:
                 nc.scalar.activation(best[u][:], bank[:], ACT.Relu)
             elif g == 0:
                 nc.scalar.copy(best[u][:], bank[:])
             elif g == 3 and u == FOLD:
                 nc.vector.tensor_tensor(
-                    h_bf[u][:], bank[:].rearrange("p t j -> p j t"), best[u][:].rearrange("p t j -> p j t"), ALU.max
+                    h_bf[u][:], best[u][:].rearrange("p t j -> p j t"), bank[:].rearrange("p t j -> p j t"), ALU.max
                 )
             else:
-                nc.vector.tensor_tensor(best[u][:], bank[:], best[u][:], ALU.max)
+                nc.vector.tensor_tensor(best[u][:], best[u][:], bank[:], ALU.max)
 
         def own_part(u):
             if u != FOLD and u not in PE_ADD_UNITS:
@@ -327,7 +344,7 @@ def tile_list_pnet_mix_res_kernel(
                 bank = next_bank([P, 4, P])
                 for t in range(4):
                     own_pass(bank, u, t, True)
-                nc.vector.tensor_tensor(pre[u][:], bank[:], best[u][:], ALU.add)
+                nc.vector.tensor_tensor(pre[u][:], best[u][:], bank[:], ALU.add)
             elif u != FOLD:
                 nc.gpsimd.tensor_tensor(pre[u][:], best[u][:], own[u][:], ALU.add)
 
@@ -379,7 +396,7 @@ def tile_list_pnet_mix_res_kernel(
                 for a in range(2):
                     second_pass(opened[jt][a][:], jt, a)
                 for a in range(2):
-                    nc.vector.tensor_tensor(o[:, a, :], opened[jt][a][:], res_sb[:, a, cols], ALU.add)
+                    nc.vector.tensor_tensor(o[:, a, :], res_sb[:, a, cols], opened[jt][a][:], ALU.add)
             else:
                 y = next_bank([P, 2, P])
                 for a in range(2):
@@ -389,7 +406,7 @@ def tile_list_pnet_mix_res_kernel(
                     nc.scalar.copy(o[:], y[:])
                     nc.gpsimd.tensor_tensor(o[:], o[:], res_sb[:, :, cols], ALU.add)
                 else:
-                    nc.vector.tensor_tensor(o[:], y[:], res_sb[:, :, cols], ALU.add)
+                    nc.vector.tensor_tensor(o[:], res_sb[:, :, cols], y[:], ALU.add)
             nc.sync.dma_start(out=out_v[:, :, cols], in_=o[:])
 
         steps = {

@@ -19,96 +19,96 @@ ACT = mybir.ActivationFunctionType
 P = 128
 HALF = 512
 FOLD = 7
-PE_ADD_UNITS = (6, 7)
-DMA_ORDER = "V s T W C r x"
+PE_ADD_UNITS = (4, 6)
+DMA_ORDER = "V s T W C x r"
 C_ON_G = (0,)
 C_GATE = 1
-Y_EARLY = (3,)
-Y_ON_G = ()
+Y_EARLY = (1, 2)
+Y_ON_G = (1,)
 LATE = 4
-FOLD_S = 1
+FOLD_S = 4
 SPLIT = ()
 ORDER = (
-    ("n", 1, 0),
-    ("cc", 0),
-    ("n", 0, 0),
-    ("cw", 3),
-    ("n", 2, 0),
-    ("qc", 0),
-    ("n", 0, 1),
     ("cw", 2),
-    ("qw", 3),
     ("cc", 1),
-    ("n", 0, 2),
+    ("cw", 3),
     ("n", 3, 0),
+    ("qw", 3),
+    ("cc", 0),
+    ("qc", 0),
+    ("n", 2, 0),
+    ("qw", 2),
+    ("n", 1, 0),
+    ("n", 0, 0),
+    ("n", 0, 1),
+    ("n", 1, 1),
+    ("n", 0, 2),
     ("n", 2, 1),
     ("n", 3, 1),
-    ("n", 1, 1),
-    ("qw", 2),
     ("n", 1, 2),
-    ("qc", 1),
-    ("n", 2, 2),
-    ("n", 4, 0),
     ("o", 0),
-    ("n", 0, 3),
+    ("n", 4, 0),
+    ("n", 2, 2),
     ("n", 3, 2),
+    ("qc", 1),
+    ("n", 0, 3),
+    ("o", 6),
+    ("o", 4),
     ("o", 5),
-    ("a", 0),
-    ("n", 1, 3),
     ("n", 2, 3),
     ("o", 2),
     ("o", 1),
+    ("a", 2),
+    ("n", 3, 3),
     ("n", 5, 0),
     ("n", 4, 1),
-    ("t", 0),
-    ("n", 3, 3),
-    ("n", 4, 2),
-    ("o", 6),
-    ("o", 3),
-    ("n", 5, 1),
+    ("n", 1, 3),
     ("n", 6, 0),
-    ("n", 5, 2),
-    ("a", 2),
-    ("n", 6, 1),
-    ("n", 4, 3),
-    ("a", 1),
-    ("o", 4),
+    ("n", 5, 1),
+    ("o", 3),
     ("n", 7, 0),
-    ("a", 4),
-    ("n", 5, 3),
     ("a", 3),
-    ("n", 6, 2),
+    ("n", 4, 2),
+    ("n", 5, 2),
+    ("n", 4, 3),
+    ("a", 0),
+    ("n", 6, 1),
+    ("a", 1),
     ("n", 7, 1),
+    ("n", 5, 3),
+    ("n", 6, 2),
+    ("t", 0),
+    ("t", 2),
+    ("a", 4),
+    ("t", 4),
+    ("o", 7),
     ("n", 6, 3),
     ("n", 7, 2),
-    ("t", 1),
-    ("t", 3),
-    ("t", 4),
-    ("a", 6),
-    ("q", 3),
-    ("o", 7),
     ("q", 0),
+    ("t", 1),
+    ("a", 6),
     ("q", 4),
-    ("f", 3),
-    ("q", 1),
-    ("t", 2),
-    ("a", 5),
     ("n", 7, 3),
-    ("t", 5),
-    ("q", 5),
-    ("a", 7),
-    ("q", 2),
-    ("t", 6),
+    ("q", 1),
+    ("t", 3),
+    ("q", 3),
     ("f", 0),
-    ("t", 7),
-    ("q", 7),
-    ("y", 0),
+    ("t", 6),
+    ("a", 7),
     ("q", 6),
+    ("q", 2),
+    ("a", 5),
     ("f", 1),
+    ("t", 5),
+    ("f", 3),
+    ("t", 7),
+    ("q", 5),
+    ("q", 7),
     ("f", 2),
-    ("y", 1),
-    ("y", 3),
     ("y", 2),
+    ("y", 0),
+    ("y", 3),
+    ("y", 1),
 )
 
 
@@ -185,8 +185,8 @@ def tile_list_pnet_mix_res_kernel(
         wcp_w = keep.tile([P, 2 * R], U8, name="wcp_w", align_bytes=64)
         for h in range(2):
             nc.vector.tensor_copy(
-                wcp_w[:, 2 * HALF * h : 2 * HALF * (h + 1)].rearrange("p (t m b) -> p m t b", t=4, b=2),
-                wc_w[:, 2 * HALF * h : 2 * HALF * (h + 1)].rearrange("p (m t b) -> p m t b", t=4, b=2),
+                wcp_w[:, 2 * HALF * h : 2 * HALF * (h + 1)].rearrange("p (t m b) -> p t m b", t=4, b=2),
+                wc_w[:, 2 * HALF * h : 2 * HALF * (h + 1)].rearrange("p (m t b) -> p t m b", t=4, b=2),
             )
 
         used_banks = []
@@ -209,8 +209,8 @@ def tile_list_pnet_mix_res_kernel(
         picked_w = [picked_early[:, 0, :], picked_early[:, 1, :]]
         wcp_s = keep.tile([P, R], U8, name="wcp_s", align_bytes=64)
         nc.vector.tensor_copy(
-            wcp_s[:].rearrange("p (h t m) -> p h m t", h=2, t=4),
-            wc_s[:].rearrange("p (h m t) -> p h m t", h=2, t=4),
+            wcp_s[:].rearrange("p (h t m) -> p h t m", h=2, t=4),
+            wc_s[:].rearrange("p (h m t) -> p h t m", h=2, t=4),
         )
 
         def gather_words(g):

@@ -18,98 +18,11 @@ ACT = mybir.ActivationFunctionType
 
 P = 128
 HALF = 512
-FOLD = 7
-PE_ADD_UNITS = (4, 6)
-DMA_ORDER = "V s T W C x r"
-C_ON_G = (0,)
-C_GATE = 1
-Y_EARLY = (1, 2)
-Y_ON_G = (1,)
-LATE = 4
-FOLD_S = 4
-SPLIT = ()
-ORDER = (
-    ("cw", 2),
-    ("cc", 1),
-    ("cw", 3),
-    ("n", 3, 0),
-    ("qw", 3),
-    ("cc", 0),
-    ("qc", 0),
-    ("n", 2, 0),
-    ("qw", 2),
-    ("n", 1, 0),
-    ("n", 0, 0),
-    ("n", 0, 1),
-    ("n", 1, 1),
-    ("n", 0, 2),
-    ("n", 2, 1),
-    ("n", 3, 1),
-    ("n", 1, 2),
-    ("o", 0),
-    ("n", 4, 0),
-    ("n", 2, 2),
-    ("n", 3, 2),
-    ("qc", 1),
-    ("n", 0, 3),
-    ("o", 6),
-    ("o", 4),
-    ("o", 5),
-    ("n", 2, 3),
-    ("o", 2),
-    ("o", 1),
-    ("a", 2),
-    ("n", 3, 3),
-    ("n", 5, 0),
-    ("n", 4, 1),
-    ("n", 1, 3),
-    ("n", 6, 0),
-    ("n", 5, 1),
-    ("o", 3),
-    ("n", 7, 0),
-    ("a", 3),
-    ("n", 4, 2),
-    ("n", 5, 2),
-    ("n", 4, 3),
-    ("a", 0),
-    ("n", 6, 1),
-    ("a", 1),
-    ("n", 7, 1),
-    ("n", 5, 3),
-    ("n", 6, 2),
-    ("t", 0),
-    ("t", 2),
-    ("a", 4),
-    ("t", 4),
-    ("o", 7),
-    ("n", 6, 3),
-    ("n", 7, 2),
-    ("q", 0),
-    ("t", 1),
-    ("a", 6),
-    ("q", 4),
-    ("n", 7, 3),
-    ("q", 1),
-    ("t", 3),
-    ("q", 3),
-    ("f", 0),
-    ("t", 6),
-    ("a", 7),
-    ("q", 6),
-    ("q", 2),
-    ("a", 5),
-    ("f", 1),
-    ("t", 5),
-    ("f", 3),
-    ("t", 7),
-    ("q", 5),
-    ("q", 7),
-    ("f", 2),
-    ("y", 2),
-    ("y", 0),
-    ("y", 3),
-    ("y", 1),
-)
+QUARTER = 256
+UNIT = 4 * P
+POOLED = 6
+FOLD = 6
+LAST = 7
 
 
 def load_scale_rows(queue, plane, rows):
@@ -128,106 +41,84 @@ def tile_list_pnet_mix_res_kernel(
         psum = ctx.enter_context(tc.psum_pool(name="psum", bufs=1))
 
         w_k = w.rearrange("(p i) r -> p i r", i=4)
+        c_k = c.rearrange("(p i) j -> p i j", i=4)
 
         offsets = keep.tile([P, G * J // 16], U16, name="offsets")
         nc.sync.dma_start(offsets[:], offs)
 
-        table_s = keep.tile([P, T], U8, name="table_s", align_bytes=64)
-        nc.vector.memset(table_s[:].bitcast(I32), 0)
         wc_s = keep.tile([P, R], U8, name="wc_s", align_bytes=64)
         nc.vector.memset(wc_s[:].bitcast(I32), 0)
-        wd = keep.tile([P, 4 * N + 2 * N + 2 * N], U8, name="wd", align_bytes=64)
+        table_s = keep.tile([P, T], U8, name="table_s", align_bytes=64)
+        nc.gpsimd.memset(table_s[:, 0 : T // 2].bitcast(I32), 0)
+        nc.vector.memset(table_s[:, T // 2 : T].bitcast(I32), 0)
+        wcp_s = keep.tile([P, R], U8, name="wcp_s", align_bytes=64)
+        nc.gpsimd.memset(wcp_s[:].bitcast(I32), 0)
+        wd = keep.tile([P, 8 * N], U8, name="wd", align_bytes=64)
         wd8_w, wd4_w = wd[:, 0 : 4 * N], wd[:, 4 * N : 6 * N]
         wd8_s, wd4_s = wd[:, 6 * N : 7 * N], wd[:, 7 * N : 8 * N]
-        nc.vector.memset(wd[:, 6 * N :].bitcast(I32), 0)
-        wc_w = keep.tile([P, 2 * R], U8, name="wc_w", align_bytes=64)
-        for h in range(2):
-            nc.sync.dma_start(out=wc_w[:, R * h : R * (h + 1)].bitcast(I32), in_=wc_words[0][:, R * h : R * (h + 1)].bitcast(I32))
-        load_scale_rows(nc.sync, table_s, tab_scales[0])
-        table_w = late.tile([P, T], I32, name="table_w", align_bytes=64, offset=0)
-        c_k = c.rearrange("(p i) j -> p i j", i=4)
-        def halves(name, whole):
-            if whole:
-                both = keep.tile([P, 4, 512], F32, name=name, align_bytes=64)
-                return both, [both[:, :, 0:256], both[:, :, 256:512]]
-            return None, [keep.tile([P, 4, 256], F32, name=f"{name}{q}", align_bytes=64)[:] for q in range(2)]
+        nc.gpsimd.memset(wd[:, 6 * N :].bitcast(I32), 0)
 
-        c_all, c_raw = halves("c_raw", "C" in DMA_ORDER)
-        w_zero, w_first = halves("w_first", "V" in DMA_ORDER)
-        w_second, w_last = halves("w_second", "W" in DMA_ORDER)
-        w_raw = w_first + w_last
+        wc_w = keep.tile([P, 2 * R], U8, name="wc_w", align_bytes=64)
+        table_w = reuse.tile([P, T], I32, name="table_w", tag="table", align_bytes=64)
+        w_raw = [keep.tile([P, 4, QUARTER], F32, name=f"w_raw{q}", align_bytes=64) for q in range(4)]
+        c_raw = [
+            keep.tile([P, 4, QUARTER], F32, name="c_raw0", align_bytes=64),
+            reuse.tile([P, 4, QUARTER], F32, name="c_raw1", tag="c", align_bytes=64),
+        ]
         res_sb = keep.tile([P, 2, J], F32, name="res_sb", align_bytes=64)
-        for step in DMA_ORDER.split():
-            if step[0] == "c":
-                q = int(step[1])
-                nc.sync.dma_start(out=c_raw[q], in_=c_k[:, :, 256 * q : 256 * (q + 1)])
-            if step[0] == "w":
-                q = int(step[1])
-                nc.sync.dma_start(out=w_raw[q], in_=w_k[:, :, 256 * q : 256 * (q + 1)])
-            if step == "C":
-                nc.sync.dma_start(out=c_all[:], in_=c_k)
-            if step == "W":
-                nc.sync.dma_start(out=w_second[:], in_=w_k[:, :, HALF:R])
-            if step == "T":
-                nc.sync.dma_start(out=table_w[:], in_=tab_words[0].rearrange("p t i -> p (t i)").bitcast(I32))
-            if step == "V":
-                nc.sync.dma_start(out=w_zero[:], in_=w_k[:, :, 0:HALF])
-            if step == "x":
-                nc.sync.dma_start(out=wd4_w.bitcast(I32), in_=wd4_words[0].bitcast(I32))
-                nc.sync.dma_start(out=wd8_w.bitcast(I32), in_=wd8_words[0].rearrange("p n i -> p (n i)").bitcast(I32))
-            if step == "s":
-                load_scale_rows(nc.sync, wc_s, wc_scales[0])
-            if step == "r":
-                nc.sync.dma_start(out=res_sb[:], in_=res.rearrange("(a p) j -> p a j", p=P))
+
+        def load_w(q):
+            nc.sync.dma_start(out=w_raw[q][:], in_=w_k[:, :, QUARTER * q : QUARTER * (q + 1)])
+
+        nc.sync.dma_start(out=wc_w[:].bitcast(I32), in_=wc_words[0].bitcast(I32))
+        nc.sync.dma_start(out=wc_s[0:P:8, :].bitcast(I32), in_=wc_scales[0].bitcast(I32))
+        load_scale_rows(nc.sync, table_s, tab_scales[0])
+        nc.sync.dma_start(out=table_w[:], in_=tab_words[0].rearrange("p t i -> p (t i)").bitcast(I32))
+        load_w(0)
+        load_w(1)
+        wcp_w = keep.tile([P, 2 * R], U8, name="wcp_w", align_bytes=64)
+        nc.vector.tensor_copy(
+            wcp_w[:].bitcast(U16).rearrange("p (h t m) -> p h t m", h=2, t=4),
+            wc_w[:].bitcast(U16).rearrange("p (h m t) -> p h t m", h=2, t=4),
+        )
+        dealt_s = keep.tile([P, R], U8, name="dealt_s", align_bytes=64)
+        nc.vector.tensor_copy(
+            dealt_s[:].rearrange("p (h t m) -> p h t m", h=2, t=4),
+            wc_s[:].rearrange("p (h m t) -> p h t m", h=2, t=4),
+        )
+        for r in range(4):
+            nc.sync.dma_start(out=wcp_s[r:P:32, :].bitcast(I32), in_=dealt_s[8 * r : P : 32, :].bitcast(I32))
+        for q in range(2):
+            nc.sync.dma_start(out=c_raw[q][:], in_=c_k[:, :, QUARTER * q : QUARTER * (q + 1)])
+        load_w(2)
+        load_w(3)
+        nc.sync.dma_start(out=wd4_w.bitcast(I32), in_=wd4_words[0].bitcast(I32))
+        nc.sync.dma_start(out=wd8_w.bitcast(I32), in_=wd8_words[0].rearrange("p n i -> p (n i)").bitcast(I32))
+        nc.sync.dma_start(out=res_sb[:], in_=res.rearrange("(a p) j -> p a j", p=P))
         load_scale_rows(nc.sync, wd8_s, wd8_scales[0])
         load_scale_rows(nc.sync, wd4_s, wd4_scales[0])
 
-        wcp_w = keep.tile([P, 2 * R], U8, name="wcp_w", align_bytes=64)
-        for h in range(2):
+
+        picked_s = keep.tile([P, G * J], U8, name="picked_s", align_bytes=64)
+        nc.vector.tensor_copy(picked_s[:], table_s[:].indirect(offsets[:]))
+
+        picked_w = []
+
+        def gather_words(g, tile):
+            picked_w.append(tile)
             nc.vector.tensor_copy(
-                wcp_w[:, 2 * HALF * h : 2 * HALF * (h + 1)].rearrange("p (t m b) -> p t m b", t=4, b=2),
-                wc_w[:, 2 * HALF * h : 2 * HALF * (h + 1)].rearrange("p (m t b) -> p t m b", t=4, b=2),
+                tile[:].bitcast(U32),
+                table_w[:].bitcast(U32).indirect(offsets[:, g * (J // 16) : (g + 1) * (J // 16)]),
             )
-
-        used_banks = []
-
-        def next_bank(shape):
-            used_banks.append(shape)
-            return psum.tile(shape, F32, name="bank", tag=f"bank{len(used_banks) % 8}")
-
-        picked_s = [keep.tile([P, J], U8, name=f"picked_s{g}", align_bytes=64) for g in range(G)]
-
-        def list_of(g):
-            return offsets[:, g * (J // 16) : (g + 1) * (J // 16)]
-
-        def gather_scales(g):
-            nc.vector.tensor_copy(picked_s[g][:], table_s[:].indirect(list_of(g)))
-
-        for g in range(G):
-            gather_scales(g)
-        picked_early = keep.tile([P, 2, J], I32, name="picked_early", align_bytes=64)
-        picked_w = [picked_early[:, 0, :], picked_early[:, 1, :]]
-        wcp_s = keep.tile([P, R], U8, name="wcp_s", align_bytes=64)
-        nc.vector.tensor_copy(
-            wcp_s[:].rearrange("p (h t m) -> p h t m", h=2, t=4),
-            wc_s[:].rearrange("p (h m t) -> p h t m", h=2, t=4),
-        )
-
-        def gather_words(g):
-            nc.vector.tensor_copy(picked_w[g][:, :].bitcast(U32), table_w[:].bitcast(U32).indirect(list_of(g)))
 
         w_codes = [keep.tile([P, HALF], U32, name=f"w_codes{h}", align_bytes=64) for h in range(2)]
         w_sc = [keep.tile([P, HALF], U8, name=f"w_sc{h}", align_bytes=64) for h in range(2)]
-
-        w_bf = [
-            reuse.tile([P, 4, P, 4], BF16, name="w_bf0", tag="slot_d", align_bytes=64),
-            keep.tile([P, 4, P, 4], BF16, name="w_bf1", align_bytes=64),
-        ]
+        w_bf = [reuse.tile([P, 4, P, 4], BF16, name=f"w_bf{h}", tag=f"w{h}", align_bytes=64) for h in range(2)]
 
         def cast_w(q):
             nc.scalar.copy(
                 w_bf[q // 2][:, :, 64 * (q % 2) : 64 * (q % 2 + 1), :].rearrange("p t m i -> p m i t"),
-                w_raw[q].rearrange("p i (m t) -> p m i t", t=4),
+                w_raw[q][:].rearrange("p i (m t) -> p m i t", t=4),
             )
 
         def quantize_w(h):
@@ -235,49 +126,50 @@ def tile_list_pnet_mix_res_kernel(
                 out=w_codes[h][:].bitcast(E4), scales=w_sc[h][:], in_=w_bf[h][:].rearrange("p t m i -> p (t m i)")
             )
 
-        for g in range(2, LATE):
-            picked_w.append(keep.tile([P, J], I32, name=f"picked_w{g}", align_bytes=64))
-        for g in range(LATE):
-            gather_words(g)
+        for g in range(G - 1):
+            gather_words(g, keep.tile([P, J], I32, name=f"picked_w{g}", align_bytes=64))
         cast_w(0)
         cast_w(1)
         quantize_w(0)
-        if LATE < G:
-            picked_late = reuse.tile([P, G - LATE, J], I32, name="picked_late", tag="slot_d", align_bytes=64)
-            for g in range(LATE, G):
-                picked_w.append(picked_late[:, g - LATE, :])
-                gather_words(g)
+        gather_words(G - 1, reuse.tile([P, J], I32, name="picked_w3", tag="w0", align_bytes=64))
 
-        c_codes = keep.tile([P, J], U32, name="c_codes", align_bytes=64)
-        c_sc = keep.tile([P, J], U8, name="c_sc", align_bytes=64)
         c_bf = [
-            late.tile([P, 256, 4], BF16, name=f"c_bf{q}", align_bytes=64, offset=(2048 * q if (q in C_ON_G and C_GATE) else 4 * T + 2048 * q))
-            for q in range(2)
+            keep.tile([P, QUARTER, 4], BF16, name="c_bf0", align_bytes=64),
+            reuse.tile([P, QUARTER, 4], BF16, name="c_bf1", tag="table", align_bytes=64),
         ]
+        nc.scalar.copy(
+            c_bf[0][:].rearrange("p (a b) i -> p a i b", b=4), c_raw[0][:].rearrange("p i (a b) -> p a i b", b=4)
+        )
+        nc.gpsimd.tensor_scalar(c_bf[1][:], c_raw[1][:].rearrange("p i j -> p j i"), 1.0, 0.0, ALU.mult, ALU.add)
+        c_codes = reuse.tile([P, J], U32, name="c_codes", tag="c", align_bytes=64)
+        c_sc = keep.tile([P, J], U8, name="c_sc", align_bytes=64)
 
-        def cast_c(q):
-            if q not in C_ON_G:
-                nc.scalar.copy(
-                    c_bf[q][:].rearrange("p (a b) i -> p a i b", b=4),
-                    c_raw[q].rearrange("p i (a b) -> p a i b", b=4),
+        def quantize_c():
+            for q in range(2):
+                nc.vector.quantize_mx(
+                    out=c_codes[:, QUARTER * q : QUARTER * (q + 1)].bitcast(E4),
+                    scales=c_sc[:, QUARTER * q : QUARTER * (q + 1)],
+                    in_=c_bf[q][:].rearrange("p j i -> p (j i)"),
                 )
-            else:
-                nc.gpsimd.tensor_scalar(c_bf[q][:], c_raw[q].rearrange("p i j -> p j i"), 1.0, 0.0, ALU.mult, ALU.add)
 
-        def quantize_c(q):
-            nc.vector.quantize_mx(
-                out=c_codes[:, 256 * q : 256 * (q + 1)].bitcast(E4),
-                scales=c_sc[:, 256 * q : 256 * (q + 1)],
-                in_=c_bf[q][:].rearrange("p j i -> p (j i)"),
-            )
+        used_banks = []
 
-        best = [keep.tile([P, 4, P], F32, name=f"best{u}", align_bytes=64) for u in range(8)]
-        own = [keep.tile([P, 4, P], F32, name=f"own{u}", align_bytes=64) for u in range(8)]
-        pre = [keep.tile([P, 4, P], BF16, name=f"pre{u}", align_bytes=64) for u in range(8)]
-        folded = keep.tile([P, 4, P, 4], BF16, name="folded", align_bytes=64)
-        h_bf = [keep.tile([P, P, 4], BF16, name=f"h_bf{u}", align_bytes=64) for u in range(8)]
-        h_codes = [keep.tile([P, P], U32, name=f"h_codes{u}", align_bytes=64) for u in range(8)]
-        h_sc = [keep.tile([P, P], U8, name=f"h_sc{u}", align_bytes=64) for u in range(8)]
+        def next_bank(shape):
+            used_banks.append(shape)
+            return psum.tile(shape, F32, name="bank", tag=f"bank{len(used_banks) % 8}")
+
+        best, own = {}, {}
+        for u in range(8):
+            if u == POOLED - 1:
+                best[u] = late.tile([P, P, 4], F32, name=f"best{u}", align_bytes=64, offset=2048)
+                own[u] = late.tile([P, P, 4], F32, name=f"own{u}", align_bytes=64, offset=4096)
+            elif u != FOLD:
+                best[u] = keep.tile([P, P, 4], F32, name=f"best{u}", align_bytes=64)
+                if u != LAST:
+                    own[u] = keep.tile([P, P, 4], F32, name=f"own{u}", align_bytes=64)
+        pre = [None, keep.tile([P, 4, P, 4], BF16, name="pre1", align_bytes=64)]
+        h_bf = [keep.tile([P, 4, P, 4], BF16, name=f"h_bf{h}", align_bytes=64) for h in range(2)]
+        folded = keep.tile([P, G, P, 4], BF16, name="folded", align_bytes=64)
 
         def own_pass(bank, u, t, start):
             h, cols = u // 4, slice(u % 4 * P, (u % 4 + 1) * P)
@@ -293,134 +185,143 @@ def tile_list_pnet_mix_res_kernel(
             )
 
         def neighbour(u, g):
-            h, cols = u // 4, slice(u % 4 * P, (u % 4 + 1) * P)
+            h, j0 = u // 4, u % 4 * P
             bank = next_bank([P, 4, P])
             for t in range(4):
                 nc.tensor.matmul_mx(
                     out=bank[:, t, :],
                     lhsT=w_codes[h][:, P * t : P * (t + 1)].bitcast(E4),
                     lhsT_scale=w_sc[h][:, P * t : P * (t + 1)],
-                    rhs=picked_w[g][:, cols].bitcast(E4),
-                    rhs_scale=picked_s[g][:, cols],
+                    rhs=picked_w[g][:, j0 : j0 + P].bitcast(E4),
+                    rhs_scale=picked_s[:, g * J + j0 : g * J + j0 + P],
                     start=True,
                     stop=u != FOLD,
                 )
                 if u == FOLD:
                     own_pass(bank, u, t, False)
             woven = bank[:].rearrange("p t j -> p j t")
-            if u == FOLD and FOLD_S > 1 and g < FOLD_S:
+            if u == FOLD:
                 nc.scalar.activation(folded[:, g, :, :], woven, ACT.Relu)
-                if g == 3:
-                    nc.vector.tensor_tensor(folded[:, 0:2, :, :], folded[:, 0:2, :, :], folded[:, 2:4, :, :], ALU.max)
-                    nc.vector.tensor_tensor(h_bf[u][:], folded[:, 0, :, :], folded[:, 1, :, :], ALU.max)
-            elif u == FOLD and FOLD_S > 1:
-                k = g - FOLD_S if FOLD_S == 2 else 2
-                nc.vector.tensor_tensor(folded[:, k, :, :], folded[:, k, :, :], woven, ALU.max)
-                if g == 3 and FOLD_S == 2:
-                    nc.vector.tensor_tensor(h_bf[u][:], folded[:, 0, :, :], folded[:, 1, :, :], ALU.max)
-                elif g == 3:
-                    nc.vector.tensor_tensor(folded[:, 0, :, :], folded[:, 0, :, :], folded[:, 1, :, :], ALU.max)
-                    nc.vector.tensor_tensor(h_bf[u][:], folded[:, 0, :, :], folded[:, 2, :, :], ALU.max)
-            elif g == 0 and u == FOLD:
-                nc.scalar.activation(best[u][:], bank[:], ACT.Relu)
             elif g == 0:
-                nc.scalar.copy(best[u][:], bank[:])
-            elif g == 3 and u == FOLD:
-                nc.vector.tensor_tensor(
-                    h_bf[u][:], best[u][:].rearrange("p t j -> p j t"), bank[:].rearrange("p t j -> p j t"), ALU.max
-                )
+                nc.scalar.copy(best[u][:], woven)
             else:
-                nc.vector.tensor_tensor(best[u][:], best[u][:], bank[:], ALU.max)
+                nc.vector.tensor_tensor(best[u][:], best[u][:], woven, ALU.max)
+
+        def own_bank(u):
+            bank = next_bank([P, 4, P])
+            for t in range(4):
+                own_pass(bank, u, t, True)
+            return bank[:].rearrange("p t j -> p j t")
 
         def own_part(u):
-            if u != FOLD and u not in PE_ADD_UNITS:
-                bank = next_bank([P, 4, P])
-                for t in range(4):
-                    own_pass(bank, u, t, True)
-                nc.scalar.copy(own[u][:], bank[:])
+            nc.scalar.copy(own[u][:], own_bank(u))
 
         def add_own(u):
-            if u != FOLD and u in PE_ADD_UNITS:
-                bank = next_bank([P, 4, P])
-                for t in range(4):
-                    own_pass(bank, u, t, True)
-                nc.vector.tensor_tensor(pre[u][:], best[u][:], bank[:], ALU.add)
-            elif u != FOLD:
-                nc.gpsimd.tensor_tensor(pre[u][:], best[u][:], own[u][:], ALU.add)
+            nc.gpsimd.tensor_tensor(pre[u // 4][:, u % 4, :, :], best[u][:], own[u][:], ALU.add)
 
-        def turn(u):
-            if u != FOLD:
-                nc.scalar.activation(h_bf[u][:], pre[u][:].rearrange("p t j -> p j t"), ACT.Relu)
+        def relu(u):
+            nc.scalar.activation(h_bf[u // 4][:, u % 4, :, :], pre[u // 4][:, u % 4, :, :], ACT.Relu)
 
-        def quantize_h(u):
+        chained = [u for u in range(8) if u != FOLD]
+        neighbour(0, 0)
+        for s, u in enumerate(chained):
+            if s + 1 < len(chained):
+                neighbour(chained[s + 1], 0)
+            neighbour(u, 1)
+            if s > 0:
+                neighbour(chained[s - 1], 3)
+            if s in (2, 3, 4):
+                own_part(2 * (s - 2))
+            if s == 5:
+                relu(0)
+                relu(1)
+            if s == 6:
+                relu(2)
+                relu(3)
+            neighbour(u, 2)
+            if s in (2, 3, 4):
+                own_part(2 * (s - 2) + 1)
+            if s == 6:
+                neighbour(FOLD, 0)
+            if s == 0:
+                quantize_c()
+                cast_w(2)
+            if s == 1:
+                cast_w(3)
+                quantize_w(1)
+                pre[0] = reuse.tile([P, 4, P, 4], BF16, name="pre0", tag="w1", align_bytes=64)
+            if s == 2:
+                add_own(0)
+            if s >= 2:
+                add_own(s - 1)
+        neighbour(LAST, 3)
+        neighbour(FOLD, 1)
+        nc.vector.tensor_tensor(pre[1][:, 3, :, :], best[LAST][:], own_bank(LAST), ALU.add)
+        neighbour(FOLD, 2)
+        neighbour(FOLD, 3)
+        relu(4)
+        relu(5)
+
+        pair_max = late.tile([P, 2, P, 4], BF16, name="pair_max", align_bytes=64, offset=64)
+        h_codes = [late.tile([P, J], U32, name=f"h_codes{h}", align_bytes=64, offset=2112 + 2048 * h) for h in range(2)]
+        h_sc = [keep.tile([P, J], U8, name=f"h_sc{h}", align_bytes=64) for h in range(2)]
+
+        def quantize_h(h, jt, n):
+            cols = slice(jt * P, (jt + n) * P)
             nc.vector.quantize_mx(
-                out=h_codes[u][:].bitcast(E4), scales=h_sc[u][:], in_=h_bf[u][:].rearrange("p j t -> p (j t)")
+                out=h_codes[h][:, cols].bitcast(E4),
+                scales=h_sc[h][:, cols],
+                in_=h_bf[h][:, jt : jt + n, :, :].rearrange("p u j t -> p (u j t)"),
             )
 
         out_v = out.rearrange("(a p) j -> p a j", p=P)
 
-        opened = {}
+        def open_layer(jt, n):
+            cols = slice(jt * P, (jt + n) * P)
+            y = next_bank([P, 2, n * P])
+            for a in range(2):
+                nc.tensor.matmul_mx(
+                    out=y[:, a, :],
+                    lhsT=wd8_w[:, 4 * P * a : 4 * P * (a + 1)].bitcast(E4),
+                    lhsT_scale=wd8_s[:, P * a : P * (a + 1)],
+                    rhs=h_codes[0][:, cols].bitcast(E4),
+                    rhs_scale=h_sc[0][:, cols],
+                    start=a == 0,
+                    stop=False,
+                )
+            return y
 
-        def first_pass(y, jt, a):
-            nc.tensor.matmul_mx(
-                out=y,
-                lhsT=wd8_w[:, 4 * P * a : 4 * P * (a + 1)].bitcast(E4),
-                lhsT_scale=wd8_s[:, P * a : P * (a + 1)],
-                rhs=h_codes[jt][:].bitcast(E4),
-                rhs_scale=h_sc[jt][:],
-                start=True,
-                stop=False,
-            )
+        def close_layer(y, jt, n):
+            for a in range(2):
+                for k in range(n):
+                    cols = slice((jt + k) * P, (jt + k + 1) * P)
+                    nc.tensor.matmul_mx(
+                        out=y[:, a, k * P : (k + 1) * P],
+                        lhsT=wd4_w[:, 2 * P * a : 2 * P * (a + 1)].bitcast(E2),
+                        lhsT_scale=wd4_s[:, P * a : P * (a + 1)],
+                        rhs=h_codes[1][:, cols].bitcast(E4),
+                        rhs_scale=h_sc[1][:, cols],
+                        start=False,
+                        stop=a == 1 and k == n - 1,
+                    )
 
-        def second_pass(y, jt, a):
-            nc.tensor.matmul_mx(
-                out=y,
-                lhsT=wd4_w[:, 2 * P * a : 2 * P * (a + 1)].bitcast(E2),
-                lhsT_scale=wd4_s[:, P * a : P * (a + 1)],
-                rhs=h_codes[4 + jt][:].bitcast(E4),
-                rhs_scale=h_sc[4 + jt][:],
-                start=False,
-                stop=True,
-            )
-
-        def open_layer(jt):
-            if jt in Y_EARLY:
-                opened[jt] = [next_bank([P, P]), next_bank([P, P])]
-                for a in range(2):
-                    first_pass(opened[jt][a][:], jt, a)
-
-        def second_layer(jt):
-            cols = slice(jt * P, (jt + 1) * P)
-            o = keep.tile([P, 2, P], F32, name=f"o{jt}", align_bytes=64)
-            if jt in Y_EARLY:
-                for a in range(2):
-                    second_pass(opened[jt][a][:], jt, a)
-                for a in range(2):
-                    nc.vector.tensor_tensor(o[:, a, :], res_sb[:, a, cols], opened[jt][a][:], ALU.add)
-            else:
-                y = next_bank([P, 2, P])
-                for a in range(2):
-                    first_pass(y[:, a, :], jt, a)
-                    second_pass(y[:, a, :], jt, a)
-                if jt in Y_ON_G:
-                    nc.scalar.copy(o[:], y[:])
-                    nc.gpsimd.tensor_tensor(o[:], o[:], res_sb[:, :, cols], ALU.add)
-                else:
-                    nc.vector.tensor_tensor(o[:], res_sb[:, :, cols], y[:], ALU.add)
+        def finish(y, jt, n):
+            cols = slice(jt * P, (jt + n) * P)
+            o = keep.tile([P, 2, n * P], F32, name=f"o{jt}", align_bytes=64)
+            nc.vector.tensor_tensor(o[:], res_sb[:, :, cols], y[:], ALU.add)
             nc.sync.dma_start(out=out_v[:, :, cols], in_=o[:])
 
-        steps = {
-            "n": neighbour,
-            "o": own_part,
-            "a": add_own,
-            "t": turn,
-            "q": quantize_h,
-            "y": second_layer,
-            "f": open_layer,
-            "cc": cast_c,
-            "qc": quantize_c,
-            "cw": cast_w,
-            "qw": lambda q: quantize_w(1) if q == 3 else None,
-        }
-        for step in ORDER:
-            steps[step[0]](*step[1:])
+        quantize_h(0, 0, 4)
+        y_last, y_pair, y_fold = open_layer(3, 1), open_layer(0, 2), open_layer(2, 1)
+        nc.vector.tensor_scalar_max(h_bf[1][:, 3, :, :], pre[1][:, 3, :, :], 0.0)
+        nc.vector.tensor_tensor(pair_max[:], folded[:, 0:2, :, :], folded[:, 2:4, :, :], ALU.max)
+        quantize_h(1, 3, 1)
+        close_layer(y_last, 3, 1)
+        nc.vector.tensor_tensor(h_bf[1][:, 2, :, :], pair_max[:, 0, :, :], pair_max[:, 1, :, :], ALU.max)
+        quantize_h(1, 0, 2)
+        close_layer(y_pair, 0, 2)
+        quantize_h(1, 2, 1)
+        close_layer(y_fold, 2, 1)
+        finish(y_last, 3, 1)
+        finish(y_pair, 0, 2)
+        finish(y_fold, 2, 1)

@@ -30,6 +30,11 @@ def load_scale_rows(queue, plane, rows):
         queue.dma_start(out=plane[r:P:32, :].bitcast(I32), in_=rows[r:16:4, :].bitcast(I32))
 
 
+def carry_scale_rows(queue, plane, spread):
+    for r in range(4):
+        queue.dma_start(out=plane[r:P:32, :].bitcast(I32), in_=spread[16 + r : 32 : 4, :].bitcast(I32))
+
+
 def tile_list_pnet_mix_res_kernel(
     tc, tab_words, tab_scales, c, w, wc_words, wc_scales, wd8_words, wd8_scales, wd4_words, wd4_scales, res, offs, out
 ):
@@ -38,6 +43,10 @@ def tile_list_pnet_mix_res_kernel(
         keep = ctx.enter_context(tc.tile_pool(name="keep", bufs=1))
         reuse = ctx.enter_context(tc.tile_pool(name="reuse", bufs=1))
         late = ctx.enter_context(tc.tile_pool(name="late", bufs=1))
+        head = ctx.enter_context(tc.tile_pool(name="head", bufs=1))
+        dealt = ctx.enter_context(tc.tile_pool(name="dealt", bufs=1))
+        second = ctx.enter_context(tc.tile_pool(name="second", bufs=1))
+        early = ctx.enter_context(tc.tile_pool(name="early", bufs=1))
         psum = ctx.enter_context(tc.psum_pool(name="psum", bufs=1))
 
         w_k = w.rearrange("(p i) r -> p i r", i=4)
@@ -49,76 +58,65 @@ def tile_list_pnet_mix_res_kernel(
         wc_s = keep.tile([P, R], U8, name="wc_s", align_bytes=64)
         nc.vector.memset(wc_s[:].bitcast(I32), 0)
         table_s = keep.tile([P, T], U8, name="table_s", align_bytes=64)
-        nc.gpsimd.memset(table_s[:, 0 : T // 2].bitcast(I32), 0)
-        nc.vector.memset(table_s[:, T // 2 : T].bitcast(I32), 0)
-        wcp_s = keep.tile([P, R], U8, name="wcp_s", align_bytes=64)
-        nc.gpsimd.memset(wcp_s[:].bitcast(I32), 0)
+        nc.gpsimd.memset(table_s[0:16, :].bitcast(I32), 0)
+        nc.gpsimd.memset(table_s[32:64, :].bitcast(I32), 0)
+        nc.vector.memset(table_s[64:P, :].bitcast(I32), 0)
+        picked_s = keep.tile([P, G * J], U8, name="picked_s", align_bytes=64)
+        nc.gpsimd.memset(picked_s[:].bitcast(I32), 0)
         wd = keep.tile([P, 8 * N], U8, name="wd", align_bytes=64)
         wd8_w, wd4_w = wd[:, 0 : 4 * N], wd[:, 4 * N : 6 * N]
         wd8_s, wd4_s = wd[:, 6 * N : 7 * N], wd[:, 7 * N : 8 * N]
         nc.gpsimd.memset(wd[:, 6 * N :].bitcast(I32), 0)
 
-        wc_w = keep.tile([P, 2 * R], U8, name="wc_w", align_bytes=64)
-        table_w = reuse.tile([P, T], I32, name="table_w", tag="table", align_bytes=64)
-        w_raw = [keep.tile([P, 4, QUARTER], F32, name=f"w_raw{q}", align_bytes=64) for q in range(4)]
+        wc_w = dealt.tile([P, 2 * R], U8, name="wc_w", align_bytes=64, offset=0)
+        table_w = keep.tile([P, T], I32, name="table_w", align_bytes=64)
+        w_raw = [keep.tile([P, 4, QUARTER], F32, name=f"w_raw{q}", align_bytes=64)[:] for q in range(2)]
+        w_raw = w_raw + [
+            early.tile([P, 4, QUARTER], F32, name=f"w_raw{q}", align_bytes=64, offset=4096 * (q - 1))[:] for q in (2, 3)
+        ]
         c_raw = [
-            keep.tile([P, 4, QUARTER], F32, name="c_raw0", align_bytes=64),
+            early.tile([P, 4, QUARTER], F32, name="c_raw0", align_bytes=64, offset=0),
             reuse.tile([P, 4, QUARTER], F32, name="c_raw1", tag="c", align_bytes=64),
         ]
         res_sb = keep.tile([P, 2, J], F32, name="res_sb", align_bytes=64)
 
         def load_w(q):
-            nc.sync.dma_start(out=w_raw[q][:], in_=w_k[:, :, QUARTER * q : QUARTER * (q + 1)])
+            nc.sync.dma_start(out=w_raw[q], in_=w_k[:, :, QUARTER * q : QUARTER * (q + 1)])
 
-        nc.sync.dma_start(out=wc_w[:].bitcast(I32), in_=wc_words[0].bitcast(I32))
-        nc.sync.dma_start(out=wc_s[0:P:8, :].bitcast(I32), in_=wc_scales[0].bitcast(I32))
-        load_scale_rows(nc.sync, table_s, tab_scales[0])
+        nc.sync.dma_start(out=table_s[16:32, :].bitcast(I32), in_=tab_scales[0].bitcast(I32))
         nc.sync.dma_start(out=table_w[:], in_=tab_words[0].rearrange("p t i -> p (t i)").bitcast(I32))
         load_w(0)
         load_w(1)
-        wcp_w = keep.tile([P, 2 * R], U8, name="wcp_w", align_bytes=64)
-        nc.vector.tensor_copy(
-            wcp_w[:].bitcast(U16).rearrange("p (h t m) -> p h t m", h=2, t=4),
-            wc_w[:].bitcast(U16).rearrange("p (h m t) -> p h t m", h=2, t=4),
-        )
-        dealt_s = keep.tile([P, R], U8, name="dealt_s", align_bytes=64)
-        nc.vector.tensor_copy(
-            dealt_s[:].rearrange("p (h t m) -> p h t m", h=2, t=4),
-            wc_s[:].rearrange("p (h m t) -> p h t m", h=2, t=4),
-        )
-        for r in range(4):
-            nc.sync.dma_start(out=wcp_s[r:P:32, :].bitcast(I32), in_=dealt_s[8 * r : P : 32, :].bitcast(I32))
-        for q in range(2):
-            nc.sync.dma_start(out=c_raw[q][:], in_=c_k[:, :, QUARTER * q : QUARTER * (q + 1)])
+        load_scale_rows(nc.scalar, wc_s, wc_scales[0])
+        gathered_s = keep.tile([P, G * J], U8, name="gathered_s", align_bytes=64)
+        nc.vector.tensor_copy(gathered_s[:], table_s[:].indirect(offsets[:]))
+        carry_scale_rows(nc.sync, picked_s, gathered_s)
+        nc.sync.dma_start(out=c_raw[0][:], in_=c_k[:, :, 0:QUARTER])
+        nc.sync.dma_start(out=wc_w[:].bitcast(I32), in_=wc_words[0].bitcast(I32))
+        nc.sync.dma_start(out=c_raw[1][:], in_=c_k[:, :, QUARTER:J])
         load_w(2)
         load_w(3)
-        nc.sync.dma_start(out=wd4_w.bitcast(I32), in_=wd4_words[0].bitcast(I32))
-        nc.sync.dma_start(out=wd8_w.bitcast(I32), in_=wd8_words[0].rearrange("p n i -> p (n i)").bitcast(I32))
-        nc.sync.dma_start(out=res_sb[:], in_=res.rearrange("(a p) j -> p a j", p=P))
-        load_scale_rows(nc.sync, wd8_s, wd8_scales[0])
-        load_scale_rows(nc.sync, wd4_s, wd4_scales[0])
-
-
-        picked_s = keep.tile([P, G * J], U8, name="picked_s", align_bytes=64)
-        nc.vector.tensor_copy(picked_s[:], table_s[:].indirect(offsets[:]))
 
         picked_w = []
 
         def gather_words(g, tile):
             picked_w.append(tile)
             nc.vector.tensor_copy(
-                tile[:].bitcast(U32),
+                tile.bitcast(U32),
                 table_w[:].bitcast(U32).indirect(offsets[:, g * (J // 16) : (g + 1) * (J // 16)]),
             )
 
         w_codes = [keep.tile([P, HALF], U32, name=f"w_codes{h}", align_bytes=64) for h in range(2)]
         w_sc = [keep.tile([P, HALF], U8, name=f"w_sc{h}", align_bytes=64) for h in range(2)]
-        w_bf = [reuse.tile([P, 4, P, 4], BF16, name=f"w_bf{h}", tag=f"w{h}", align_bytes=64) for h in range(2)]
+        w_bf = [
+            head.tile([P, 4, P, 4], BF16, name="w_bf0", align_bytes=64, offset=1024),
+            second.tile([P, 4, P, 4], BF16, name="w_bf1", align_bytes=64, offset=1024),
+        ]
 
         def cast_w(q):
             nc.scalar.copy(
                 w_bf[q // 2][:, :, 64 * (q % 2) : 64 * (q % 2 + 1), :].rearrange("p t m i -> p m i t"),
-                w_raw[q][:].rearrange("p i (m t) -> p m i t", t=4),
+                w_raw[q].rearrange("p i (m t) -> p m i t", t=4),
             )
 
         def quantize_w(h):
@@ -127,15 +125,33 @@ def tile_list_pnet_mix_res_kernel(
             )
 
         for g in range(G - 1):
-            gather_words(g, keep.tile([P, J], I32, name=f"picked_w{g}", align_bytes=64))
+            gather_words(g, keep.tile([P, J], I32, name=f"picked_w{g}", align_bytes=64)[:])
         cast_w(0)
         cast_w(1)
         quantize_w(0)
-        gather_words(G - 1, reuse.tile([P, J], I32, name="picked_w3", tag="w0", align_bytes=64))
+        gather_words(G - 1, head.tile([P, J], I32, name="picked_w3", align_bytes=64, offset=0)[:])
+        wcp_s = keep.tile([P, R], U8, name="wcp_s", align_bytes=64)
+        nc.vector.tensor_copy(
+            wcp_s[:].rearrange("p (h t m) -> p h t m", h=2, t=4),
+            wc_s[:].rearrange("p (h m t) -> p h t m", h=2, t=4),
+        )
+        wcp_w = keep.tile([P, 2 * R], U8, name="wcp_w", align_bytes=64)
+        nc.vector.tensor_copy(
+            wcp_w[:].bitcast(U16).rearrange("p (h t m) -> p h t m", h=2, t=4),
+            wc_w[:].bitcast(U16).rearrange("p (h m t) -> p h t m", h=2, t=4),
+        )
+
+
+        nc.sync.dma_start(out=wd4_w.bitcast(I32), in_=wd4_words[0].bitcast(I32))
+        nc.sync.dma_start(out=wd8_w.bitcast(I32), in_=wd8_words[0].rearrange("p n i -> p (n i)").bitcast(I32))
+        nc.sync.dma_start(out=res_sb[:], in_=res.rearrange("(a p) j -> p a j", p=P))
+        load_scale_rows(nc.sync, wd8_s, wd8_scales[0])
+        load_scale_rows(nc.sync, wd4_s, wd4_scales[0])
+
 
         c_bf = [
             keep.tile([P, QUARTER, 4], BF16, name="c_bf0", align_bytes=64),
-            reuse.tile([P, QUARTER, 4], BF16, name="c_bf1", tag="table", align_bytes=64),
+            dealt.tile([P, QUARTER, 4], BF16, name="c_bf1", align_bytes=64, offset=R),
         ]
         nc.scalar.copy(
             c_bf[0][:].rearrange("p (a b) i -> p a i b", b=4), c_raw[0][:].rearrange("p i (a b) -> p a i b", b=4)
@@ -164,9 +180,12 @@ def tile_list_pnet_mix_res_kernel(
                 best[u] = late.tile([P, P, 4], F32, name=f"best{u}", align_bytes=64, offset=2048)
                 own[u] = late.tile([P, P, 4], F32, name=f"own{u}", align_bytes=64, offset=4096)
             elif u != FOLD:
-                best[u] = keep.tile([P, P, 4], F32, name=f"best{u}", align_bytes=64)
+                if u != 2:
+                    best[u] = keep.tile([P, P, 4], F32, name=f"best{u}", align_bytes=64)
                 if u != LAST:
                     own[u] = keep.tile([P, P, 4], F32, name=f"own{u}", align_bytes=64)
+        first = [early.tile([P, P, 4], F32, name=f"first{u}", align_bytes=64, offset=2048 * (u + max(0, min(u, 4) - 2)))
+            for u in range(8)]
         pre = [None, keep.tile([P, 4, P, 4], BF16, name="pre1", align_bytes=64)]
         h_bf = [keep.tile([P, 4, P, 4], BF16, name=f"h_bf{h}", align_bytes=64) for h in range(2)]
         folded = keep.tile([P, G, P, 4], BF16, name="folded", align_bytes=64)
@@ -203,9 +222,9 @@ def tile_list_pnet_mix_res_kernel(
             if u == FOLD:
                 nc.scalar.activation(folded[:, g, :, :], woven, ACT.Relu)
             elif g == 0:
-                nc.scalar.copy(best[u][:], woven)
+                nc.scalar.copy(first[u][:], woven)
             else:
-                nc.vector.tensor_tensor(best[u][:], best[u][:], woven, ALU.max)
+                nc.vector.tensor_tensor(best[u][:], (first if g == 1 else best)[u][:], woven, ALU.max)
 
         def own_bank(u):
             bank = next_bank([P, 4, P])
@@ -225,9 +244,12 @@ def tile_list_pnet_mix_res_kernel(
         chained = [u for u in range(8) if u != FOLD]
         neighbour(0, 0)
         for s, u in enumerate(chained):
+            if u != LAST:
+                neighbour(u, 1)
+            else:
+                neighbour(u, 2)
             if s + 1 < len(chained):
                 neighbour(chained[s + 1], 0)
-            neighbour(u, 1)
             if s > 0:
                 neighbour(chained[s - 1], 3)
             if s in (2, 3, 4):
@@ -238,18 +260,22 @@ def tile_list_pnet_mix_res_kernel(
             if s == 6:
                 relu(2)
                 relu(3)
-            neighbour(u, 2)
+            if s == 5:
+                neighbour(LAST, 1)
+            if u != LAST:
+                neighbour(u, 2)
             if s in (2, 3, 4):
                 own_part(2 * (s - 2) + 1)
             if s == 6:
                 neighbour(FOLD, 0)
             if s == 0:
-                quantize_c()
                 cast_w(2)
             if s == 1:
                 cast_w(3)
+                quantize_c()
                 quantize_w(1)
-                pre[0] = reuse.tile([P, 4, P, 4], BF16, name="pre0", tag="w1", align_bytes=64)
+                pre[0] = second.tile([P, 4, P, 4], BF16, name="pre0", align_bytes=64, offset=2048)
+                best[2] = second.tile([P, P, 4], F32, name="best2", align_bytes=64, offset=0)
             if s == 2:
                 add_own(0)
             if s >= 2:
@@ -257,9 +283,9 @@ def tile_list_pnet_mix_res_kernel(
         neighbour(LAST, 3)
         neighbour(FOLD, 1)
         nc.vector.tensor_tensor(pre[1][:, 3, :, :], best[LAST][:], own_bank(LAST), ALU.add)
+        relu(4)
         neighbour(FOLD, 2)
         neighbour(FOLD, 3)
-        relu(4)
         relu(5)
 
         pair_max = late.tile([P, 2, P, 4], BF16, name="pair_max", align_bytes=64, offset=64)
@@ -312,16 +338,16 @@ def tile_list_pnet_mix_res_kernel(
             nc.sync.dma_start(out=out_v[:, :, cols], in_=o[:])
 
         quantize_h(0, 0, 4)
-        y_last, y_pair, y_fold = open_layer(3, 1), open_layer(0, 2), open_layer(2, 1)
+        y = [open_layer(jt, 1) for jt in range(4)]
         nc.vector.tensor_scalar_max(h_bf[1][:, 3, :, :], pre[1][:, 3, :, :], 0.0)
         nc.vector.tensor_tensor(pair_max[:], folded[:, 0:2, :, :], folded[:, 2:4, :, :], ALU.max)
-        quantize_h(1, 3, 1)
-        close_layer(y_last, 3, 1)
-        nc.vector.tensor_tensor(h_bf[1][:, 2, :, :], pair_max[:, 0, :, :], pair_max[:, 1, :, :], ALU.max)
         quantize_h(1, 0, 2)
-        close_layer(y_pair, 0, 2)
+        close_layer(y[0], 0, 1)
+        close_layer(y[1], 1, 1)
+        nc.vector.tensor_tensor(h_bf[1][:, 2, :, :], pair_max[:, 0, :, :], pair_max[:, 1, :, :], ALU.max)
+        quantize_h(1, 3, 1)
+        close_layer(y[3], 3, 1)
         quantize_h(1, 2, 1)
-        close_layer(y_fold, 2, 1)
-        finish(y_last, 3, 1)
-        finish(y_pair, 0, 2)
-        finish(y_fold, 2, 1)
+        close_layer(y[2], 2, 1)
+        for jt in (0, 1, 3, 2):
+            finish(y[jt], jt, 1)

@@ -130,7 +130,7 @@ def tile_list_pnet_mix_res_kernel(
         cast_w(1)
         quantize_w(0)
         gather_words(G - 1, head.tile([P, J], I32, name="picked_w3", align_bytes=64, offset=0)[:])
-        wcp_s = keep.tile([P, R], U8, name="wcp_s", align_bytes=64)
+        wcp_s = head.tile([P, R], U8, name="wcp_s", align_bytes=64, offset=2048)
         nc.vector.tensor_copy(
             wcp_s[:].rearrange("p (h t m) -> p h t m", h=2, t=4),
             wc_s[:].rearrange("p (h m t) -> p h t m", h=2, t=4),
@@ -177,16 +177,16 @@ def tile_list_pnet_mix_res_kernel(
         best, own = {}, {}
         for u in range(8):
             if u == POOLED - 1:
-                best[u] = late.tile([P, P, 4], F32, name=f"best{u}", align_bytes=64, offset=2048)
-                own[u] = late.tile([P, P, 4], F32, name=f"own{u}", align_bytes=64, offset=4096)
+                best[u] = late.tile([P, 4, P], F32, name=f"best{u}", align_bytes=64, offset=2048)
+                own[u] = late.tile([P, 4, P], F32, name=f"own{u}", align_bytes=64, offset=4096)
             elif u != FOLD:
                 if u != 2:
-                    best[u] = keep.tile([P, P, 4], F32, name=f"best{u}", align_bytes=64)
+                    best[u] = keep.tile([P, 4, P], F32, name=f"best{u}", align_bytes=64)
                 if u != LAST:
-                    own[u] = keep.tile([P, P, 4], F32, name=f"own{u}", align_bytes=64)
-        first = [early.tile([P, P, 4], F32, name=f"first{u}", align_bytes=64, offset=2048 * (u + max(0, min(u, 4) - 2)))
+                    own[u] = keep.tile([P, 4, P], F32, name=f"own{u}", align_bytes=64)
+        first = [early.tile([P, 4, P], F32, name=f"first{u}", align_bytes=64, offset=2048 * (u + max(0, min(u, 4) - 2)))
             for u in range(8)]
-        pre = [None, keep.tile([P, 4, P, 4], BF16, name="pre1", align_bytes=64)]
+        pre = [None, keep.tile([P, 4, 4, P], BF16, name="pre1", align_bytes=64)]
         h_bf = [keep.tile([P, 4, P, 4], BF16, name=f"h_bf{h}", align_bytes=64) for h in range(2)]
         folded = keep.tile([P, G, P, 4], BF16, name="folded", align_bytes=64)
 
@@ -222,15 +222,15 @@ def tile_list_pnet_mix_res_kernel(
             if u == FOLD:
                 nc.scalar.activation(folded[:, g, :, :], woven, ACT.Relu)
             elif g == 0:
-                nc.scalar.copy(first[u][:], woven)
+                nc.scalar.copy(first[u][:], bank[:])
             else:
-                nc.vector.tensor_tensor(best[u][:], (first if g == 1 else best)[u][:], woven, ALU.max)
+                nc.vector.tensor_tensor(best[u][:], (first if g == 1 else best)[u][:], bank[:], ALU.max)
 
         def own_bank(u):
             bank = next_bank([P, 4, P])
             for t in range(4):
                 own_pass(bank, u, t, True)
-            return bank[:].rearrange("p t j -> p j t")
+            return bank[:]
 
         def own_part(u):
             nc.scalar.copy(own[u][:], own_bank(u))
@@ -239,7 +239,7 @@ def tile_list_pnet_mix_res_kernel(
             nc.gpsimd.tensor_tensor(pre[u // 4][:, u % 4, :, :], best[u][:], own[u][:], ALU.add)
 
         def relu(u):
-            nc.scalar.activation(h_bf[u // 4][:, u % 4, :, :], pre[u // 4][:, u % 4, :, :], ACT.Relu)
+            nc.scalar.activation(h_bf[u // 4][:, u % 4, :, :], pre[u // 4][:, u % 4, :, :].rearrange("p t j -> p j t"), ACT.Relu)
 
         chained = [u for u in range(8) if u != FOLD]
         neighbour(0, 0)
@@ -274,8 +274,8 @@ def tile_list_pnet_mix_res_kernel(
                 cast_w(3)
                 quantize_c()
                 quantize_w(1)
-                pre[0] = second.tile([P, 4, P, 4], BF16, name="pre0", align_bytes=64, offset=2048)
-                best[2] = second.tile([P, P, 4], F32, name="best2", align_bytes=64, offset=0)
+                pre[0] = second.tile([P, 4, 4, P], BF16, name="pre0", align_bytes=64, offset=2048)
+                best[2] = second.tile([P, 4, P], F32, name="best2", align_bytes=64, offset=0)
             if s == 2:
                 add_own(0)
             if s >= 2:
@@ -339,7 +339,7 @@ def tile_list_pnet_mix_res_kernel(
 
         quantize_h(0, 0, 4)
         y = [open_layer(jt, 1) for jt in range(4)]
-        nc.vector.tensor_scalar_max(h_bf[1][:, 3, :, :], pre[1][:, 3, :, :], 0.0)
+        nc.vector.tensor_scalar_max(h_bf[1][:, 3, :, :], pre[1][:, 3, :, :].rearrange("p t j -> p j t"), 0.0)
         nc.vector.tensor_tensor(pair_max[:], folded[:, 0:2, :, :], folded[:, 2:4, :, :], ALU.max)
         quantize_h(1, 0, 2)
         close_layer(y[0], 0, 1)

@@ -21,8 +21,8 @@ HALF = 512
 QUARTER = 256
 UNIT = 4 * P
 POOLED = 6
-FOLD = 6
-LAST = 7
+FOLD = 7
+LAST = 6
 
 
 def load_scale_rows(queue, plane, rows):
@@ -177,16 +177,16 @@ def tile_list_pnet_mix_res_kernel(
         best, own = {}, {}
         for u in range(8):
             if u == POOLED - 1:
-                best[u] = late.tile([P, 4, P], F32, name=f"best{u}", align_bytes=64, offset=2048)
-                own[u] = late.tile([P, 4, P], F32, name=f"own{u}", align_bytes=64, offset=4096)
+                best[u] = late.tile([P, P, 4], F32, name=f"best{u}", align_bytes=64, offset=2048)
+                own[u] = late.tile([P, P, 4], F32, name=f"own{u}", align_bytes=64, offset=4096)
             elif u != FOLD:
                 if u != 2:
-                    best[u] = keep.tile([P, 4, P], F32, name=f"best{u}", align_bytes=64)
+                    best[u] = keep.tile([P, P, 4], F32, name=f"best{u}", align_bytes=64)
                 if u != LAST:
-                    own[u] = keep.tile([P, 4, P], F32, name=f"own{u}", align_bytes=64)
-        first = [early.tile([P, 4, P], F32, name=f"first{u}", align_bytes=64, offset=2048 * (u + max(0, min(u, 4) - 2)))
+                    own[u] = keep.tile([P, P, 4], F32, name=f"own{u}", align_bytes=64)
+        first = [early.tile([P, P, 4], F32, name=f"first{u}", align_bytes=64, offset=2048 * (u + max(0, min(u, 4) - 2)))
             for u in range(8)]
-        pre = [None, keep.tile([P, 4, 4, P], BF16, name="pre1", align_bytes=64)]
+        pre = [None, keep.tile([P, 4, P, 4], BF16, name="pre1", align_bytes=64)]
         h_bf = [keep.tile([P, 4, P, 4], BF16, name=f"h_bf{h}", align_bytes=64) for h in range(2)]
         folded = keep.tile([P, G, P, 4], BF16, name="folded", align_bytes=64)
 
@@ -222,15 +222,15 @@ def tile_list_pnet_mix_res_kernel(
             if u == FOLD:
                 nc.scalar.activation(folded[:, g, :, :], woven, ACT.Relu)
             elif g == 0:
-                nc.scalar.copy(first[u][:], bank[:])
+                nc.scalar.copy(first[u][:], woven)
             else:
-                nc.vector.tensor_tensor(best[u][:], (first if g == 1 else best)[u][:], bank[:], ALU.max)
+                nc.vector.tensor_tensor(best[u][:], (first if g == 1 else best)[u][:], woven, ALU.max)
 
         def own_bank(u):
             bank = next_bank([P, 4, P])
             for t in range(4):
                 own_pass(bank, u, t, True)
-            return bank[:]
+            return bank[:].rearrange("p t j -> p j t")
 
         def own_part(u):
             nc.scalar.copy(own[u][:], own_bank(u))
@@ -239,7 +239,7 @@ def tile_list_pnet_mix_res_kernel(
             nc.gpsimd.tensor_tensor(pre[u // 4][:, u % 4, :, :], best[u][:], own[u][:], ALU.add)
 
         def relu(u):
-            nc.scalar.activation(h_bf[u // 4][:, u % 4, :, :], pre[u // 4][:, u % 4, :, :].rearrange("p t j -> p j t"), ACT.Relu)
+            nc.scalar.activation(h_bf[u // 4][:, u % 4, :, :], pre[u // 4][:, u % 4, :, :], ACT.Relu)
 
         chained = [u for u in range(8) if u != FOLD]
         neighbour(0, 0)
@@ -274,19 +274,17 @@ def tile_list_pnet_mix_res_kernel(
                 cast_w(3)
                 quantize_c()
                 quantize_w(1)
-                pre[0] = second.tile([P, 4, 4, P], BF16, name="pre0", align_bytes=64, offset=2048)
-                best[2] = second.tile([P, 4, P], F32, name="best2", align_bytes=64, offset=0)
+                pre[0] = second.tile([P, 4, P, 4], BF16, name="pre0", align_bytes=64, offset=2048)
+                best[2] = second.tile([P, P, 4], F32, name="best2", align_bytes=64, offset=0)
             if s == 2:
                 add_own(0)
             if s >= 2:
                 add_own(s - 1)
         neighbour(LAST, 3)
         neighbour(FOLD, 1)
-        nc.vector.tensor_tensor(pre[1][:, 3, :, :], best[LAST][:], own_bank(LAST), ALU.add)
-        relu(4)
+        nc.vector.tensor_tensor(pre[1][:, 2, :, :], best[LAST][:], own_bank(LAST), ALU.add)
         neighbour(FOLD, 2)
         neighbour(FOLD, 3)
-        relu(5)
 
         pair_max = late.tile([P, 2, P, 4], BF16, name="pair_max", align_bytes=64, offset=64)
         h_codes = [late.tile([P, J], U32, name=f"h_codes{h}", align_bytes=64, offset=2112 + 2048 * h) for h in range(2)]
@@ -339,15 +337,14 @@ def tile_list_pnet_mix_res_kernel(
 
         quantize_h(0, 0, 4)
         y = [open_layer(jt, 1) for jt in range(4)]
-        nc.vector.tensor_scalar_max(h_bf[1][:, 3, :, :], pre[1][:, 3, :, :].rearrange("p t j -> p j t"), 0.0)
+        nc.vector.tensor_scalar_max(h_bf[1][:, 0:3, :, :], pre[1][:, 0:3, :, :], 0.0)
         nc.vector.tensor_tensor(pair_max[:], folded[:, 0:2, :, :], folded[:, 2:4, :, :], ALU.max)
         quantize_h(1, 0, 2)
         close_layer(y[0], 0, 1)
         close_layer(y[1], 1, 1)
-        nc.vector.tensor_tensor(h_bf[1][:, 2, :, :], pair_max[:, 0, :, :], pair_max[:, 1, :, :], ALU.max)
-        quantize_h(1, 3, 1)
-        close_layer(y[3], 3, 1)
-        quantize_h(1, 2, 1)
-        close_layer(y[2], 2, 1)
-        for jt in (0, 1, 3, 2):
+        nc.vector.tensor_tensor(h_bf[1][:, 3, :, :], pair_max[:, 0, :, :], pair_max[:, 1, :, :], ALU.max)
+        for jt in (2, 3):
+            quantize_h(1, jt, 1)
+            close_layer(y[jt], jt, 1)
+        for jt in range(4):
             finish(y[jt], jt, 1)

@@ -19,20 +19,14 @@ ACT = mybir.ActivationFunctionType
 P = 128
 HALF = 512
 QUARTER = 256
-UNIT = 4 * P
-POOLED = 6
-FOLD = 7
+STAGE = P - 16
 LAST = 6
+FOLD = 7
 
 
 def load_scale_rows(queue, plane, rows):
     for r in range(4):
         queue.dma_start(out=plane[r:P:32, :].bitcast(I32), in_=rows[r:16:4, :].bitcast(I32))
-
-
-def carry_scale_rows(queue, plane, spread):
-    for r in range(4):
-        queue.dma_start(out=plane[r:P:32, :].bitcast(I32), in_=spread[16 + r : 32 : 4, :].bitcast(I32))
 
 
 def tile_list_pnet_mix_res_kernel(
@@ -41,13 +35,16 @@ def tile_list_pnet_mix_res_kernel(
     nc = tc.nc
     with ExitStack() as ctx:
         keep = ctx.enter_context(tc.tile_pool(name="keep", bufs=1))
-        reuse = ctx.enter_context(tc.tile_pool(name="reuse", bufs=1))
-        late = ctx.enter_context(tc.tile_pool(name="late", bufs=1))
-        head = ctx.enter_context(tc.tile_pool(name="head", bufs=1))
-        dealt = ctx.enter_context(tc.tile_pool(name="dealt", bufs=1))
-        second = ctx.enter_context(tc.tile_pool(name="second", bufs=1))
-        early = ctx.enter_context(tc.tile_pool(name="early", bufs=1))
+        on_table = ctx.enter_context(tc.tile_pool(name="on_table", bufs=1))
+        on_c_raw = ctx.enter_context(tc.tile_pool(name="on_c_raw", bufs=1))
+        on_w_raw = ctx.enter_context(tc.tile_pool(name="on_w_raw", bufs=1))
+        on_c_bf = ctx.enter_context(tc.tile_pool(name="on_c_bf", bufs=1))
         psum = ctx.enter_context(tc.psum_pool(name="psum", bufs=1))
+
+        def tile(shape, dtype, name, pool=keep, offset=None):
+            if offset is None:
+                return pool.tile(shape, dtype, name=name, align_bytes=64)
+            return pool.tile(shape, dtype, name=name, align_bytes=64, offset=offset)
 
         w_k = w.rearrange("(p i) r -> p i r", i=4)
         c_k = c.rearrange("(p i) j -> p i j", i=4)
@@ -55,68 +52,54 @@ def tile_list_pnet_mix_res_kernel(
         offsets = keep.tile([P, G * J // 16], U16, name="offsets")
         nc.sync.dma_start(offsets[:], offs)
 
-        wc_s = keep.tile([P, R], U8, name="wc_s", align_bytes=64)
+        wc_s = tile([P, R], U8, "wc_s")
+        table_s = tile([P, T], U8, "table_s")
+        picked_s = tile([P, G * J], U8, "picked_s")
+        wd_s = tile([P, 2 * N], U8, "wd_s")
+        wd8_s, wd4_s = wd_s[:, 0:N], wd_s[:, N : 2 * N]
         nc.vector.memset(wc_s[:].bitcast(I32), 0)
-        table_s = keep.tile([P, T], U8, name="table_s", align_bytes=64)
-        nc.gpsimd.memset(table_s[0:16, :].bitcast(I32), 0)
-        nc.gpsimd.memset(table_s[32:64, :].bitcast(I32), 0)
-        nc.vector.memset(table_s[64:P, :].bitcast(I32), 0)
-        picked_s = keep.tile([P, G * J], U8, name="picked_s", align_bytes=64)
-        nc.gpsimd.memset(picked_s[:].bitcast(I32), 0)
-        wd = keep.tile([P, 8 * N], U8, name="wd", align_bytes=64)
-        wd8_w, wd4_w = wd[:, 0 : 4 * N], wd[:, 4 * N : 6 * N]
-        wd8_s, wd4_s = wd[:, 6 * N : 7 * N], wd[:, 7 * N : 8 * N]
-        nc.gpsimd.memset(wd[:, 6 * N :].bitcast(I32), 0)
+        nc.vector.memset(table_s[0:STAGE, :].bitcast(I32), 0)
+        nc.vector.memset(picked_s[:].bitcast(I32), 0)
+        nc.vector.memset(wd_s[:].bitcast(I32), 0)
 
-        wc_w = dealt.tile([P, 2 * R], U8, name="wc_w", align_bytes=64, offset=0)
-        table_w = keep.tile([P, T], I32, name="table_w", align_bytes=64)
-        w_raw = [keep.tile([P, 4, QUARTER], F32, name=f"w_raw{q}", align_bytes=64)[:] for q in range(2)]
-        w_raw = w_raw + [
-            early.tile([P, 4, QUARTER], F32, name=f"w_raw{q}", align_bytes=64, offset=4096 * (q - 1))[:] for q in (2, 3)
-        ]
-        c_raw = [
-            early.tile([P, 4, QUARTER], F32, name="c_raw0", align_bytes=64, offset=0),
-            reuse.tile([P, 4, QUARTER], F32, name="c_raw1", tag="c", align_bytes=64),
-        ]
-        res_sb = keep.tile([P, 2, J], F32, name="res_sb", align_bytes=64)
+        wc_w = tile([P, 2 * R], U8, "wc_w")
+        table_w = tile([P, T], I32, "table_w", on_table, 0)
+        w_raw0 = [tile([P, 4, QUARTER], F32, f"w_raw0{q}") for q in range(2)]
+        w_raw1 = tile([P, 4, HALF], F32, "w_raw1", on_w_raw, 0)
+        c_raw = [tile([P, 4, QUARTER], F32, "c_raw0", on_c_raw, 0), tile([P, 4, QUARTER], F32, "c_raw1")]
+        wd8_w = tile([P, 4 * N], U8, "wd8_w")
+        wd4_w = tile([P, 2 * N], U8, "wd4_w")
+        res_sb = tile([P, 2, J], F32, "res_sb")
 
-        def load_w(q):
-            nc.sync.dma_start(out=w_raw[q], in_=w_k[:, :, QUARTER * q : QUARTER * (q + 1)])
-
-        nc.sync.dma_start(out=table_s[16:32, :].bitcast(I32), in_=tab_scales[0].bitcast(I32))
-        nc.sync.dma_start(out=table_w[:], in_=tab_words[0].rearrange("p t i -> p (t i)").bitcast(I32))
-        load_w(0)
-        load_w(1)
-        load_scale_rows(nc.scalar, wc_s, wc_scales[0])
-        gathered_s = keep.tile([P, G * J], U8, name="gathered_s", align_bytes=64)
-        nc.vector.tensor_copy(gathered_s[:], table_s[:].indirect(offsets[:]))
-        carry_scale_rows(nc.sync, picked_s, gathered_s)
-        nc.sync.dma_start(out=c_raw[0][:], in_=c_k[:, :, 0:QUARTER])
+        nc.sync.dma_start(out=table_s[STAGE:P, :].bitcast(I32), in_=tab_scales[0].bitcast(I32))
         nc.sync.dma_start(out=wc_w[:].bitcast(I32), in_=wc_words[0].bitcast(I32))
+        load_scale_rows(nc.sync, wc_s, wc_scales[0])
+        for q in range(2):
+            nc.sync.dma_start(out=w_raw0[q][:], in_=w_k[:, :, QUARTER * q : QUARTER * (q + 1)])
+        nc.sync.dma_start(out=table_w[:], in_=tab_words[0].rearrange("p t i -> p (t i)").bitcast(I32))
+        nc.sync.dma_start(out=c_raw[0][:], in_=c_k[:, :, 0:QUARTER])
+
+        gathered_s = tile([P, G * J], U8, "gathered_s")
+        nc.vector.tensor_copy(gathered_s[:], table_s[:].indirect(offsets[:]))
+        for r in range(4):
+            nc.sync.dma_start(out=picked_s[r:P:32, :].bitcast(I32), in_=gathered_s[STAGE + r : P : 4, :].bitcast(I32))
+        nc.sync.dma_start(out=w_raw1[:], in_=w_k[:, :, HALF:R])
         nc.sync.dma_start(out=c_raw[1][:], in_=c_k[:, :, QUARTER:J])
-        load_w(2)
-        load_w(3)
+        nc.sync.dma_start(out=wd8_w[:].bitcast(I32), in_=wd8_words[0].rearrange("p n i -> p (n i)").bitcast(I32))
+        nc.sync.dma_start(out=wd4_w[:].bitcast(I32), in_=wd4_words[0].bitcast(I32))
+        load_scale_rows(nc.sync, wd8_s, wd8_scales[0])
+        load_scale_rows(nc.sync, wd4_s, wd4_scales[0])
+        nc.sync.dma_start(out=res_sb[:], in_=res.rearrange("(a p) j -> p a j", p=P))
 
-        picked_w = []
+        w_bf = [tile([P, 4, P, 4], BF16, f"w_bf{h}") for h in range(2)]
+        w_codes = [tile([P, HALF], U32, f"w_codes{h}") for h in range(2)]
+        w_sc = [tile([P, HALF], U8, f"w_sc{h}") for h in range(2)]
 
-        def gather_words(g, tile):
-            picked_w.append(tile)
-            nc.vector.tensor_copy(
-                tile.bitcast(U32),
-                table_w[:].bitcast(U32).indirect(offsets[:, g * (J // 16) : (g + 1) * (J // 16)]),
-            )
-
-        w_codes = [keep.tile([P, HALF], U32, name=f"w_codes{h}", align_bytes=64) for h in range(2)]
-        w_sc = [keep.tile([P, HALF], U8, name=f"w_sc{h}", align_bytes=64) for h in range(2)]
-        w_bf = [
-            head.tile([P, 4, P, 4], BF16, name="w_bf0", align_bytes=64, offset=1024),
-            second.tile([P, 4, P, 4], BF16, name="w_bf1", align_bytes=64, offset=1024),
-        ]
-
-        def cast_w(q):
+        def cast_w(h, q):
+            raw = w_raw0[q][:] if h == 0 else w_raw1[:, :, QUARTER * q : QUARTER * (q + 1)]
             nc.scalar.copy(
-                w_bf[q // 2][:, :, 64 * (q % 2) : 64 * (q % 2 + 1), :].rearrange("p t m i -> p m i t"),
-                w_raw[q].rearrange("p i (m t) -> p m i t", t=4),
+                w_bf[h][:, :, 64 * q : 64 * (q + 1), :].rearrange("p t m i -> p m i t"),
+                raw.rearrange("p i (m t) -> p m i t", t=4),
             )
 
         def quantize_w(h):
@@ -124,49 +107,50 @@ def tile_list_pnet_mix_res_kernel(
                 out=w_codes[h][:].bitcast(E4), scales=w_sc[h][:], in_=w_bf[h][:].rearrange("p t m i -> p (t m i)")
             )
 
-        for g in range(G - 1):
-            gather_words(g, keep.tile([P, J], I32, name=f"picked_w{g}", align_bytes=64)[:])
-        cast_w(0)
-        cast_w(1)
+        cast_w(0, 0)
+        cast_w(0, 1)
         quantize_w(0)
-        gather_words(G - 1, head.tile([P, J], I32, name="picked_w3", align_bytes=64, offset=0)[:])
-        wcp_s = head.tile([P, R], U8, name="wcp_s", align_bytes=64, offset=2048)
-        nc.vector.tensor_copy(
-            wcp_s[:].rearrange("p (h t m) -> p h t m", h=2, t=4),
-            wc_s[:].rearrange("p (h m t) -> p h t m", h=2, t=4),
-        )
-        wcp_w = keep.tile([P, 2 * R], U8, name="wcp_w", align_bytes=64)
+
+        wcp_s = tile([P, R], U8, "wcp_s")
+        wcp_w = tile([P, 2 * R], U8, "wcp_w")
         nc.vector.tensor_copy(
             wcp_w[:].bitcast(U16).rearrange("p (h t m) -> p h t m", h=2, t=4),
             wc_w[:].bitcast(U16).rearrange("p (h m t) -> p h t m", h=2, t=4),
         )
-
-
-        nc.sync.dma_start(out=wd4_w.bitcast(I32), in_=wd4_words[0].bitcast(I32))
-        nc.sync.dma_start(out=wd8_w.bitcast(I32), in_=wd8_words[0].rearrange("p n i -> p (n i)").bitcast(I32))
-        nc.sync.dma_start(out=res_sb[:], in_=res.rearrange("(a p) j -> p a j", p=P))
-        load_scale_rows(nc.sync, wd8_s, wd8_scales[0])
-        load_scale_rows(nc.sync, wd4_s, wd4_scales[0])
-
-
-        c_bf = [
-            keep.tile([P, QUARTER, 4], BF16, name="c_bf0", align_bytes=64),
-            dealt.tile([P, QUARTER, 4], BF16, name="c_bf1", align_bytes=64, offset=R),
-        ]
-        nc.scalar.copy(
-            c_bf[0][:].rearrange("p (a b) i -> p a i b", b=4), c_raw[0][:].rearrange("p i (a b) -> p a i b", b=4)
+        nc.vector.tensor_copy(
+            wcp_s[:].rearrange("p (h t m) -> p h t m", h=2, t=4),
+            wc_s[:].rearrange("p (h m t) -> p h t m", h=2, t=4),
         )
-        nc.gpsimd.tensor_scalar(c_bf[1][:], c_raw[1][:].rearrange("p i j -> p j i"), 1.0, 0.0, ALU.mult, ALU.add)
-        c_codes = reuse.tile([P, J], U32, name="c_codes", tag="c", align_bytes=64)
-        c_sc = keep.tile([P, J], U8, name="c_sc", align_bytes=64)
 
-        def quantize_c():
-            for q in range(2):
-                nc.vector.quantize_mx(
-                    out=c_codes[:, QUARTER * q : QUARTER * (q + 1)].bitcast(E4),
-                    scales=c_sc[:, QUARTER * q : QUARTER * (q + 1)],
-                    in_=c_bf[q][:].rearrange("p j i -> p (j i)"),
-                )
+        picked_w = []
+
+        def gather_words(g, dst):
+            picked_w.append(dst)
+            nc.vector.tensor_copy(
+                dst[:].bitcast(U32),
+                table_w[:].bitcast(U32).indirect(offsets[:, g * (J // 16) : (g + 1) * (J // 16)]),
+            )
+
+        c_codes = tile([P, J], U32, "c_codes")
+        c_sc = tile([P, J], U8, "c_sc")
+
+        def quantize_c(q, c_bf):
+            nc.vector.quantize_mx(
+                out=c_codes[:, QUARTER * q : QUARTER * (q + 1)].bitcast(E4),
+                scales=c_sc[:, QUARTER * q : QUARTER * (q + 1)],
+                in_=c_bf[:].rearrange("p j i -> p (j i)"),
+            )
+
+        for g in range(G - 1):
+            gather_words(g, tile([P, J], I32, f"picked_w{g}"))
+        c_bf0 = tile([P, QUARTER, 4], BF16, "c_bf0", on_c_bf, 0)
+        nc.scalar.copy(
+            c_bf0[:].rearrange("p (a b) i -> p a i b", b=4), c_raw[0][:].rearrange("p i (a b) -> p a i b", b=4)
+        )
+        quantize_c(0, c_bf0)
+        gather_words(G - 1, tile([P, J], I32, "picked_w3", on_c_bf, 0))
+        c_bf1 = tile([P, QUARTER, 4], BF16, "c_bf1", on_table, 0)
+        nc.gpsimd.tensor_scalar(c_bf1[:], c_raw[1][:].rearrange("p i j -> p j i"), 1.0, 0.0, ALU.mult, ALU.add)
 
         used_banks = []
 
@@ -174,21 +158,20 @@ def tile_list_pnet_mix_res_kernel(
             used_banks.append(shape)
             return psum.tile(shape, F32, name="bank", tag=f"bank{len(used_banks) % 8}")
 
-        best, own = {}, {}
-        for u in range(8):
-            if u == POOLED - 1:
-                best[u] = late.tile([P, P, 4], F32, name=f"best{u}", align_bytes=64, offset=2048)
-                own[u] = late.tile([P, P, 4], F32, name=f"own{u}", align_bytes=64, offset=4096)
-            elif u != FOLD:
-                if u != 2:
-                    best[u] = keep.tile([P, P, 4], F32, name=f"best{u}", align_bytes=64)
-                if u != LAST:
-                    own[u] = keep.tile([P, P, 4], F32, name=f"own{u}", align_bytes=64)
-        first = [early.tile([P, P, 4], F32, name=f"first{u}", align_bytes=64, offset=2048 * (u + max(0, min(u, 4) - 2)))
-            for u in range(8)]
-        pre = [None, keep.tile([P, 4, P, 4], BF16, name="pre1", align_bytes=64)]
-        h_bf = [keep.tile([P, 4, P, 4], BF16, name=f"h_bf{h}", align_bytes=64) for h in range(2)]
-        folded = keep.tile([P, G, P, 4], BF16, name="folded", align_bytes=64)
+        first = [tile([P, P, 4], F32, f"first{u}", on_c_raw, 2048 * u) for u in range(2)]
+        first = first + [tile([P, P, 4], F32, f"first{u}") for u in range(2, FOLD)]
+        best = [
+            tile([P, P, 4], F32, f"best{u}", on_table, 0) if u == 2 else tile([P, P, 4], F32, f"best{u}")
+            for u in range(FOLD)
+        ]
+        own = [tile([P, P, 4], F32, f"own{u}", on_w_raw, 2048 * u) for u in range(2)]
+        own = own + [tile([P, P, 4], F32, f"own{u}") for u in range(2, LAST)]
+        pre = [tile([P, P, 4], BF16, f"pre{u}") for u in range(FOLD)]
+        h_bf = [tile([P, 4, P, 4], BF16, f"h_bf{h}") for h in range(2)]
+        folded = tile([P, G, P, 4], BF16, "folded")
+        pair_max = tile([P, 2, P, 4], BF16, "pair_max")
+        h_codes = [tile([P, J], U32, f"h_codes{h}") for h in range(2)]
+        h_sc = [tile([P, J], U8, f"h_sc{h}") for h in range(2)]
 
         def own_pass(bank, u, t, start):
             h, cols = u // 4, slice(u % 4 * P, (u % 4 + 1) * P)
@@ -236,61 +219,13 @@ def tile_list_pnet_mix_res_kernel(
             nc.scalar.copy(own[u][:], own_bank(u))
 
         def add_own(u):
-            nc.gpsimd.tensor_tensor(pre[u // 4][:, u % 4, :, :], best[u][:], own[u][:], ALU.add)
+            nc.gpsimd.tensor_tensor(pre[u][:], best[u][:], own[u][:], ALU.add)
 
         def relu(u):
-            nc.scalar.activation(h_bf[u // 4][:, u % 4, :, :], pre[u // 4][:, u % 4, :, :], ACT.Relu)
+            nc.scalar.activation(h_bf[u // 4][:, u % 4, :, :], pre[u][:], ACT.Relu)
 
-        chained = [u for u in range(8) if u != FOLD]
-        neighbour(0, 0)
-        for s, u in enumerate(chained):
-            if u != LAST:
-                neighbour(u, 1)
-            else:
-                neighbour(u, 2)
-            if s + 1 < len(chained):
-                neighbour(chained[s + 1], 0)
-            if s > 0:
-                neighbour(chained[s - 1], 3)
-            if s in (2, 3, 4):
-                own_part(2 * (s - 2))
-            if s == 5:
-                relu(0)
-                relu(1)
-            if s == 6:
-                relu(2)
-                relu(3)
-            if s == 5:
-                neighbour(LAST, 1)
-            if u != LAST:
-                neighbour(u, 2)
-            if s in (2, 3, 4):
-                own_part(2 * (s - 2) + 1)
-            if s == 6:
-                neighbour(FOLD, 0)
-            if s == 0:
-                cast_w(2)
-            if s == 1:
-                cast_w(3)
-                quantize_c()
-                quantize_w(1)
-                pre[0] = second.tile([P, 4, P, 4], BF16, name="pre0", align_bytes=64, offset=2048)
-                best[2] = second.tile([P, P, 4], F32, name="best2", align_bytes=64, offset=0)
-            if s == 2:
-                add_own(0)
-            if s >= 2:
-                add_own(s - 1)
-        neighbour(LAST, 3)
-        neighbour(FOLD, 1)
-        nc.vector.tensor_tensor(pre[1][:, 2, :, :], best[LAST][:], own_bank(LAST), ALU.add)
-        neighbour(FOLD, 2)
-        neighbour(FOLD, 3)
-
-        pair_max = late.tile([P, 2, P, 4], BF16, name="pair_max", align_bytes=64, offset=64)
-        h_codes = [late.tile([P, J], U32, name=f"h_codes{h}", align_bytes=64, offset=2112 + 2048 * h) for h in range(2)]
-        h_sc = [keep.tile([P, J], U8, name=f"h_sc{h}", align_bytes=64) for h in range(2)]
-
-        def quantize_h(h, jt, n):
+        def quantize_h(u, n=1):
+            h, jt = u // 4, u % 4
             cols = slice(jt * P, (jt + n) * P)
             nc.vector.quantize_mx(
                 out=h_codes[h][:, cols].bitcast(E4),
@@ -298,11 +233,70 @@ def tile_list_pnet_mix_res_kernel(
                 in_=h_bf[h][:, jt : jt + n, :, :].rearrange("p u j t -> p (u j t)"),
             )
 
+        neighbour(0, 0)
+        neighbour(1, 0)
+        neighbour(2, 0)
+        neighbour(0, 1)
+        cast_w(1, 0)
+        cast_w(1, 1)
+        neighbour(1, 1)
+        neighbour(0, 2)
+        neighbour(1, 2)
+        neighbour(0, 3)
+        own_part(0)
+        own_part(1)
+        quantize_c(1, c_bf1)
+        add_own(0)
+        neighbour(2, 1)
+        neighbour(1, 3)
+        neighbour(3, 0)
+        quantize_w(1)
+        add_own(1)
+        neighbour(2, 2)
+        neighbour(3, 1)
+        own_part(2)
+        neighbour(2, 3)
+        add_own(2)
+        relu(0)
+        neighbour(3, 2)
+        neighbour(4, 0)
+        own_part(3)
+        relu(1)
+        neighbour(4, 1)
+        neighbour(3, 3)
+        quantize_h(0, 2)
+        add_own(3)
+        neighbour(5, 0)
+        own_part(4)
+        neighbour(4, 2)
+        relu(2)
+        neighbour(5, 1)
+        neighbour(6, 0)
+        neighbour(4, 3)
+        quantize_h(2)
+        add_own(4)
+        own_part(5)
+        neighbour(6, 1)
+        neighbour(FOLD, 0)
+        relu(3)
+        neighbour(5, 2)
+        neighbour(FOLD, 1)
+        neighbour(6, 2)
+        neighbour(5, 3)
+        quantize_h(3)
+        add_own(5)
+        neighbour(FOLD, 2)
+        relu(4)
+        neighbour(6, 3)
+        neighbour(FOLD, 3)
+        nc.vector.tensor_tensor(pre[LAST][:], best[LAST][:], own_bank(LAST), ALU.add)
+        relu(5)
+
         out_v = out.rearrange("(a p) j -> p a j", p=P)
 
-        def open_layer(jt, n):
-            cols = slice(jt * P, (jt + n) * P)
-            y = next_bank([P, 2, n * P])
+        def open_layer(jt):
+            cols = slice(jt * P, (jt + 1) * P)
+            y = next_bank([P, 2, P])
             for a in range(2):
                 nc.tensor.matmul_mx(
                     out=y[:, a, :],
@@ -315,36 +309,37 @@ def tile_list_pnet_mix_res_kernel(
                 )
             return y
 
-        def close_layer(y, jt, n):
+        def close_layer(y, jt):
+            cols = slice(jt * P, (jt + 1) * P)
             for a in range(2):
-                for k in range(n):
-                    cols = slice((jt + k) * P, (jt + k + 1) * P)
-                    nc.tensor.matmul_mx(
-                        out=y[:, a, k * P : (k + 1) * P],
-                        lhsT=wd4_w[:, 2 * P * a : 2 * P * (a + 1)].bitcast(E2),
-                        lhsT_scale=wd4_s[:, P * a : P * (a + 1)],
-                        rhs=h_codes[1][:, cols].bitcast(E4),
-                        rhs_scale=h_sc[1][:, cols],
-                        start=False,
-                        stop=a == 1 and k == n - 1,
-                    )
+                nc.tensor.matmul_mx(
+                    out=y[:, a, :],
+                    lhsT=wd4_w[:, 2 * P * a : 2 * P * (a + 1)].bitcast(E2),
+                    lhsT_scale=wd4_s[:, P * a : P * (a + 1)],
+                    rhs=h_codes[1][:, cols].bitcast(E4),
+                    rhs_scale=h_sc[1][:, cols],
+                    start=False,
+                    stop=a == 1,
+                )
 
-        def finish(y, jt, n):
-            cols = slice(jt * P, (jt + n) * P)
-            o = keep.tile([P, 2, n * P], F32, name=f"o{jt}", align_bytes=64)
+        def finish(y, jt):
+            cols = slice(jt * P, (jt + 1) * P)
+            o = tile([P, 2, P], F32, f"o{jt}")
             nc.vector.tensor_tensor(o[:], res_sb[:, :, cols], y[:], ALU.add)
             nc.sync.dma_start(out=out_v[:, :, cols], in_=o[:])
 
-        quantize_h(0, 0, 4)
-        y = [open_layer(jt, 1) for jt in range(4)]
-        nc.vector.tensor_scalar_max(h_bf[1][:, 0:3, :, :], pre[1][:, 0:3, :, :], 0.0)
+        y = [open_layer(jt) for jt in range(4)]
+        quantize_h(4)
+        close_layer(y[0], 0)
+        nc.vector.tensor_scalar_max(h_bf[1][:, 2, :, :], pre[LAST][:], 0.0)
         nc.vector.tensor_tensor(pair_max[:], folded[:, 0:2, :, :], folded[:, 2:4, :, :], ALU.max)
-        quantize_h(1, 0, 2)
-        close_layer(y[0], 0, 1)
-        close_layer(y[1], 1, 1)
+        quantize_h(LAST)
+        close_layer(y[2], 2)
         nc.vector.tensor_tensor(h_bf[1][:, 3, :, :], pair_max[:, 0, :, :], pair_max[:, 1, :, :], ALU.max)
-        for jt in (2, 3):
-            quantize_h(1, jt, 1)
-            close_layer(y[jt], jt, 1)
-        for jt in range(4):
-            finish(y[jt], jt, 1)
+        quantize_h(5)
+        close_layer(y[1], 1)
+        finish(y[0], 0)
+        quantize_h(FOLD)
+        close_layer(y[3], 3)
+        for jt in (2, 1, 3):
+            finish(y[jt], jt)

@@ -35,10 +35,11 @@ def tile_list_pnet_mix_res_kernel(
     nc = tc.nc
     with ExitStack() as ctx:
         keep = ctx.enter_context(tc.tile_pool(name="keep", bufs=1))
-        on_table = ctx.enter_context(tc.tile_pool(name="on_table", bufs=1))
-        on_c_raw = ctx.enter_context(tc.tile_pool(name="on_c_raw", bufs=1))
         on_w_raw = ctx.enter_context(tc.tile_pool(name="on_w_raw", bufs=1))
-        on_c_bf = ctx.enter_context(tc.tile_pool(name="on_c_bf", bufs=1))
+        on_w_bf0 = ctx.enter_context(tc.tile_pool(name="on_w_bf0", bufs=1))
+        on_w_bf1 = ctx.enter_context(tc.tile_pool(name="on_w_bf1", bufs=1))
+        on_wc = ctx.enter_context(tc.tile_pool(name="on_wc", bufs=1))
+        on_last = ctx.enter_context(tc.tile_pool(name="on_last", bufs=1))
         psum = ctx.enter_context(tc.psum_pool(name="psum", bufs=1))
 
         def tile(shape, dtype, name, pool=keep, offset=None):
@@ -62,28 +63,28 @@ def tile_list_pnet_mix_res_kernel(
         nc.vector.memset(picked_s[:].bitcast(I32), 0)
         nc.vector.memset(wd_s[:].bitcast(I32), 0)
 
-        wc_w = tile([P, 2 * R], U8, "wc_w")
-        table_w = tile([P, T], I32, "table_w", on_table, 0)
-        w_raw0 = [tile([P, 4, QUARTER], F32, f"w_raw0{q}") for q in range(2)]
-        w_raw1 = tile([P, 4, HALF], F32, "w_raw1", on_w_raw, 0)
-        c_raw = [tile([P, 4, QUARTER], F32, "c_raw0", on_c_raw, 0), tile([P, 4, QUARTER], F32, "c_raw1")]
+        wc_w = tile([P, 2 * R], U8, "wc_w", on_wc, 0)
+        table_w = tile([P, T], I32, "table_w")
+        w_raw = [tile([P, 4, QUARTER], F32, f"w_raw{q}", on_w_raw, 4096 * q) for q in range(4)]
+        c_raw = [tile([P, 4, QUARTER], F32, f"c_raw{q}") for q in range(2)]
         wd8_w = tile([P, 4 * N], U8, "wd8_w")
         wd4_w = tile([P, 2 * N], U8, "wd4_w")
         res_sb = tile([P, 2, J], F32, "res_sb")
 
         nc.sync.dma_start(out=table_s[STAGE:P, :].bitcast(I32), in_=tab_scales[0].bitcast(I32))
-        nc.sync.dma_start(out=wc_w[:].bitcast(I32), in_=wc_words[0].bitcast(I32))
-        load_scale_rows(nc.sync, wc_s, wc_scales[0])
-        for q in range(2):
-            nc.sync.dma_start(out=w_raw0[q][:], in_=w_k[:, :, QUARTER * q : QUARTER * (q + 1)])
         nc.sync.dma_start(out=table_w[:], in_=tab_words[0].rearrange("p t i -> p (t i)").bitcast(I32))
+        for q in range(2):
+            nc.sync.dma_start(out=w_raw[q][:], in_=w_k[:, :, QUARTER * q : QUARTER * (q + 1)])
         nc.sync.dma_start(out=c_raw[0][:], in_=c_k[:, :, 0:QUARTER])
 
+        load_scale_rows(nc.scalar, wc_s, wc_scales[0])
         gathered_s = tile([P, G * J], U8, "gathered_s")
         nc.vector.tensor_copy(gathered_s[:], table_s[:].indirect(offsets[:]))
         for r in range(4):
             nc.sync.dma_start(out=picked_s[r:P:32, :].bitcast(I32), in_=gathered_s[STAGE + r : P : 4, :].bitcast(I32))
-        nc.sync.dma_start(out=w_raw1[:], in_=w_k[:, :, HALF:R])
+        nc.sync.dma_start(out=wc_w[:].bitcast(I32), in_=wc_words[0].bitcast(I32))
+        for q in (2, 3):
+            nc.sync.dma_start(out=w_raw[q][:], in_=w_k[:, :, QUARTER * q : QUARTER * (q + 1)])
         nc.sync.dma_start(out=c_raw[1][:], in_=c_k[:, :, QUARTER:J])
         nc.sync.dma_start(out=wd8_w[:].bitcast(I32), in_=wd8_words[0].rearrange("p n i -> p (n i)").bitcast(I32))
         nc.sync.dma_start(out=wd4_w[:].bitcast(I32), in_=wd4_words[0].bitcast(I32))
@@ -91,36 +92,20 @@ def tile_list_pnet_mix_res_kernel(
         load_scale_rows(nc.sync, wd4_s, wd4_scales[0])
         nc.sync.dma_start(out=res_sb[:], in_=res.rearrange("(a p) j -> p a j", p=P))
 
-        w_bf = [tile([P, 4, P, 4], BF16, f"w_bf{h}") for h in range(2)]
+        w_bf = [tile([P, 4, P, 4], BF16, "w_bf0", on_w_bf0, 0), tile([P, 4, P, 4], BF16, "w_bf1", on_w_bf1, 0)]
         w_codes = [tile([P, HALF], U32, f"w_codes{h}") for h in range(2)]
         w_sc = [tile([P, HALF], U8, f"w_sc{h}") for h in range(2)]
 
         def cast_w(h, q):
-            raw = w_raw0[q][:] if h == 0 else w_raw1[:, :, QUARTER * q : QUARTER * (q + 1)]
             nc.scalar.copy(
                 w_bf[h][:, :, 64 * q : 64 * (q + 1), :].rearrange("p t m i -> p m i t"),
-                raw.rearrange("p i (m t) -> p m i t", t=4),
+                w_raw[2 * h + q][:].rearrange("p i (m t) -> p m i t", t=4),
             )
 
         def quantize_w(h):
             nc.vector.quantize_mx(
                 out=w_codes[h][:].bitcast(E4), scales=w_sc[h][:], in_=w_bf[h][:].rearrange("p t m i -> p (t m i)")
             )
-
-        cast_w(0, 0)
-        cast_w(0, 1)
-        quantize_w(0)
-
-        wcp_s = tile([P, R], U8, "wcp_s")
-        wcp_w = tile([P, 2 * R], U8, "wcp_w")
-        nc.vector.tensor_copy(
-            wcp_w[:].bitcast(U16).rearrange("p (h t m) -> p h t m", h=2, t=4),
-            wc_w[:].bitcast(U16).rearrange("p (h m t) -> p h t m", h=2, t=4),
-        )
-        nc.vector.tensor_copy(
-            wcp_s[:].rearrange("p (h t m) -> p h t m", h=2, t=4),
-            wc_s[:].rearrange("p (h m t) -> p h t m", h=2, t=4),
-        )
 
         picked_w = []
 
@@ -143,13 +128,26 @@ def tile_list_pnet_mix_res_kernel(
 
         for g in range(G - 1):
             gather_words(g, tile([P, J], I32, f"picked_w{g}"))
-        c_bf0 = tile([P, QUARTER, 4], BF16, "c_bf0", on_c_bf, 0)
+        cast_w(0, 0)
+        cast_w(0, 1)
+        quantize_w(0)
+        gather_words(G - 1, tile([P, J], I32, "picked_w3", on_w_bf0, 0))
+        wcp_w = tile([P, 2 * R], U8, "wcp_w")
+        nc.vector.tensor_copy(
+            wcp_w[:].bitcast(U16).rearrange("p (h t m) -> p h t m", h=2, t=4),
+            wc_w[:].bitcast(U16).rearrange("p (h m t) -> p h t m", h=2, t=4),
+        )
+        wcp_s = tile([P, R], U8, "wcp_s")
+        nc.vector.tensor_copy(
+            wcp_s[:].rearrange("p (h t m) -> p h t m", h=2, t=4),
+            wc_s[:].rearrange("p (h m t) -> p h t m", h=2, t=4),
+        )
+        c_bf0 = tile([P, QUARTER, 4], BF16, "c_bf0")
         nc.scalar.copy(
             c_bf0[:].rearrange("p (a b) i -> p a i b", b=4), c_raw[0][:].rearrange("p i (a b) -> p a i b", b=4)
         )
         quantize_c(0, c_bf0)
-        gather_words(G - 1, tile([P, J], I32, "picked_w3", on_c_bf, 0))
-        c_bf1 = tile([P, QUARTER, 4], BF16, "c_bf1", on_table, 0)
+        c_bf1 = tile([P, QUARTER, 4], BF16, "c_bf1", on_wc, 0)
         nc.gpsimd.tensor_scalar(c_bf1[:], c_raw[1][:].rearrange("p i j -> p j i"), 1.0, 0.0, ALU.mult, ALU.add)
 
         used_banks = []
@@ -158,19 +156,20 @@ def tile_list_pnet_mix_res_kernel(
             used_banks.append(shape)
             return psum.tile(shape, F32, name="bank", tag=f"bank{len(used_banks) % 8}")
 
-        first = [tile([P, P, 4], F32, f"first{u}", on_c_raw, 2048 * u) for u in range(2)]
-        first = first + [tile([P, P, 4], F32, f"first{u}") for u in range(2, FOLD)]
-        best = [
-            tile([P, P, 4], F32, f"best{u}", on_table, 0) if u == 2 else tile([P, P, 4], F32, f"best{u}")
-            for u in range(FOLD)
-        ]
-        own = [tile([P, P, 4], F32, f"own{u}", on_w_raw, 2048 * u) for u in range(2)]
+        first = [None if u in (2, 3) else tile([P, P, 4], F32, f"first{u}") for u in range(FOLD)]
+        best = [tile([P, P, 4], F32, f"best{u}") for u in range(LAST)]
+        best.append(tile([P, P, 4], F32, "best6", on_last, 0))
+        second2 = tile([P, P, 4], F32, "second2", on_w_bf1, 2048)
+        own = [tile([P, P, 4], F32, f"own{u}", on_w_raw, 4096 * (2 + u)) for u in range(2)]
         own = own + [tile([P, P, 4], F32, f"own{u}") for u in range(2, LAST)]
-        pre = [tile([P, P, 4], BF16, f"pre{u}") for u in range(FOLD)]
+        for u in (2, 3):
+            first[u] = tile([P, P, 4], F32, f"first{u}", on_w_raw, 4096 * u + 2048)
+        pre = [tile([P, P, 4], BF16, f"pre{u}", on_wc, 1024 * u) for u in range(2)]
+        pre = pre + [tile([P, P, 4], BF16, f"pre{u}") for u in range(2, FOLD)]
         h_bf = [tile([P, 4, P, 4], BF16, f"h_bf{h}") for h in range(2)]
         folded = tile([P, G, P, 4], BF16, "folded")
         pair_max = tile([P, 2, P, 4], BF16, "pair_max")
-        h_codes = [tile([P, J], U32, f"h_codes{h}") for h in range(2)]
+        h_codes = [tile([P, J], U32, "h_codes0", on_last, 0), tile([P, J], U32, "h_codes1")]
         h_sc = [tile([P, J], U8, f"h_sc{h}") for h in range(2)]
 
         def own_pass(bank, u, t, start):
@@ -207,7 +206,8 @@ def tile_list_pnet_mix_res_kernel(
             elif g == 0:
                 nc.scalar.copy(first[u][:], woven)
             else:
-                nc.vector.tensor_tensor(best[u][:], (first if g == 1 else best)[u][:], woven, ALU.max)
+                steps = [first[u], best[u], second2 if u == 2 else best[u], best[u]]
+                nc.vector.tensor_tensor(steps[g][:], steps[g - 1][:], woven, ALU.max)
 
         def own_bank(u):
             bank = next_bank([P, 4, P])
@@ -235,61 +235,58 @@ def tile_list_pnet_mix_res_kernel(
 
         neighbour(0, 0)
         neighbour(1, 0)
-        neighbour(2, 0)
         neighbour(0, 1)
-        cast_w(1, 0)
-        cast_w(1, 1)
         neighbour(1, 1)
+        cast_w(1, 0)
         neighbour(0, 2)
+        neighbour(2, 0)
+        cast_w(1, 1)
         neighbour(1, 2)
         neighbour(0, 3)
+        neighbour(2, 1)
+        neighbour(3, 0)
+        neighbour(1, 3)
         own_part(0)
-        own_part(1)
+        quantize_w(1)
         quantize_c(1, c_bf1)
         add_own(0)
-        neighbour(2, 1)
-        neighbour(1, 3)
-        neighbour(3, 0)
-        quantize_w(1)
+        own_part(1)
         add_own(1)
-        neighbour(2, 2)
         neighbour(3, 1)
-        own_part(2)
-        neighbour(2, 3)
-        add_own(2)
-        relu(0)
-        neighbour(3, 2)
+        neighbour(2, 2)
         neighbour(4, 0)
-        own_part(3)
-        relu(1)
+        neighbour(3, 2)
+        neighbour(2, 3)
+        own_part(2)
+        add_own(2)
         neighbour(4, 1)
-        neighbour(3, 3)
-        quantize_h(0, 2)
-        add_own(3)
         neighbour(5, 0)
-        own_part(4)
+        neighbour(3, 3)
+        own_part(3)
+        add_own(3)
         neighbour(4, 2)
-        relu(2)
-        neighbour(5, 1)
         neighbour(6, 0)
+        relu(0)
+        neighbour(5, 1)
+        own_part(4)
         neighbour(4, 3)
-        quantize_h(2)
         add_own(4)
-        own_part(5)
+        relu(1)
         neighbour(6, 1)
-        neighbour(FOLD, 0)
-        relu(3)
+        own_part(5)
         neighbour(5, 2)
-        neighbour(FOLD, 1)
+        neighbour(FOLD, 0)
+        relu(2)
         neighbour(6, 2)
+        neighbour(FOLD, 1)
         neighbour(5, 3)
-        quantize_h(3)
         add_own(5)
-        neighbour(FOLD, 2)
-        relu(4)
+        relu(3)
         neighbour(6, 3)
-        neighbour(FOLD, 3)
+        neighbour(FOLD, 2)
         nc.vector.tensor_tensor(pre[LAST][:], best[LAST][:], own_bank(LAST), ALU.add)
+        neighbour(FOLD, 3)
+        relu(4)
         relu(5)
 
         out_v = out.rearrange("(a p) j -> p a j", p=P)
@@ -328,11 +325,12 @@ def tile_list_pnet_mix_res_kernel(
             nc.vector.tensor_tensor(o[:], res_sb[:, :, cols], y[:], ALU.add)
             nc.sync.dma_start(out=out_v[:, :, cols], in_=o[:])
 
+        quantize_h(0, 4)
         y = [open_layer(jt) for jt in range(4)]
-        quantize_h(4)
-        close_layer(y[0], 0)
         nc.vector.tensor_scalar_max(h_bf[1][:, 2, :, :], pre[LAST][:], 0.0)
         nc.vector.tensor_tensor(pair_max[:], folded[:, 0:2, :, :], folded[:, 2:4, :, :], ALU.max)
+        quantize_h(4)
+        close_layer(y[0], 0)
         quantize_h(LAST)
         close_layer(y[2], 2)
         nc.vector.tensor_tensor(h_bf[1][:, 3, :, :], pair_max[:, 0, :, :], pair_max[:, 1, :, :], ALU.max)

@@ -20,6 +20,7 @@ P = 128
 HALF = 512
 QUARTER = 256
 STAGE = P - 16
+HALVES = (slice(0, P // 2), slice(P // 2, P))
 LAST = 6
 FOLD = 7
 
@@ -36,7 +37,6 @@ def tile_list_pnet_mix_res_kernel(
     with ExitStack() as ctx:
         keep = ctx.enter_context(tc.tile_pool(name="keep", bufs=1))
         on_w_raw = ctx.enter_context(tc.tile_pool(name="on_w_raw", bufs=1))
-        on_w_bf0 = ctx.enter_context(tc.tile_pool(name="on_w_bf0", bufs=1))
         on_w_bf1 = ctx.enter_context(tc.tile_pool(name="on_w_bf1", bufs=1))
         on_wc = ctx.enter_context(tc.tile_pool(name="on_wc", bufs=1))
         on_last = ctx.enter_context(tc.tile_pool(name="on_last", bufs=1))
@@ -83,16 +83,16 @@ def tile_list_pnet_mix_res_kernel(
         for r in range(4):
             nc.sync.dma_start(out=picked_s[r:P:32, :].bitcast(I32), in_=gathered_s[STAGE + r : P : 4, :].bitcast(I32))
         nc.sync.dma_start(out=wc_w[:].bitcast(I32), in_=wc_words[0].bitcast(I32))
-        for q in (2, 3):
-            nc.sync.dma_start(out=w_raw[q][:], in_=w_k[:, :, QUARTER * q : QUARTER * (q + 1)])
+        nc.sync.dma_start(out=w_raw[2][:], in_=w_k[:, :, QUARTER * 2 : QUARTER * 3])
         nc.sync.dma_start(out=c_raw[1][:], in_=c_k[:, :, QUARTER:J])
+        nc.sync.dma_start(out=w_raw[3][:], in_=w_k[:, :, QUARTER * 3 : R])
         nc.sync.dma_start(out=wd8_w[:].bitcast(I32), in_=wd8_words[0].rearrange("p n i -> p (n i)").bitcast(I32))
         nc.sync.dma_start(out=wd4_w[:].bitcast(I32), in_=wd4_words[0].bitcast(I32))
         load_scale_rows(nc.sync, wd8_s, wd8_scales[0])
         load_scale_rows(nc.sync, wd4_s, wd4_scales[0])
         nc.sync.dma_start(out=res_sb[:], in_=res.rearrange("(a p) j -> p a j", p=P))
 
-        w_bf = [tile([P, 4, P, 4], BF16, "w_bf0", on_w_bf0, 0), tile([P, 4, P, 4], BF16, "w_bf1", on_w_bf1, 0)]
+        w_bf = [tile([P, 4, P, 4], BF16, "w_bf0"), tile([P, 4, P, 4], BF16, "w_bf1", on_w_bf1, 0)]
         w_codes = [tile([P, HALF], U32, f"w_codes{h}") for h in range(2)]
         w_sc = [tile([P, HALF], U8, f"w_sc{h}") for h in range(2)]
 
@@ -131,7 +131,7 @@ def tile_list_pnet_mix_res_kernel(
         cast_w(0, 0)
         cast_w(0, 1)
         quantize_w(0)
-        gather_words(G - 1, tile([P, J], I32, "picked_w3", on_w_bf0, 0))
+        gather_words(G - 1, tile([P, J], I32, "picked_w3", on_w_raw, 4096))
         wcp_w = tile([P, 2 * R], U8, "wcp_w")
         nc.vector.tensor_copy(
             wcp_w[:].bitcast(U16).rearrange("p (h t m) -> p h t m", h=2, t=4),
@@ -157,15 +157,18 @@ def tile_list_pnet_mix_res_kernel(
             return psum.tile(shape, F32, name="bank", tag=f"bank{len(used_banks) % 8}")
 
         first = [None if u in (2, 3) else tile([P, P, 4], F32, f"first{u}") for u in range(FOLD)]
-        best = [tile([P, P, 4], F32, f"best{u}") for u in range(LAST)]
-        best.append(tile([P, P, 4], F32, "best6", on_last, 0))
+        best = [None if u == 5 else tile([P, P, 4], F32, f"best{u}") for u in range(LAST)]
+        best.append(tile([P, P, 4], F32, "best6"))
+        best[5] = tile([P, P, 4], F32, "best5", on_last, 0)
         second2 = tile([P, P, 4], F32, "second2", on_w_bf1, 2048)
         own = [tile([P, P, 4], F32, f"own{u}", on_w_raw, 4096 * (2 + u)) for u in range(2)]
         own = own + [tile([P, P, 4], F32, f"own{u}") for u in range(2, LAST)]
         for u in (2, 3):
             first[u] = tile([P, P, 4], F32, f"first{u}", on_w_raw, 4096 * u + 2048)
-        pre = [tile([P, P, 4], BF16, f"pre{u}", on_wc, 1024 * u) for u in range(2)]
-        pre = pre + [tile([P, P, 4], BF16, f"pre{u}") for u in range(2, FOLD)]
+        pre = [tile([P, P, 4], BF16, f"pre{u}", on_w_bf1, 1024 * u) for u in range(2)]
+        pre = pre + [tile([P, P, 4], BF16, f"pre{u}") for u in range(2, 5)]
+        pre_last = tile([P, 2, P, 4], BF16, "pre_last")
+        pre = pre + [pre_last[:, 0, :, :], pre_last[:, 1, :, :]]
         h_bf = [tile([P, 4, P, 4], BF16, f"h_bf{h}") for h in range(2)]
         folded = tile([P, G, P, 4], BF16, "folded")
         pair_max = tile([P, 2, P, 4], BF16, "pair_max")
@@ -205,6 +208,9 @@ def tile_list_pnet_mix_res_kernel(
                 nc.scalar.activation(folded[:, g, :, :], woven, ACT.Relu)
             elif g == 0:
                 nc.scalar.copy(first[u][:], woven)
+            elif u == LAST and g > 1:
+                for cols in HALVES:
+                    nc.vector.tensor_tensor(best[u][:, cols, :], best[u][:, cols, :], woven[:, cols, :], ALU.max)
             else:
                 steps = [first[u], best[u], second2 if u == 2 else best[u], best[u]]
                 nc.vector.tensor_tensor(steps[g][:], steps[g - 1][:], woven, ALU.max)
@@ -240,54 +246,55 @@ def tile_list_pnet_mix_res_kernel(
         cast_w(1, 0)
         neighbour(0, 2)
         neighbour(2, 0)
-        cast_w(1, 1)
         neighbour(1, 2)
         neighbour(0, 3)
+        quantize_c(1, c_bf1)
+        own_part(0)
+        cast_w(1, 1)
         neighbour(2, 1)
         neighbour(3, 0)
         neighbour(1, 3)
-        own_part(0)
-        quantize_w(1)
-        quantize_c(1, c_bf1)
-        add_own(0)
         own_part(1)
+        quantize_w(1)
+        add_own(0)
         add_own(1)
         neighbour(3, 1)
         neighbour(2, 2)
+        own_part(2)
         neighbour(4, 0)
         neighbour(3, 2)
         neighbour(2, 3)
-        own_part(2)
         add_own(2)
+        own_part(3)
         neighbour(4, 1)
         neighbour(5, 0)
         neighbour(3, 3)
-        own_part(3)
         add_own(3)
-        neighbour(4, 2)
-        neighbour(6, 0)
         relu(0)
-        neighbour(5, 1)
+        neighbour(4, 2)
         own_part(4)
+        neighbour(5, 1)
+        neighbour(6, 0)
+        relu(1)
         neighbour(4, 3)
         add_own(4)
-        relu(1)
-        neighbour(6, 1)
         own_part(5)
         neighbour(5, 2)
-        neighbour(FOLD, 0)
         relu(2)
-        neighbour(6, 2)
-        neighbour(FOLD, 1)
+        neighbour(6, 1)
+        neighbour(FOLD, 0)
         neighbour(5, 3)
         add_own(5)
         relu(3)
-        neighbour(6, 3)
+        neighbour(FOLD, 1)
+        neighbour(6, 2)
         neighbour(FOLD, 2)
-        nc.vector.tensor_tensor(pre[LAST][:], best[LAST][:], own_bank(LAST), ALU.add)
-        neighbour(FOLD, 3)
+        neighbour(6, 3)
+        last_own = own_bank(LAST)
+        for cols in HALVES:
+            nc.vector.tensor_tensor(pre[LAST][:, cols, :], best[LAST][:, cols, :], last_own[:, cols, :], ALU.add)
         relu(4)
-        relu(5)
+        neighbour(FOLD, 3)
 
         out_v = out.rearrange("(a p) j -> p a j", p=P)
 
@@ -327,17 +334,16 @@ def tile_list_pnet_mix_res_kernel(
 
         quantize_h(0, 4)
         y = [open_layer(jt) for jt in range(4)]
-        nc.vector.tensor_scalar_max(h_bf[1][:, 2, :, :], pre[LAST][:], 0.0)
-        nc.vector.tensor_tensor(pair_max[:], folded[:, 0:2, :, :], folded[:, 2:4, :, :], ALU.max)
         quantize_h(4)
         close_layer(y[0], 0)
-        quantize_h(LAST)
+        nc.vector.tensor_scalar_max(h_bf[1][:, 1:3, :, :], pre_last[:], 0.0)
+        nc.vector.tensor_tensor(pair_max[:], folded[:, 0:2, :, :], folded[:, 2:4, :, :], ALU.max)
+        quantize_h(5, 2)
+        close_layer(y[1], 1)
         close_layer(y[2], 2)
         nc.vector.tensor_tensor(h_bf[1][:, 3, :, :], pair_max[:, 0, :, :], pair_max[:, 1, :, :], ALU.max)
-        quantize_h(5)
-        close_layer(y[1], 1)
         finish(y[0], 0)
         quantize_h(FOLD)
         close_layer(y[3], 3)
-        for jt in (2, 1, 3):
+        for jt in (1, 2, 3):
             finish(y[jt], jt)

@@ -19,7 +19,6 @@ ACT = mybir.ActivationFunctionType
 P = 128
 HALF = 512
 QUARTER = 256
-STAGE = P - 16
 HALVES = (slice(0, P // 2), slice(P // 2, P))
 LAST = 6
 FOLD = 7
@@ -40,6 +39,7 @@ def tile_list_pnet_mix_res_kernel(
         on_w_bf1 = ctx.enter_context(tc.tile_pool(name="on_w_bf1", bufs=1))
         on_wc = ctx.enter_context(tc.tile_pool(name="on_wc", bufs=1))
         on_last = ctx.enter_context(tc.tile_pool(name="on_last", bufs=1))
+        on_w_raw3 = ctx.enter_context(tc.tile_pool(name="on_w_raw3", bufs=1))
         psum = ctx.enter_context(tc.psum_pool(name="psum", bufs=1))
 
         def tile(shape, dtype, name, pool=keep, offset=None):
@@ -59,29 +59,30 @@ def tile_list_pnet_mix_res_kernel(
         wd_s = tile([P, 2 * N], U8, "wd_s")
         wd8_s, wd4_s = wd_s[:, 0:N], wd_s[:, N : 2 * N]
         nc.vector.memset(wc_s[:].bitcast(I32), 0)
-        nc.vector.memset(table_s[0:STAGE, :].bitcast(I32), 0)
+        nc.vector.memset(table_s[:].bitcast(I32), 0)
         nc.vector.memset(picked_s[:].bitcast(I32), 0)
         nc.vector.memset(wd_s[:].bitcast(I32), 0)
 
         wc_w = tile([P, 2 * R], U8, "wc_w", on_wc, 0)
         table_w = tile([P, T], I32, "table_w")
-        w_raw = [tile([P, 4, QUARTER], F32, f"w_raw{q}", on_w_raw, 4096 * q) for q in range(4)]
+        w_raw = [tile([P, 4, QUARTER], F32, f"w_raw{q}", on_w_raw, 4096 * q) for q in range(3)]
+        w_raw.append(tile([P, 4, QUARTER], F32, "w_raw3", on_w_raw3, 1024))
         c_raw = [tile([P, 4, QUARTER], F32, f"c_raw{q}") for q in range(2)]
         wd8_w = tile([P, 4 * N], U8, "wd8_w")
         wd4_w = tile([P, 2 * N], U8, "wd4_w")
         res_sb = tile([P, 2, J], F32, "res_sb")
 
-        nc.sync.dma_start(out=table_s[STAGE:P, :].bitcast(I32), in_=tab_scales[0].bitcast(I32))
+        load_scale_rows(nc.sync, wc_s, wc_scales[0])
+        nc.sync.dma_start(out=table_s[0:P:8, :].bitcast(I32), in_=tab_scales[0].bitcast(I32))
         nc.sync.dma_start(out=table_w[:], in_=tab_words[0].rearrange("p t i -> p (t i)").bitcast(I32))
         for q in range(2):
             nc.sync.dma_start(out=w_raw[q][:], in_=w_k[:, :, QUARTER * q : QUARTER * (q + 1)])
         nc.sync.dma_start(out=c_raw[0][:], in_=c_k[:, :, 0:QUARTER])
 
-        load_scale_rows(nc.scalar, wc_s, wc_scales[0])
         gathered_s = tile([P, G * J], U8, "gathered_s")
         nc.vector.tensor_copy(gathered_s[:], table_s[:].indirect(offsets[:]))
         for r in range(4):
-            nc.sync.dma_start(out=picked_s[r:P:32, :].bitcast(I32), in_=gathered_s[STAGE + r : P : 4, :].bitcast(I32))
+            nc.sync.dma_start(out=picked_s[r:P:32, :].bitcast(I32), in_=gathered_s[8 * r : P : 32, :].bitcast(I32))
         nc.sync.dma_start(out=wc_w[:].bitcast(I32), in_=wc_words[0].bitcast(I32))
         nc.sync.dma_start(out=w_raw[2][:], in_=w_k[:, :, QUARTER * 2 : QUARTER * 3])
         nc.sync.dma_start(out=c_raw[1][:], in_=c_k[:, :, QUARTER:J])
@@ -128,9 +129,15 @@ def tile_list_pnet_mix_res_kernel(
 
         for g in range(G - 1):
             gather_words(g, tile([P, J], I32, f"picked_w{g}"))
-        cast_w(0, 0)
-        cast_w(0, 1)
-        quantize_w(0)
+        for q in range(2):
+            cast_w(0, q)
+            for t in range(4):
+                cols = slice(P * t + 64 * q, P * t + 64 * (q + 1))
+                nc.vector.quantize_mx(
+                    out=w_codes[0][:, cols].bitcast(E4),
+                    scales=w_sc[0][:, cols],
+                    in_=w_bf[0][:, t, 64 * q : 64 * (q + 1), :].rearrange("p m i -> p (m i)"),
+                )
         gather_words(G - 1, tile([P, J], I32, "picked_w3", on_w_raw, 4096))
         wcp_w = tile([P, 2 * R], U8, "wcp_w")
         nc.vector.tensor_copy(
@@ -160,15 +167,15 @@ def tile_list_pnet_mix_res_kernel(
         best = [None if u == 5 else tile([P, P, 4], F32, f"best{u}") for u in range(LAST)]
         best.append(tile([P, P, 4], F32, "best6"))
         best[5] = tile([P, P, 4], F32, "best5", on_last, 0)
-        second2 = tile([P, P, 4], F32, "second2", on_w_bf1, 2048)
-        own = [tile([P, P, 4], F32, f"own{u}", on_w_raw, 4096 * (2 + u)) for u in range(2)]
+        second2 = tile([P, P, 4], F32, "second2", on_w_raw3, 0)
+        own = [tile([P, P, 4], F32, "own0", on_w_raw, 4096 * 2), tile([P, P, 4], F32, "own1", on_w_raw3, 4096)]
         own = own + [tile([P, P, 4], F32, f"own{u}") for u in range(2, LAST)]
-        for u in (2, 3):
-            first[u] = tile([P, P, 4], F32, f"first{u}", on_w_raw, 4096 * u + 2048)
+        first[2] = tile([P, P, 4], F32, "first2", on_w_raw, 4096 * 2 + 2048)
+        first[3] = tile([P, P, 4], F32, "first3", on_w_raw3, 2048)
         pre = [tile([P, P, 4], BF16, f"pre{u}", on_w_bf1, 1024 * u) for u in range(2)]
-        pre = pre + [tile([P, P, 4], BF16, f"pre{u}") for u in range(2, 5)]
-        pre_last = tile([P, 2, P, 4], BF16, "pre_last")
-        pre = pre + [pre_last[:, 0, :, :], pre_last[:, 1, :, :]]
+        pre = pre + [tile([P, P, 4], BF16, f"pre{u}") for u in range(2, 4)]
+        pre_late = tile([P, 3, P, 4], BF16, "pre_late")
+        pre = pre + [pre_late[:, k, :, :] for k in range(3)]
         h_bf = [tile([P, 4, P, 4], BF16, f"h_bf{h}") for h in range(2)]
         folded = tile([P, G, P, 4], BF16, "folded")
         pair_max = tile([P, 2, P, 4], BF16, "pair_max")
@@ -258,12 +265,12 @@ def tile_list_pnet_mix_res_kernel(
         quantize_w(1)
         add_own(0)
         add_own(1)
-        neighbour(3, 1)
         neighbour(2, 2)
+        neighbour(3, 1)
         own_part(2)
         neighbour(4, 0)
-        neighbour(3, 2)
         neighbour(2, 3)
+        neighbour(3, 2)
         add_own(2)
         own_part(3)
         neighbour(4, 1)
@@ -288,12 +295,11 @@ def tile_list_pnet_mix_res_kernel(
         relu(3)
         neighbour(FOLD, 1)
         neighbour(6, 2)
-        neighbour(FOLD, 2)
         neighbour(6, 3)
         last_own = own_bank(LAST)
         for cols in HALVES:
             nc.vector.tensor_tensor(pre[LAST][:, cols, :], best[LAST][:, cols, :], last_own[:, cols, :], ALU.add)
-        relu(4)
+        neighbour(FOLD, 2)
         neighbour(FOLD, 3)
 
         out_v = out.rearrange("(a p) j -> p a j", p=P)
@@ -332,11 +338,12 @@ def tile_list_pnet_mix_res_kernel(
             nc.vector.tensor_tensor(o[:], res_sb[:, :, cols], y[:], ALU.add)
             nc.sync.dma_start(out=out_v[:, :, cols], in_=o[:])
 
+        nc.vector.tensor_scalar_max(h_bf[1][:, 0:2, :, :], pre_late[:, 0:2, :, :], 0.0)
         quantize_h(0, 4)
         y = [open_layer(jt) for jt in range(4)]
         quantize_h(4)
         close_layer(y[0], 0)
-        nc.vector.tensor_scalar_max(h_bf[1][:, 1:3, :, :], pre_last[:], 0.0)
+        nc.vector.tensor_scalar_max(h_bf[1][:, 2, :, :], pre[LAST], 0.0)
         nc.vector.tensor_tensor(pair_max[:], folded[:, 0:2, :, :], folded[:, 2:4, :, :], ALU.max)
         quantize_h(5, 2)
         close_layer(y[1], 1)

@@ -19,6 +19,7 @@ ACT = mybir.ActivationFunctionType
 P = 128
 HALF = 512
 QUARTER = 256
+STAGE = P - 16
 HALVES = (slice(0, P // 2), slice(P // 2, P))
 LAST = 6
 FOLD = 7
@@ -59,7 +60,7 @@ def tile_list_pnet_mix_res_kernel(
         wd_s = tile([P, 2 * N], U8, "wd_s")
         wd8_s, wd4_s = wd_s[:, 0:N], wd_s[:, N : 2 * N]
         nc.vector.memset(wc_s[:].bitcast(I32), 0)
-        nc.vector.memset(table_s[:].bitcast(I32), 0)
+        nc.vector.memset(table_s[0:STAGE, :].bitcast(I32), 0)
         nc.vector.memset(picked_s[:].bitcast(I32), 0)
         nc.vector.memset(wd_s[:].bitcast(I32), 0)
 
@@ -72,17 +73,17 @@ def tile_list_pnet_mix_res_kernel(
         wd4_w = tile([P, 2 * N], U8, "wd4_w")
         res_sb = tile([P, 2, J], F32, "res_sb")
 
-        load_scale_rows(nc.sync, wc_s, wc_scales[0])
-        nc.sync.dma_start(out=table_s[0:P:8, :].bitcast(I32), in_=tab_scales[0].bitcast(I32))
+        nc.sync.dma_start(out=table_s[STAGE:P, :].bitcast(I32), in_=tab_scales[0].bitcast(I32))
         nc.sync.dma_start(out=table_w[:], in_=tab_words[0].rearrange("p t i -> p (t i)").bitcast(I32))
         for q in range(2):
             nc.sync.dma_start(out=w_raw[q][:], in_=w_k[:, :, QUARTER * q : QUARTER * (q + 1)])
         nc.sync.dma_start(out=c_raw[0][:], in_=c_k[:, :, 0:QUARTER])
 
+        load_scale_rows(nc.scalar, wc_s, wc_scales[0])
         gathered_s = tile([P, G * J], U8, "gathered_s")
         nc.vector.tensor_copy(gathered_s[:], table_s[:].indirect(offsets[:]))
         for r in range(4):
-            nc.sync.dma_start(out=picked_s[r:P:32, :].bitcast(I32), in_=gathered_s[8 * r : P : 32, :].bitcast(I32))
+            nc.sync.dma_start(out=picked_s[r:P:32, :].bitcast(I32), in_=gathered_s[STAGE + r : P : 4, :].bitcast(I32))
         nc.sync.dma_start(out=wc_w[:].bitcast(I32), in_=wc_words[0].bitcast(I32))
         nc.sync.dma_start(out=w_raw[2][:], in_=w_k[:, :, QUARTER * 2 : QUARTER * 3])
         nc.sync.dma_start(out=c_raw[1][:], in_=c_k[:, :, QUARTER:J])

@@ -41,6 +41,7 @@ def tile_list_pnet_mix_res_kernel(
         on_wc = ctx.enter_context(tc.tile_pool(name="on_wc", bufs=1))
         on_last = ctx.enter_context(tc.tile_pool(name="on_last", bufs=1))
         on_w_raw3 = ctx.enter_context(tc.tile_pool(name="on_w_raw3", bufs=1))
+        on_h = ctx.enter_context(tc.tile_pool(name="on_h", bufs=1))
         psum = ctx.enter_context(tc.psum_pool(name="psum", bufs=1))
 
         def tile(shape, dtype, name, pool=keep, offset=None):
@@ -160,28 +161,41 @@ def tile_list_pnet_mix_res_kernel(
 
         used_banks = []
 
-        def next_bank(shape):
-            used_banks.append(shape)
-            return psum.tile(shape, F32, name="bank", tag=f"bank{len(used_banks) % 8}")
+        def next_bank(shape, back=None):
+            if back is None:
+                used_banks.append(shape)
+            return psum.tile(shape, F32, name="bank", tag=f"bank{(len(used_banks) - (back or 0)) % 8}")
 
         first = [None if u in (2, 3) else tile([P, P, 4], F32, f"first{u}") for u in range(FOLD)]
-        best = [None if u == 5 else tile([P, P, 4], F32, f"best{u}") for u in range(LAST)]
-        best.append(tile([P, P, 4], F32, "best6"))
-        best[5] = tile([P, P, 4], F32, "best5", on_last, 0)
+        best = [tile([P, P, 4], F32, f"best{u}") for u in range(FOLD)]
+        last = [tile([P, P // 2, 4], F32, f"last{k}", on_last, 2048 * k) for k in range(2)]
         second2 = tile([P, P, 4], F32, "second2", on_w_raw3, 0)
         own = [tile([P, P, 4], F32, "own0", on_w_raw, 4096 * 2), tile([P, P, 4], F32, "own1", on_w_raw3, 4096)]
         own = own + [tile([P, P, 4], F32, f"own{u}") for u in range(2, LAST)]
         first[2] = tile([P, P, 4], F32, "first2", on_w_raw, 4096 * 2 + 2048)
         first[3] = tile([P, P, 4], F32, "first3", on_w_raw3, 2048)
         pre = [tile([P, P, 4], BF16, f"pre{u}", on_w_bf1, 1024 * u) for u in range(2)]
-        pre = pre + [tile([P, P, 4], BF16, f"pre{u}") for u in range(2, 4)]
-        pre_late = tile([P, 3, P, 4], BF16, "pre_late")
-        pre = pre + [pre_late[:, k, :, :] for k in range(3)]
-        h_bf = [tile([P, 4, P, 4], BF16, f"h_bf{h}") for h in range(2)]
+        pre = pre + [tile([P, P, 4], BF16, f"pre{u}") for u in range(2, 5)]
+        pre_last = tile([P, 2, P, 4], BF16, "pre_last", on_h, 0)
+        pre = pre + [pre_last[:, 0, :, :], pre_last[:, 1, :, :]]
+        h_bf = [tile([P, 2, P, 4], BF16, "h_bf0", on_h, 0), tile([P, 2, P, 4], BF16, "h_bf1")]
+        h_bf.append(tile([P, 4, P, 4], BF16, "h_bf2"))
         folded = tile([P, G, P, 4], BF16, "folded")
         pair_max = tile([P, 2, P, 4], BF16, "pair_max")
-        h_codes = [tile([P, J], U32, "h_codes0", on_last, 0), tile([P, J], U32, "h_codes1")]
+        h_codes = [tile([P, QUARTER], U32, "h_codes0"), tile([P, QUARTER], U32, "h_codes1", on_last, 0)]
+        h_codes.append(tile([P, J], U32, "h_codes2", on_last, 2048))
         h_sc = [tile([P, J], U8, f"h_sc{h}") for h in range(2)]
+
+        def place(u):
+            return (u // 2, u % 2) if u < 4 else (2, u - 4)
+
+        def codes_of(u, n=1):
+            part, k = place(u)
+            return h_codes[part][:, k * P : (k + n) * P].bitcast(E4)
+
+        def values_of(u, n=1):
+            part, k = place(u)
+            return h_bf[part][:, k : k + n, :, :]
 
         def own_pass(bank, u, t, start):
             h, cols = u // 4, slice(u % 4 * P, (u % 4 + 1) * P)
@@ -217,8 +231,9 @@ def tile_list_pnet_mix_res_kernel(
             elif g == 0:
                 nc.scalar.copy(first[u][:], woven)
             elif u == LAST and g > 1:
-                for cols in HALVES:
-                    nc.vector.tensor_tensor(best[u][:, cols, :], best[u][:, cols, :], woven[:, cols, :], ALU.max)
+                for k, cols in enumerate(HALVES):
+                    dst = best[u][:, cols, :] if g == 2 else last[k][:]
+                    nc.vector.tensor_tensor(dst, best[u][:, cols, :], woven[:, cols, :], ALU.max)
             else:
                 steps = [first[u], best[u], second2 if u == 2 else best[u], best[u]]
                 nc.vector.tensor_tensor(steps[g][:], steps[g - 1][:], woven, ALU.max)
@@ -236,16 +251,52 @@ def tile_list_pnet_mix_res_kernel(
             nc.gpsimd.tensor_tensor(pre[u][:], best[u][:], own[u][:], ALU.add)
 
         def relu(u):
-            nc.scalar.activation(h_bf[u // 4][:, u % 4, :, :], pre[u][:], ACT.Relu)
+            nc.scalar.activation(values_of(u)[:, 0, :, :], pre[u][:], ACT.Relu)
 
         def quantize_h(u, n=1):
             h, jt = u // 4, u % 4
             cols = slice(jt * P, (jt + n) * P)
             nc.vector.quantize_mx(
-                out=h_codes[h][:, cols].bitcast(E4),
+                out=codes_of(u, n),
                 scales=h_sc[h][:, cols],
-                in_=h_bf[h][:, jt : jt + n, :, :].rearrange("p u j t -> p (u j t)"),
+                in_=values_of(u, n).rearrange("p u j t -> p (u j t)"),
             )
+
+        out_v = out.rearrange("(a p) j -> p a j", p=P)
+
+        def open_layer(jt):
+            cols = slice(jt * P, (jt + 1) * P)
+            y = next_bank([P, 2, P], back=(2, 1, 3, 4)[jt])
+            for a in range(2):
+                nc.tensor.matmul_mx(
+                    out=y[:, a, :],
+                    lhsT=wd8_w[:, 4 * P * a : 4 * P * (a + 1)].bitcast(E4),
+                    lhsT_scale=wd8_s[:, P * a : P * (a + 1)],
+                    rhs=codes_of(jt),
+                    rhs_scale=h_sc[0][:, cols],
+                    start=a == 0,
+                    stop=False,
+                )
+            return y
+
+        def close_layer(y, jt):
+            cols = slice(jt * P, (jt + 1) * P)
+            for a in range(2):
+                nc.tensor.matmul_mx(
+                    out=y[:, a, :],
+                    lhsT=wd4_w[:, 2 * P * a : 2 * P * (a + 1)].bitcast(E2),
+                    lhsT_scale=wd4_s[:, P * a : P * (a + 1)],
+                    rhs=codes_of(4 + jt),
+                    rhs_scale=h_sc[1][:, cols],
+                    start=False,
+                    stop=a == 1,
+                )
+
+        def finish(y, jt):
+            cols = slice(jt * P, (jt + 1) * P)
+            o = tile([P, 2, P], F32, f"o{jt}")
+            nc.vector.tensor_tensor(o[:], res_sb[:, :, cols], y[:], ALU.add)
+            nc.sync.dma_start(out=out_v[:, :, cols], in_=o[:])
 
         neighbour(0, 0)
         neighbour(1, 0)
@@ -292,64 +343,29 @@ def tile_list_pnet_mix_res_kernel(
         neighbour(6, 1)
         neighbour(FOLD, 0)
         neighbour(5, 3)
+        quantize_h(0, 2)
         add_own(5)
         relu(3)
         neighbour(FOLD, 1)
         neighbour(6, 2)
+        neighbour(FOLD, 2)
         neighbour(6, 3)
         last_own = own_bank(LAST)
-        for cols in HALVES:
-            nc.vector.tensor_tensor(pre[LAST][:, cols, :], best[LAST][:, cols, :], last_own[:, cols, :], ALU.add)
-        neighbour(FOLD, 2)
+        for k, cols in enumerate(HALVES):
+            nc.vector.tensor_tensor(pre[LAST][:, cols, :], last[k][:], last_own[:, cols, :], ALU.add)
+        relu(4)
         neighbour(FOLD, 3)
 
-        out_v = out.rearrange("(a p) j -> p a j", p=P)
-
-        def open_layer(jt):
-            cols = slice(jt * P, (jt + 1) * P)
-            y = next_bank([P, 2, P])
-            for a in range(2):
-                nc.tensor.matmul_mx(
-                    out=y[:, a, :],
-                    lhsT=wd8_w[:, 4 * P * a : 4 * P * (a + 1)].bitcast(E4),
-                    lhsT_scale=wd8_s[:, P * a : P * (a + 1)],
-                    rhs=h_codes[0][:, cols].bitcast(E4),
-                    rhs_scale=h_sc[0][:, cols],
-                    start=a == 0,
-                    stop=False,
-                )
-            return y
-
-        def close_layer(y, jt):
-            cols = slice(jt * P, (jt + 1) * P)
-            for a in range(2):
-                nc.tensor.matmul_mx(
-                    out=y[:, a, :],
-                    lhsT=wd4_w[:, 2 * P * a : 2 * P * (a + 1)].bitcast(E2),
-                    lhsT_scale=wd4_s[:, P * a : P * (a + 1)],
-                    rhs=h_codes[1][:, cols].bitcast(E4),
-                    rhs_scale=h_sc[1][:, cols],
-                    start=False,
-                    stop=a == 1,
-                )
-
-        def finish(y, jt):
-            cols = slice(jt * P, (jt + 1) * P)
-            o = tile([P, 2, P], F32, f"o{jt}")
-            nc.vector.tensor_tensor(o[:], res_sb[:, :, cols], y[:], ALU.add)
-            nc.sync.dma_start(out=out_v[:, :, cols], in_=o[:])
-
-        nc.vector.tensor_scalar_max(h_bf[1][:, 0:2, :, :], pre_late[:, 0:2, :, :], 0.0)
-        quantize_h(0, 4)
+        quantize_h(2, 2)
         y = [open_layer(jt) for jt in range(4)]
         quantize_h(4)
         close_layer(y[0], 0)
-        nc.vector.tensor_scalar_max(h_bf[1][:, 2, :, :], pre[LAST], 0.0)
+        nc.vector.tensor_scalar_max(values_of(5, 2), pre_last[:], 0.0)
         nc.vector.tensor_tensor(pair_max[:], folded[:, 0:2, :, :], folded[:, 2:4, :, :], ALU.max)
         quantize_h(5, 2)
         close_layer(y[1], 1)
         close_layer(y[2], 2)
-        nc.vector.tensor_tensor(h_bf[1][:, 3, :, :], pair_max[:, 0, :, :], pair_max[:, 1, :, :], ALU.max)
+        nc.vector.tensor_tensor(values_of(FOLD)[:, 0, :, :], pair_max[:, 0, :, :], pair_max[:, 1, :, :], ALU.max)
         finish(y[0], 0)
         quantize_h(FOLD)
         close_layer(y[3], 3)

@@ -30,6 +30,11 @@ def load_scale_rows(queue, plane, rows):
         queue.dma_start(out=plane[r:P:32, :].bitcast(I32), in_=rows[r:16:4, :].bitcast(I32))
 
 
+def carry_scale_rows(queue, plane, staged):
+    for r in range(4):
+        queue.dma_start(out=plane[r:P:32, :].bitcast(I32), in_=staged[STAGE + r : P : 4, :].bitcast(I32))
+
+
 def tile_list_pnet_mix_res_kernel(
     tc, tab_words, tab_scales, c, w, wc_words, wc_scales, wd8_words, wd8_scales, wd4_words, wd4_scales, res, offs, out
 ):
@@ -56,12 +61,14 @@ def tile_list_pnet_mix_res_kernel(
         nc.sync.dma_start(offsets[:], offs)
 
         wc_s = tile([P, R], U8, "wc_s")
+        wcp_s = tile([P, R], U8, "wcp_s")
         table_s = tile([P, T], U8, "table_s")
         picked_s = tile([P, G * J], U8, "picked_s")
         wd_s = tile([P, 2 * N], U8, "wd_s")
         wd8_s, wd4_s = wd_s[:, 0:N], wd_s[:, N : 2 * N]
-        nc.vector.memset(wc_s[:].bitcast(I32), 0)
+        nc.vector.memset(wc_s[0:STAGE, :].bitcast(I32), 0)
         nc.vector.memset(table_s[0:STAGE, :].bitcast(I32), 0)
+        nc.vector.memset(wcp_s[:].bitcast(I32), 0)
         nc.vector.memset(picked_s[:].bitcast(I32), 0)
         nc.vector.memset(wd_s[:].bitcast(I32), 0)
 
@@ -74,17 +81,22 @@ def tile_list_pnet_mix_res_kernel(
         wd4_w = tile([P, 2 * N], U8, "wd4_w")
         res_sb = tile([P, 2, J], F32, "res_sb")
 
+        nc.sync.dma_start(out=wc_s[STAGE:P, :].bitcast(I32), in_=wc_scales[0].bitcast(I32))
         nc.sync.dma_start(out=table_s[STAGE:P, :].bitcast(I32), in_=tab_scales[0].bitcast(I32))
         nc.sync.dma_start(out=table_w[:], in_=tab_words[0].rearrange("p t i -> p (t i)").bitcast(I32))
         for q in range(2):
             nc.sync.dma_start(out=w_raw[q][:], in_=w_k[:, :, QUARTER * q : QUARTER * (q + 1)])
         nc.sync.dma_start(out=c_raw[0][:], in_=c_k[:, :, 0:QUARTER])
 
-        load_scale_rows(nc.scalar, wc_s, wc_scales[0])
+        dealt_s = tile([P, R], U8, "dealt_s")
+        nc.vector.tensor_copy(
+            dealt_s[:].rearrange("p (h t m) -> p h t m", h=2, t=4),
+            wc_s[:].rearrange("p (h m t) -> p h t m", h=2, t=4),
+        )
+        carry_scale_rows(nc.scalar, wcp_s, dealt_s)
         gathered_s = tile([P, G * J], U8, "gathered_s")
         nc.vector.tensor_copy(gathered_s[:], table_s[:].indirect(offsets[:]))
-        for r in range(4):
-            nc.sync.dma_start(out=picked_s[r:P:32, :].bitcast(I32), in_=gathered_s[STAGE + r : P : 4, :].bitcast(I32))
+        carry_scale_rows(nc.sync, picked_s, gathered_s)
         nc.sync.dma_start(out=wc_w[:].bitcast(I32), in_=wc_words[0].bitcast(I32))
         nc.sync.dma_start(out=w_raw[2][:], in_=w_k[:, :, QUARTER * 2 : QUARTER * 3])
         nc.sync.dma_start(out=c_raw[1][:], in_=c_k[:, :, QUARTER:J])
@@ -112,11 +124,11 @@ def tile_list_pnet_mix_res_kernel(
 
         picked_w = []
 
-        def gather_words(g, dst):
-            picked_w.append(dst)
+        def gather_words(g, n, dst):
+            picked_w.extend(dst[:, J * k : J * (k + 1)] for k in range(n))
             nc.vector.tensor_copy(
                 dst[:].bitcast(U32),
-                table_w[:].bitcast(U32).indirect(offsets[:, g * (J // 16) : (g + 1) * (J // 16)]),
+                table_w[:].bitcast(U32).indirect(offsets[:, g * (J // 16) : (g + n) * (J // 16)]),
             )
 
         c_codes = tile([P, J], U32, "c_codes")
@@ -129,8 +141,7 @@ def tile_list_pnet_mix_res_kernel(
                 in_=c_bf[:].rearrange("p j i -> p (j i)"),
             )
 
-        for g in range(G - 1):
-            gather_words(g, tile([P, J], I32, f"picked_w{g}"))
+        gather_words(0, G - 1, tile([P, (G - 1) * J], I32, "picked_w0"))
         for q in range(2):
             cast_w(0, q)
             for t in range(4):
@@ -140,16 +151,11 @@ def tile_list_pnet_mix_res_kernel(
                     scales=w_sc[0][:, cols],
                     in_=w_bf[0][:, t, 64 * q : 64 * (q + 1), :].rearrange("p m i -> p (m i)"),
                 )
-        gather_words(G - 1, tile([P, J], I32, "picked_w3", on_w_raw, 4096))
+        gather_words(G - 1, 1, tile([P, J], I32, "picked_w3", on_w_raw, 4096))
         wcp_w = tile([P, 2 * R], U8, "wcp_w")
         nc.vector.tensor_copy(
             wcp_w[:].bitcast(U16).rearrange("p (h t m) -> p h t m", h=2, t=4),
             wc_w[:].bitcast(U16).rearrange("p (h m t) -> p h t m", h=2, t=4),
-        )
-        wcp_s = tile([P, R], U8, "wcp_s")
-        nc.vector.tensor_copy(
-            wcp_s[:].rearrange("p (h t m) -> p h t m", h=2, t=4),
-            wc_s[:].rearrange("p (h m t) -> p h t m", h=2, t=4),
         )
         c_bf0 = tile([P, QUARTER, 4], BF16, "c_bf0")
         nc.scalar.copy(

@@ -302,7 +302,8 @@ def tile_list_pnet_mix_res_kernel(
             cols = slice(jt * P, (jt + 1) * P)
             o = tile([P, 2, P], F32, f"o{jt}")
             nc.vector.tensor_tensor(o[:], res_sb[:, :, cols], y[:], ALU.add)
-            nc.sync.dma_start(out=out_v[:, :, cols], in_=o[:])
+            for a, queue in enumerate((nc.sync, nc.scalar)):
+                queue.dma_start(out=out_v[:, a, cols], in_=o[:, a, :])
 
         neighbour(0, 0)
         neighbour(1, 0)

@@ -51,8 +51,8 @@ def tile_list_pnet_mix_res_kernel(
 
         def tile(shape, dtype, name, pool=keep, offset=None):
             if offset is None:
-                return pool.tile(shape, dtype, name=name, align_bytes=64)
-            return pool.tile(shape, dtype, name=name, align_bytes=64, offset=offset)
+                return pool.tile(shape, dtype, name=name, align_bytes=256)
+            return pool.tile(shape, dtype, name=name, align_bytes=256, offset=offset)
 
         w_k = w.rearrange("(p i) r -> p i r", i=4)
         c_k = c.rearrange("(p i) j -> p i j", i=4)

@@ -84,16 +84,16 @@ def tile_list_pnet_mix_res_kernel(
         nc.sync.dma_start(out=wc_s[STAGE:P, :].bitcast(I32), in_=wc_scales[0].bitcast(I32))
         nc.sync.dma_start(out=table_s[STAGE:P, :].bitcast(I32), in_=tab_scales[0].bitcast(I32))
         nc.sync.dma_start(out=table_w[:], in_=tab_words[0].rearrange("p t i -> p (t i)").bitcast(I32))
-        for q in range(2):
-            nc.sync.dma_start(out=w_raw[q][:], in_=w_k[:, :, QUARTER * q : QUARTER * (q + 1)])
-        nc.sync.dma_start(out=c_raw[0][:], in_=c_k[:, :, 0:QUARTER])
-
         dealt_s = tile([P, R], U8, "dealt_s")
         nc.vector.tensor_copy(
             dealt_s[:].rearrange("p (h t m) -> p h t m", h=2, t=4),
             wc_s[:].rearrange("p (h m t) -> p h t m", h=2, t=4),
         )
-        carry_scale_rows(nc.scalar, wcp_s, dealt_s)
+        carry_scale_rows(nc.sync, wcp_s, dealt_s)
+        for q in range(2):
+            nc.sync.dma_start(out=w_raw[q][:], in_=w_k[:, :, QUARTER * q : QUARTER * (q + 1)])
+        nc.sync.dma_start(out=c_raw[0][:], in_=c_k[:, :, 0:QUARTER])
+
         gathered_s = tile([P, G * J], U8, "gathered_s")
         nc.vector.tensor_copy(gathered_s[:], table_s[:].indirect(offsets[:]))
         carry_scale_rows(nc.sync, picked_s, gathered_s)

@@ -272,7 +272,7 @@ def tile_list_pnet_mix_res_kernel(
 
         def open_layer(jt):
             cols = slice(jt * P, (jt + 1) * P)
-            y = next_bank([P, 2, P], back=(2, 1, 3, 4)[jt])
+            y = next_bank([P, 2, P], back=(5, 4, 3, 2)[jt])
             for a in range(2):
                 nc.tensor.matmul_mx(
                     out=y[:, a, :],
@@ -314,23 +314,23 @@ def tile_list_pnet_mix_res_kernel(
         neighbour(2, 0)
         neighbour(1, 2)
         neighbour(0, 3)
-        quantize_c(1, c_bf1)
         own_part(0)
         cast_w(1, 1)
         neighbour(2, 1)
         neighbour(3, 0)
         neighbour(1, 3)
         own_part(1)
+        quantize_c(1, c_bf1)
         quantize_w(1)
         add_own(0)
         add_own(1)
         neighbour(2, 2)
         neighbour(3, 1)
-        own_part(2)
-        neighbour(4, 0)
         neighbour(2, 3)
         neighbour(3, 2)
+        own_part(2)
         add_own(2)
+        neighbour(4, 0)
         own_part(3)
         neighbour(4, 1)
         neighbour(5, 0)
@@ -353,14 +353,14 @@ def tile_list_pnet_mix_res_kernel(
         quantize_h(0, 2)
         add_own(5)
         relu(3)
-        neighbour(FOLD, 1)
         neighbour(6, 2)
-        neighbour(FOLD, 2)
+        neighbour(FOLD, 1)
         neighbour(6, 3)
         last_own = own_bank(LAST)
         for k, cols in enumerate(HALVES):
             nc.vector.tensor_tensor(pre[LAST][:, cols, :], last[k][:], last_own[:, cols, :], ALU.add)
         relu(4)
+        neighbour(FOLD, 2)
         neighbour(FOLD, 3)
 
         quantize_h(2, 2)

@@ -22,6 +22,9 @@ QUARTER = 256
 STAGE = P - 16
 HALVES = (slice(0, P // 2), slice(P // 2, P))
 LAST = 6
+OWN = 4
+EARLY = 12
+AHEAD = 48
 FOLD = 7
 
 
@@ -46,6 +49,8 @@ def tile_list_pnet_mix_res_kernel(
         on_wc = ctx.enter_context(tc.tile_pool(name="on_wc", bufs=1))
         on_last = ctx.enter_context(tc.tile_pool(name="on_last", bufs=1))
         on_w_raw3 = ctx.enter_context(tc.tile_pool(name="on_w_raw3", bufs=1))
+        on_c_raw1 = ctx.enter_context(tc.tile_pool(name="on_c_raw1", bufs=1))
+        on_add5 = ctx.enter_context(tc.tile_pool(name="on_add5", bufs=1))
         on_h = ctx.enter_context(tc.tile_pool(name="on_h", bufs=1))
         psum = ctx.enter_context(tc.psum_pool(name="psum", bufs=1))
 
@@ -76,7 +81,7 @@ def tile_list_pnet_mix_res_kernel(
         table_w = tile([P, T], I32, "table_w")
         w_raw = [tile([P, 4, QUARTER], F32, f"w_raw{q}", on_w_raw, 4096 * q) for q in range(3)]
         w_raw.append(tile([P, 4, QUARTER], F32, "w_raw3", on_w_raw3, 1024))
-        c_raw = [tile([P, 4, QUARTER], F32, f"c_raw{q}") for q in range(2)]
+        c_raw = [tile([P, 4, QUARTER], F32, "c_raw0"), tile([P, 4, QUARTER], F32, "c_raw1", on_c_raw1, 0)]
         wd8_w = tile([P, 4 * N], U8, "wd8_w")
         wd4_w = tile([P, 2 * N], U8, "wd4_w")
         res_sb = tile([P, 2, J], F32, "res_sb")
@@ -122,13 +127,14 @@ def tile_list_pnet_mix_res_kernel(
                 out=w_codes[h][:].bitcast(E4), scales=w_sc[h][:], in_=w_bf[h][:].rearrange("p t m i -> p (t m i)")
             )
 
-        picked_w = []
+        picked_w, picked_pair = [], []
 
-        def gather_words(g, n, dst):
-            picked_w.extend(dst[:, J * k : J * (k + 1)] for k in range(n))
+        def gather_words(first, n, dst):
+            picked_w.extend(dst[:, P * k : P * (k + 1)] for k in range(n))
+            picked_pair.extend(dst[:, 2 * P * k : 2 * P * (k + 1)] for k in range(n // 2))
             nc.vector.tensor_copy(
                 dst[:].bitcast(U32),
-                table_w[:].bitcast(U32).indirect(offsets[:, g * (J // 16) : (g + n) * (J // 16)]),
+                table_w[:].bitcast(U32).indirect(offsets[:, first * (P // 16) : (first + n) * (P // 16)]),
             )
 
         c_codes = tile([P, J], U32, "c_codes")
@@ -141,7 +147,7 @@ def tile_list_pnet_mix_res_kernel(
                 in_=c_bf[:].rearrange("p j i -> p (j i)"),
             )
 
-        gather_words(0, G - 1, tile([P, (G - 1) * J], I32, "picked_w0"))
+        gather_words(0, EARLY, tile([P, EARLY * P], I32, "picked_w0"))
         for q in range(2):
             cast_w(0, q)
             for t in range(4):
@@ -151,7 +157,7 @@ def tile_list_pnet_mix_res_kernel(
                     scales=w_sc[0][:, cols],
                     in_=w_bf[0][:, t, 64 * q : 64 * (q + 1), :].rearrange("p m i -> p (m i)"),
                 )
-        gather_words(G - 1, 1, tile([P, J], I32, "picked_w3", on_w_raw, 4096))
+        gather_words(EARLY, 16 - EARLY, tile([P, (16 - EARLY) * P], I32, "picked_w3", on_w_raw, 4096))
         wcp_w = tile([P, 2 * R], U8, "wcp_w")
         nc.vector.tensor_copy(
             wcp_w[:].bitcast(U16).rearrange("p (h t m) -> p h t m", h=2, t=4),
@@ -165,35 +171,36 @@ def tile_list_pnet_mix_res_kernel(
         c_bf1 = tile([P, QUARTER, 4], BF16, "c_bf1", on_wc, 0)
         nc.gpsimd.tensor_scalar(c_bf1[:], c_raw[1][:].rearrange("p i j -> p j i"), 1.0, 0.0, ALU.mult, ALU.add)
 
-        used_banks = []
+        free_banks = list(range(8))
 
-        def next_bank(shape, back=None):
-            if back is None:
-                used_banks.append(shape)
-            return psum.tile(shape, F32, name="bank", tag=f"bank{(len(used_banks) - (back or 0)) % 8}")
+        def take_bank(shape):
+            k = free_banks.pop(0)
+            return k, psum.tile(shape, F32, name="bank", tag=f"bank{k}")
 
         first = [None if u in (2, 3) else tile([P, P, 4], F32, f"first{u}") for u in range(FOLD)]
-        best = [tile([P, P, 4], F32, f"best{u}") for u in range(FOLD)]
+        best = [tile([P, P, 4], F32, f"best{u}") for u in range(FOLD) if u != 5]
+        best = best[0:5] + [tile([P, P, 4], F32, "best5", on_add5, 4096), best[5]]
         last = [tile([P, P // 2, 4], F32, f"last{k}", on_last, 2048 * k) for k in range(2)]
+        pre_ahead = tile([P, AHEAD, 4], BF16, "pre_ahead", on_c_raw1, 0)
+        best_pair = [tile([P, 2, 2 * P, 2], F32, f"best_pair{k}") for k in range(2)]
         second2 = tile([P, P, 4], F32, "second2", on_w_raw3, 0)
         own = [tile([P, P, 4], F32, "own0", on_w_raw, 4096 * 2), tile([P, P, 4], F32, "own1", on_w_raw3, 4096)]
-        own = own + [tile([P, P, 4], F32, f"own{u}") for u in range(2, LAST)]
+        own = own + [tile([P, P, 4], F32, f"own{u}") for u in range(2, 5)]
+        own.append(tile([P, P, 4], F32, "own5", on_add5, 0))
         first[2] = tile([P, P, 4], F32, "first2", on_w_raw, 4096 * 2 + 2048)
         first[3] = tile([P, P, 4], F32, "first3", on_w_raw3, 2048)
         pre = [tile([P, P, 4], BF16, f"pre{u}", on_w_bf1, 1024 * u) for u in range(2)]
         pre = pre + [tile([P, P, 4], BF16, f"pre{u}") for u in range(2, 5)]
         pre_last = tile([P, 2, P, 4], BF16, "pre_last", on_h, 0)
         pre = pre + [pre_last[:, 0, :, :], pre_last[:, 1, :, :]]
-        h_bf = [tile([P, 2, P, 4], BF16, "h_bf0", on_h, 0), tile([P, 2, P, 4], BF16, "h_bf1")]
-        h_bf.append(tile([P, 4, P, 4], BF16, "h_bf2"))
+        h_bf = [tile([P, 2, P, 4], BF16, "h_bf0", on_h, 0), tile([P, 6, P, 4], BF16, "h_bf1")]
         folded = tile([P, G, P, 4], BF16, "folded")
-        pair_max = tile([P, 2, P, 4], BF16, "pair_max")
-        h_codes = [tile([P, QUARTER], U32, "h_codes0"), tile([P, QUARTER], U32, "h_codes1", on_last, 0)]
-        h_codes.append(tile([P, J], U32, "h_codes2", on_last, 2048))
-        h_sc = [tile([P, J], U8, f"h_sc{h}") for h in range(2)]
+        pair_max = tile([P, 2, P, 4], BF16, "pair_max", on_add5, 4096)
+        h_codes = [tile([P, QUARTER], U32, "h_codes0"), tile([P, 6 * P], U32, "h_codes1", on_add5, 0)]
+        h_sc = tile([P, 2 * J], U8, "h_sc")
 
         def place(u):
-            return (u // 2, u % 2) if u < 4 else (2, u - 4)
+            return (0, u) if u < 2 else (1, u - 2)
 
         def codes_of(u, n=1):
             part, k = place(u)
@@ -216,55 +223,106 @@ def tile_list_pnet_mix_res_kernel(
                 stop=True,
             )
 
-        def neighbour(u, g):
+        filled = {}
+
+        def fill(u, g):
             h, j0 = u // 4, u % 4 * P
-            bank = next_bank([P, 4, P])
+            if u < 4 and g != OWN:
+                k, bank = take_bank([P, 2, 2 * P])
+                j0 = u // 2 * 2 * P
+                for n in range(2):
+                    t = u % 2 * 2 + n
+                    nc.tensor.matmul_mx(
+                        out=bank[:, n, :],
+                        lhsT=w_codes[0][:, P * t : P * (t + 1)].bitcast(E4),
+                        lhsT_scale=w_sc[0][:, P * t : P * (t + 1)],
+                        rhs=picked_pair[2 * g + u // 2].bitcast(E4),
+                        rhs_scale=picked_s[:, g * J + j0 : g * J + j0 + 2 * P],
+                        start=True,
+                        stop=True,
+                    )
+                filled[u, g] = k, bank[:].rearrange("p t j -> p j t")
+                return
+            k, bank = take_bank([P, 4, P])
             for t in range(4):
-                nc.tensor.matmul_mx(
-                    out=bank[:, t, :],
-                    lhsT=w_codes[h][:, P * t : P * (t + 1)].bitcast(E4),
-                    lhsT_scale=w_sc[h][:, P * t : P * (t + 1)],
-                    rhs=picked_w[g][:, j0 : j0 + P].bitcast(E4),
-                    rhs_scale=picked_s[:, g * J + j0 : g * J + j0 + P],
-                    start=True,
-                    stop=u != FOLD,
-                )
-                if u == FOLD:
-                    own_pass(bank, u, t, False)
-            woven = bank[:].rearrange("p t j -> p j t")
+                if g != OWN:
+                    nc.tensor.matmul_mx(
+                        out=bank[:, t, :],
+                        lhsT=w_codes[h][:, P * t : P * (t + 1)].bitcast(E4),
+                        lhsT_scale=w_sc[h][:, P * t : P * (t + 1)],
+                        rhs=picked_w[4 * g + u % 4].bitcast(E4),
+                        rhs_scale=picked_s[:, g * J + j0 : g * J + j0 + P],
+                        start=True,
+                        stop=u != FOLD,
+                    )
+                if g == OWN or u == FOLD:
+                    own_pass(bank, u, t, g == OWN)
+            filled[u, g] = k, bank[:].rearrange("p t j -> p j t")
+
+        quantized = {"w0", "c0"}
+
+        def needs(u, g):
+            need = set()
+            if g != OWN:
+                need.add(f"w{u // 4}")
+            if g == OWN or u == FOLD:
+                need.add(f"c{u % 4 // 2}")
+            return need
+
+        def refill():
+            while waiting and free_banks and all(x in quantized for x in needs(*waiting[0])):
+                fill(*waiting.pop(0))
+
+        def paired(sums):
+            return sums[:].rearrange("p j (s t) -> p (j s) t", s=2)
+
+        def read(u, g):
+            k, woven = filled[u, g]
             if u == FOLD:
                 nc.scalar.activation(folded[:, g, :, :], woven, ACT.Relu)
+            elif u == LAST and g > 1:
+                for n, cols in enumerate(HALVES):
+                    if g == OWN:
+                        nc.vector.tensor_tensor(pre[u][:, cols, :], last[n][:], woven[:, cols, :], ALU.add)
+                    else:
+                        dst = best[u][:, cols, :] if g == 2 else last[n][:]
+                        nc.vector.tensor_tensor(dst, best[u][:, cols, :], woven[:, cols, :], ALU.max)
+            elif g == OWN:
+                nc.scalar.copy(own[u][:], woven)
+            elif u < 4:
+                mine = best_pair[u // 2][:, u % 2, :, :]
+                steps = [paired(first[u]), mine, paired(second2) if u == 2 else mine, mine]
+                if g == 0:
+                    nc.scalar.copy(steps[0], woven)
+                else:
+                    nc.vector.tensor_tensor(steps[g], steps[g - 1], woven, ALU.max)
             elif g == 0:
                 nc.scalar.copy(first[u][:], woven)
-            elif u == LAST and g > 1:
-                for k, cols in enumerate(HALVES):
-                    dst = best[u][:, cols, :] if g == 2 else last[k][:]
-                    nc.vector.tensor_tensor(dst, best[u][:, cols, :], woven[:, cols, :], ALU.max)
             else:
-                steps = [first[u], best[u], second2 if u == 2 else best[u], best[u]]
-                nc.vector.tensor_tensor(steps[g][:], steps[g - 1][:], woven, ALU.max)
+                nc.vector.tensor_tensor(best[u][:], (first if g == 1 else best)[u][:], woven, ALU.max)
+            free_banks.append(k)
+            refill()
 
-        def own_bank(u):
-            bank = next_bank([P, 4, P])
-            for t in range(4):
-                own_pass(bank, u, t, True)
-            return bank[:].rearrange("p t j -> p j t")
-
-        def own_part(u):
-            nc.scalar.copy(own[u][:], own_bank(u))
-
-        def add_own(u):
-            nc.gpsimd.tensor_tensor(pre[u][:], best[u][:], own[u][:], ALU.add)
+        def add_own(u, dst=None, points=slice(0, P)):
+            if u < 4:
+                pairs = best_pair[u // 2][:].rearrange("p s j t -> p j s t")[:, P * (u % 2) : P * (u % 2 + 1), :, :]
+                split = "p j (s t) -> p j s t"
+                nc.gpsimd.tensor_tensor(
+                    (pre[u] if dst is None else dst)[:, points, :].rearrange(split, s=2),
+                    pairs[:, points, :, :],
+                    own[u][:, points, :].rearrange(split, s=2),
+                    ALU.add,
+                )
+            else:
+                nc.gpsimd.tensor_tensor(pre[u][:], best[u][:], own[u][:], ALU.add)
 
         def relu(u):
             nc.scalar.activation(values_of(u)[:, 0, :, :], pre[u][:], ACT.Relu)
 
         def quantize_h(u, n=1):
-            h, jt = u // 4, u % 4
-            cols = slice(jt * P, (jt + n) * P)
             nc.vector.quantize_mx(
                 out=codes_of(u, n),
-                scales=h_sc[h][:, cols],
+                scales=h_sc[:, u * P : (u + n) * P],
                 in_=values_of(u, n).rearrange("p u j t -> p (u j t)"),
             )
 
@@ -272,28 +330,27 @@ def tile_list_pnet_mix_res_kernel(
 
         def open_layer(jt):
             cols = slice(jt * P, (jt + 1) * P)
-            y = next_bank([P, 2, P], back=(5, 4, 3, 2)[jt])
+            y = psum.tile([P, 2, P], F32, name="bank", tag=f"bank{free_banks[(4, 5, 3, 2)[jt]]}")
             for a in range(2):
                 nc.tensor.matmul_mx(
                     out=y[:, a, :],
                     lhsT=wd8_w[:, 4 * P * a : 4 * P * (a + 1)].bitcast(E4),
                     lhsT_scale=wd8_s[:, P * a : P * (a + 1)],
                     rhs=codes_of(jt),
-                    rhs_scale=h_sc[0][:, cols],
+                    rhs_scale=h_sc[:, cols],
                     start=a == 0,
                     stop=False,
                 )
             return y
 
         def close_layer(y, jt):
-            cols = slice(jt * P, (jt + 1) * P)
             for a in range(2):
                 nc.tensor.matmul_mx(
                     out=y[:, a, :],
                     lhsT=wd4_w[:, 2 * P * a : 2 * P * (a + 1)].bitcast(E2),
                     lhsT_scale=wd4_s[:, P * a : P * (a + 1)],
                     rhs=codes_of(4 + jt),
-                    rhs_scale=h_sc[1][:, cols],
+                    rhs_scale=h_sc[:, J + jt * P : J + (jt + 1) * P],
                     start=False,
                     stop=a == 1,
                 )
@@ -305,67 +362,73 @@ def tile_list_pnet_mix_res_kernel(
             for a, queue in enumerate((nc.sync, nc.scalar)):
                 queue.dma_start(out=out_v[:, a, cols], in_=o[:, a, :])
 
-        neighbour(0, 0)
-        neighbour(1, 0)
-        neighbour(0, 1)
-        neighbour(1, 1)
+        waiting = [(0, 0), (1, 0), (0, 1), (1, 1), (0, 2), (1, 2), (2, 0), (0, 3), (1, 3), (0, OWN), (2, 1), (3, 0)]
+        waiting.extend([(1, OWN), (3, 1), (2, 2), (3, 2), (2, 3), (3, 3), (2, OWN), (4, 0), (3, OWN), (5, 0)])
+        waiting.extend([(4, 1), (5, 1), (4, 2), (4, OWN), (5, 2), (6, 0), (4, 3), (5, OWN), (6, 1)])
+        waiting.extend([(7, 0), (5, 3), (6, 2), (7, 1), (6, 3), (6, OWN), (7, 2), (7, 3)])
+        refill()
+        read(0, 0)
+        read(1, 0)
         cast_w(1, 0)
-        neighbour(0, 2)
-        neighbour(2, 0)
-        neighbour(1, 2)
-        neighbour(0, 3)
-        own_part(0)
+        read(0, 1)
+        read(1, 1)
+        read(0, 2)
+        read(2, 0)
+        read(1, 2)
+        read(0, 3)
+        read(0, OWN)
         cast_w(1, 1)
-        neighbour(2, 1)
-        neighbour(3, 0)
-        neighbour(1, 3)
-        own_part(1)
+        read(1, 3)
+        add_own(0, pre_ahead, slice(0, AHEAD))
+        read(2, 1)
         quantize_c(1, c_bf1)
+        quantized.add("c1")
         quantize_w(1)
-        add_own(0)
+        quantized.add("w1")
+        read(3, 0)
+        read(1, OWN)
+        add_own(0, None, slice(AHEAD, P))
         add_own(1)
-        neighbour(2, 2)
-        neighbour(3, 1)
-        neighbour(2, 3)
-        neighbour(3, 2)
-        own_part(2)
+        read(3, 1)
+        read(2, 2)
+        read(3, 2)
+        read(2, 3)
+        read(3, 3)
+        read(2, OWN)
+        read(4, 0)
+        read(3, OWN)
+        read(5, 0)
         add_own(2)
-        neighbour(4, 0)
-        own_part(3)
-        neighbour(4, 1)
-        neighbour(5, 0)
-        neighbour(3, 3)
         add_own(3)
-        relu(0)
-        neighbour(4, 2)
-        own_part(4)
-        neighbour(5, 1)
-        neighbour(6, 0)
+        nc.scalar.activation(values_of(0)[:, 0, 0:AHEAD, :], pre_ahead[:], ACT.Relu)
+        nc.scalar.activation(values_of(0)[:, 0, AHEAD:P, :], pre[0][:, AHEAD:P, :], ACT.Relu)
+        read(4, 1)
+        read(4, OWN)
+        read(5, 1)
         relu(1)
-        neighbour(4, 3)
+        read(4, 2)
+        read(6, 0)
+        read(5, 2)
+        read(5, OWN)
+        read(4, 3)
         add_own(4)
-        own_part(5)
-        neighbour(5, 2)
         relu(2)
-        neighbour(6, 1)
-        neighbour(FOLD, 0)
-        neighbour(5, 3)
+        read(6, 1)
+        read(FOLD, 0)
+        relu(3)
+        read(5, 3)
         quantize_h(0, 2)
         add_own(5)
-        relu(3)
-        neighbour(6, 2)
-        neighbour(FOLD, 1)
-        neighbour(6, 3)
-        last_own = own_bank(LAST)
-        for k, cols in enumerate(HALVES):
-            nc.vector.tensor_tensor(pre[LAST][:, cols, :], last[k][:], last_own[:, cols, :], ALU.add)
+        read(FOLD, 1)
         relu(4)
-        neighbour(FOLD, 2)
-        neighbour(FOLD, 3)
+        read(6, 2)
+        read(6, 3)
+        read(6, OWN)
+        read(FOLD, 2)
+        read(FOLD, 3)
 
-        quantize_h(2, 2)
+        quantize_h(2, 3)
         y = [open_layer(jt) for jt in range(4)]
-        quantize_h(4)
         close_layer(y[0], 0)
         nc.vector.tensor_scalar_max(values_of(5, 2), pre_last[:], 0.0)
         nc.vector.tensor_tensor(pair_max[:], folded[:, 0:2, :, :], folded[:, 2:4, :, :], ALU.max)

@@ -21,11 +21,13 @@ HALF = 512
 QUARTER = 256
 STAGE = P - 16
 HALVES = (slice(0, P // 2), slice(P // 2, P))
+BANKS = 8
+OWN = G
 LAST = 6
-OWN = 4
+FOLD = 7
+BLOCKS = G * J // P
 EARLY = 12
 AHEAD = 48
-FOLD = 7
 
 
 def load_scale_rows(queue, plane, rows):
@@ -47,7 +49,6 @@ def tile_list_pnet_mix_res_kernel(
         on_w_raw = ctx.enter_context(tc.tile_pool(name="on_w_raw", bufs=1))
         on_w_bf1 = ctx.enter_context(tc.tile_pool(name="on_w_bf1", bufs=1))
         on_wc = ctx.enter_context(tc.tile_pool(name="on_wc", bufs=1))
-        on_last = ctx.enter_context(tc.tile_pool(name="on_last", bufs=1))
         on_w_raw3 = ctx.enter_context(tc.tile_pool(name="on_w_raw3", bufs=1))
         on_c_raw1 = ctx.enter_context(tc.tile_pool(name="on_c_raw1", bufs=1))
         on_add5 = ctx.enter_context(tc.tile_pool(name="on_add5", bufs=1))
@@ -147,7 +148,7 @@ def tile_list_pnet_mix_res_kernel(
                 in_=c_bf[:].rearrange("p j i -> p (j i)"),
             )
 
-        gather_words(0, EARLY, tile([P, EARLY * P], I32, "picked_w0"))
+        gather_words(0, EARLY, tile([P, EARLY * P], I32, "picked_early"))
         for q in range(2):
             cast_w(0, q)
             for t in range(4):
@@ -157,7 +158,7 @@ def tile_list_pnet_mix_res_kernel(
                     scales=w_sc[0][:, cols],
                     in_=w_bf[0][:, t, 64 * q : 64 * (q + 1), :].rearrange("p m i -> p (m i)"),
                 )
-        gather_words(EARLY, 16 - EARLY, tile([P, (16 - EARLY) * P], I32, "picked_w3", on_w_raw, 4096))
+        gather_words(EARLY, BLOCKS - EARLY, tile([P, (BLOCKS - EARLY) * P], I32, "picked_late", on_w_raw, 4096))
         wcp_w = tile([P, 2 * R], U8, "wcp_w")
         nc.vector.tensor_copy(
             wcp_w[:].bitcast(U16).rearrange("p (h t m) -> p h t m", h=2, t=4),
@@ -171,18 +172,17 @@ def tile_list_pnet_mix_res_kernel(
         c_bf1 = tile([P, QUARTER, 4], BF16, "c_bf1", on_wc, 0)
         nc.gpsimd.tensor_scalar(c_bf1[:], c_raw[1][:].rearrange("p i j -> p j i"), 1.0, 0.0, ALU.mult, ALU.add)
 
-        free_banks = list(range(8))
+        free_banks = list(range(BANKS))
 
-        def take_bank(shape):
-            k = free_banks.pop(0)
-            return k, psum.tile(shape, F32, name="bank", tag=f"bank{k}")
+        def bank_tile(shape, k):
+            return psum.tile(shape, F32, name="bank", tag=f"bank{k}")
 
         first = [None if u in (2, 3) else tile([P, P, 4], F32, f"first{u}") for u in range(FOLD)]
-        best = [tile([P, P, 4], F32, f"best{u}") for u in range(FOLD) if u != 5]
+        best = [None if u < 2 else tile([P, P, 4], F32, f"best{u}") for u in range(FOLD) if u != 5]
         best = best[0:5] + [tile([P, P, 4], F32, "best5", on_add5, 4096), best[5]]
-        last = [tile([P, P // 2, 4], F32, f"last{k}", on_last, 2048 * k) for k in range(2)]
+        last = [tile([P, P // 2, 4], F32, f"last{k}") for k in range(2)]
+        best_pair = tile([P, 2, 2 * P, 2], F32, "best_pair")
         pre_ahead = tile([P, AHEAD, 4], BF16, "pre_ahead", on_c_raw1, 0)
-        best_pair = [tile([P, 2, 2 * P, 2], F32, f"best_pair{k}") for k in range(2)]
         second2 = tile([P, P, 4], F32, "second2", on_w_raw3, 0)
         own = [tile([P, P, 4], F32, "own0", on_w_raw, 4096 * 2), tile([P, P, 4], F32, "own1", on_w_raw3, 4096)]
         own = own + [tile([P, P, 4], F32, f"own{u}") for u in range(2, 5)]
@@ -227,23 +227,23 @@ def tile_list_pnet_mix_res_kernel(
 
         def fill(u, g):
             h, j0 = u // 4, u % 4 * P
-            if u < 4 and g != OWN:
-                k, bank = take_bank([P, 2, 2 * P])
-                j0 = u // 2 * 2 * P
+            k = free_banks.pop(0)
+            if u < 2 and g != OWN:
+                bank = bank_tile([P, 2, 2 * P], k)
                 for n in range(2):
-                    t = u % 2 * 2 + n
+                    t = 2 * u + n
                     nc.tensor.matmul_mx(
                         out=bank[:, n, :],
                         lhsT=w_codes[0][:, P * t : P * (t + 1)].bitcast(E4),
                         lhsT_scale=w_sc[0][:, P * t : P * (t + 1)],
-                        rhs=picked_pair[2 * g + u // 2].bitcast(E4),
-                        rhs_scale=picked_s[:, g * J + j0 : g * J + j0 + 2 * P],
+                        rhs=picked_pair[2 * g].bitcast(E4),
+                        rhs_scale=picked_s[:, g * J : g * J + 2 * P],
                         start=True,
                         stop=True,
                     )
                 filled[u, g] = k, bank[:].rearrange("p t j -> p j t")
                 return
-            k, bank = take_bank([P, 4, P])
+            bank = bank_tile([P, 4, P], k)
             for t in range(4):
                 if g != OWN:
                     nc.tensor.matmul_mx(
@@ -259,22 +259,15 @@ def tile_list_pnet_mix_res_kernel(
                     own_pass(bank, u, t, g == OWN)
             filled[u, g] = k, bank[:].rearrange("p t j -> p j t")
 
-        quantized = {"w0", "c0"}
+        w_halves, c_halves = {0}, {0}
 
-        def needs(u, g):
-            need = set()
-            if g != OWN:
-                need.add(f"w{u // 4}")
-            if g == OWN or u == FOLD:
-                need.add(f"c{u % 4 // 2}")
-            return need
+        def ready(u, g):
+            return u // 4 in w_halves and (u % 4 // 2 in c_halves or g != OWN)
 
         def refill():
-            while waiting and free_banks and all(x in quantized for x in needs(*waiting[0])):
-                fill(*waiting.pop(0))
-
-        def paired(sums):
-            return sums[:].rearrange("p j (s t) -> p (j s) t", s=2)
+            for u, g in [x for x in waiting if ready(*x)][: len(free_banks)]:
+                waiting.remove((u, g))
+                fill(u, g)
 
         def read(u, g):
             k, woven = filled[u, g]
@@ -287,37 +280,40 @@ def tile_list_pnet_mix_res_kernel(
                     else:
                         dst = best[u][:, cols, :] if g == 2 else last[n][:]
                         nc.vector.tensor_tensor(dst, best[u][:, cols, :], woven[:, cols, :], ALU.max)
-            elif g == OWN:
-                nc.scalar.copy(own[u][:], woven)
-            elif u < 4:
-                mine = best_pair[u // 2][:, u % 2, :, :]
-                steps = [paired(first[u]), mine, paired(second2) if u == 2 else mine, mine]
+            elif u < 2 and g != OWN:
+                start = first[u][:].rearrange("p j (s t) -> p (j s) t", s=2)
                 if g == 0:
-                    nc.scalar.copy(steps[0], woven)
+                    nc.scalar.copy(start, woven)
                 else:
-                    nc.vector.tensor_tensor(steps[g], steps[g - 1], woven, ALU.max)
-            elif g == 0:
-                nc.scalar.copy(first[u][:], woven)
+                    mine = best_pair[:, u, :, :]
+                    nc.vector.tensor_tensor(mine, start if g == 1 else mine, woven, ALU.max)
+            elif g in (0, OWN):
+                nc.scalar.copy((first if g == 0 else own)[u][:], woven)
             else:
-                nc.vector.tensor_tensor(best[u][:], (first if g == 1 else best)[u][:], woven, ALU.max)
+                steps = [first[u], best[u], second2 if u == 2 else best[u], best[u]]
+                nc.vector.tensor_tensor(steps[g][:], steps[g - 1][:], woven, ALU.max)
             free_banks.append(k)
             refill()
 
-        def add_own(u, dst=None, points=slice(0, P)):
-            if u < 4:
-                pairs = best_pair[u // 2][:].rearrange("p s j t -> p j s t")[:, P * (u % 2) : P * (u % 2 + 1), :, :]
+        def parts(u):
+            if u == 0:
+                return [(pre_ahead[:], slice(0, AHEAD)), (pre[0][:, AHEAD:P, :], slice(AHEAD, P))]
+            return [(pre[u][:], slice(0, P))]
+
+        def add_own(u, part=0):
+            dst, points = parts(u)[part]
+            if u < 2:
                 split = "p j (s t) -> p j s t"
+                pairs = best_pair[:].rearrange("p s j t -> p j s t")[:, P * u : P * (u + 1), :, :][:, points, :, :]
                 nc.gpsimd.tensor_tensor(
-                    (pre[u] if dst is None else dst)[:, points, :].rearrange(split, s=2),
-                    pairs[:, points, :, :],
-                    own[u][:, points, :].rearrange(split, s=2),
-                    ALU.add,
+                    dst.rearrange(split, s=2), pairs, own[u][:, points, :].rearrange(split, s=2), ALU.add
                 )
             else:
-                nc.gpsimd.tensor_tensor(pre[u][:], best[u][:], own[u][:], ALU.add)
+                nc.gpsimd.tensor_tensor(dst, best[u][:, points, :], own[u][:, points, :], ALU.add)
 
         def relu(u):
-            nc.scalar.activation(values_of(u)[:, 0, :, :], pre[u][:], ACT.Relu)
+            for src, points in parts(u):
+                nc.scalar.activation(values_of(u)[:, 0, points, :], src, ACT.Relu)
 
         def quantize_h(u, n=1):
             nc.vector.quantize_mx(
@@ -330,7 +326,7 @@ def tile_list_pnet_mix_res_kernel(
 
         def open_layer(jt):
             cols = slice(jt * P, (jt + 1) * P)
-            y = psum.tile([P, 2, P], F32, name="bank", tag=f"bank{free_banks[(4, 5, 3, 2)[jt]]}")
+            y = bank_tile([P, 2, P], filled[late_banks[jt]][0])
             for a in range(2):
                 nc.tensor.matmul_mx(
                     out=y[:, a, :],
@@ -362,10 +358,13 @@ def tile_list_pnet_mix_res_kernel(
             for a, queue in enumerate((nc.sync, nc.scalar)):
                 queue.dma_start(out=out_v[:, a, cols], in_=o[:, a, :])
 
-        waiting = [(0, 0), (1, 0), (0, 1), (1, 1), (0, 2), (1, 2), (2, 0), (0, 3), (1, 3), (0, OWN), (2, 1), (3, 0)]
-        waiting.extend([(1, OWN), (3, 1), (2, 2), (3, 2), (2, 3), (3, 3), (2, OWN), (4, 0), (3, OWN), (5, 0)])
-        waiting.extend([(4, 1), (5, 1), (4, 2), (4, OWN), (5, 2), (6, 0), (4, 3), (5, OWN), (6, 1)])
-        waiting.extend([(7, 0), (5, 3), (6, 2), (7, 1), (6, 3), (6, OWN), (7, 2), (7, 3)])
+        waiting = [(u, g) for g in range(2) for u in range(2)] + [(0, 2), (1, 2), (2, 0), (0, 3), (1, 3), (0, OWN)]
+        waiting.extend([(2, 1), (3, 0), (1, OWN), (3, 1), (2, 2), (2, OWN), (4, 0), (3, 2), (2, 3), (3, OWN)])
+        for u in range(4, FOLD):
+            waiting.extend([(u, 1), (u + 1, 0), (u - 1, 3)] + [(u, OWN)] * (u < LAST) + [(u, 2)])
+        waiting.extend([(FOLD, 1), (LAST, 3), (LAST, OWN), (FOLD, 2), (FOLD, 3)])
+        late_banks = [(LAST, 3), (LAST, OWN), (LAST, 2), (FOLD, 1)]
+
         refill()
         read(0, 0)
         read(1, 0)
@@ -379,51 +378,40 @@ def tile_list_pnet_mix_res_kernel(
         read(0, OWN)
         cast_w(1, 1)
         read(1, 3)
-        add_own(0, pre_ahead, slice(0, AHEAD))
+        add_own(0)
         read(2, 1)
         quantize_c(1, c_bf1)
-        quantized.add("c1")
+        c_halves.add(1)
         quantize_w(1)
-        quantized.add("w1")
+        w_halves.add(1)
         read(3, 0)
         read(1, OWN)
-        add_own(0, None, slice(AHEAD, P))
+        add_own(0, 1)
         add_own(1)
         read(3, 1)
-        read(2, 2)
-        read(3, 2)
-        read(2, 3)
-        read(3, 3)
         read(2, OWN)
+        read(2, 2)
         read(4, 0)
+        read(3, 2)
         read(3, OWN)
-        read(5, 0)
+        read(2, 3)
         add_own(2)
-        add_own(3)
-        nc.scalar.activation(values_of(0)[:, 0, 0:AHEAD, :], pre_ahead[:], ACT.Relu)
-        nc.scalar.activation(values_of(0)[:, 0, AHEAD:P, :], pre[0][:, AHEAD:P, :], ACT.Relu)
-        read(4, 1)
-        read(4, OWN)
-        read(5, 1)
-        relu(1)
-        read(4, 2)
-        read(6, 0)
-        read(5, 2)
-        read(5, OWN)
-        read(4, 3)
-        add_own(4)
-        relu(2)
-        read(6, 1)
-        read(FOLD, 0)
-        relu(3)
-        read(5, 3)
-        quantize_h(0, 2)
-        add_own(5)
-        read(FOLD, 1)
+        read(5, 0)
+        relu(0)
+        for u in range(4, FOLD):
+            read(u, 1)
+            read(u - 1, 3)
+            if u == LAST:
+                quantize_h(0, 2)
+            add_own(u - 1)
+            if u < LAST:
+                read(u, OWN)
+            read(u, 2)
+            read(min(u + 2, FOLD), max(u + 2 - FOLD, 0))
+            relu(u - 3)
         relu(4)
-        read(6, 2)
-        read(6, 3)
-        read(6, OWN)
+        read(LAST, 3)
+        read(LAST, OWN)
         read(FOLD, 2)
         read(FOLD, 3)
 

from contextlib import ExitStack

import concourse.mybir as mybir

K, R, N, T, J, G = 512, 1024, 256, 4096, 512, 4
FLOPS = 2 * K * R * J * (G + 1) + 2 * R * N * J

F32 = mybir.dt.float32
BF16 = mybir.dt.bfloat16
I32 = mybir.dt.int32
U32 = mybir.dt.uint32
U16 = mybir.dt.uint16
U8 = mybir.dt.uint8
E4 = mybir.dt.float8_e4m3fn_x4
E2 = mybir.dt.float4_e2m1fn_x4
ALU = mybir.AluOpType
ACT = mybir.ActivationFunctionType

P = 128
HALF = 512
QUARTER = 256
STAGE = P - 16
HALVES = (slice(0, P // 2), slice(P // 2, P))
BANKS = 8
OWN = G
LAST = 6
FOLD = 7
BLOCKS = G * J // P
EARLY = 12
AHEAD = 48


def load_scale_rows(queue, plane, rows):
    for r in range(4):
        queue.dma_start(out=plane[r:P:32, :].bitcast(I32), in_=rows[r:16:4, :].bitcast(I32))


def carry_scale_rows(queue, plane, staged):
    for r in range(4):
        queue.dma_start(out=plane[r:P:32, :].bitcast(I32), in_=staged[STAGE + r : P : 4, :].bitcast(I32))


def tile_list_pnet_mix_res_kernel(
    tc, tab_words, tab_scales, c, w, wc_words, wc_scales, wd8_words, wd8_scales, wd4_words, wd4_scales, res, offs, out
):
    nc = tc.nc
    with ExitStack() as ctx:
        keep = ctx.enter_context(tc.tile_pool(name="keep", bufs=1))
        on_w_raw = ctx.enter_context(tc.tile_pool(name="on_w_raw", bufs=1))
        on_w_bf1 = ctx.enter_context(tc.tile_pool(name="on_w_bf1", bufs=1))
        on_wc = ctx.enter_context(tc.tile_pool(name="on_wc", bufs=1))
        on_w_raw3 = ctx.enter_context(tc.tile_pool(name="on_w_raw3", bufs=1))
        on_c_raw1 = ctx.enter_context(tc.tile_pool(name="on_c_raw1", bufs=1))
        on_add5 = ctx.enter_context(tc.tile_pool(name="on_add5", bufs=1))
        on_h = ctx.enter_context(tc.tile_pool(name="on_h", bufs=1))
        psum = ctx.enter_context(tc.psum_pool(name="psum", bufs=1))

        def tile(shape, dtype, name, pool=keep, offset=None):
            if offset is None:
                return pool.tile(shape, dtype, name=name, align_bytes=256)
            return pool.tile(shape, dtype, name=name, align_bytes=256, offset=offset)

        w_k = w.rearrange("(p i) r -> p i r", i=4)
        c_k = c.rearrange("(p i) j -> p i j", i=4)

        offsets = keep.tile([P, G * J // 16], U16, name="offsets")
        nc.sync.dma_start(offsets[:], offs)

        wc_s = tile([P, R], U8, "wc_s")
        wcp_s = tile([P, R], U8, "wcp_s")
        table_s = tile([P, T], U8, "table_s")
        picked_s = tile([P, G * J], U8, "picked_s")
        wd_s = tile([P, 2 * N], U8, "wd_s")
        wd8_s, wd4_s = wd_s[:, 0:N], wd_s[:, N : 2 * N]
        nc.vector.memset(wc_s[0:STAGE, :].bitcast(I32), 0)
        nc.vector.memset(table_s[0:STAGE, :].bitcast(I32), 0)
        nc.vector.memset(wcp_s[:].bitcast(I32), 0)
        nc.vector.memset(picked_s[:].bitcast(I32), 0)
        nc.vector.memset(wd_s[:].bitcast(I32), 0)

        wc_w = tile([P, 2 * R], U8, "wc_w", on_wc, 0)
        table_w = tile([P, T], I32, "table_w")
        w_raw = [tile([P, 4, QUARTER], F32, f"w_raw{q}", on_w_raw, 4096 * q) for q in range(3)]
        w_raw.append(tile([P, 4, QUARTER], F32, "w_raw3", on_w_raw3, 1024))
        c_raw = [tile([P, 4, QUARTER], F32, "c_raw0"), tile([P, 4, QUARTER], F32, "c_raw1", on_c_raw1, 0)]
        wd8_w = tile([P, 4 * N], U8, "wd8_w")
        wd4_w = tile([P, 2 * N], U8, "wd4_w")
        res_sb = tile([P, 2, J], F32, "res_sb")

        nc.sync.dma_start(out=wc_s[STAGE:P, :].bitcast(I32), in_=wc_scales[0].bitcast(I32))
        nc.sync.dma_start(out=table_s[STAGE:P, :].bitcast(I32), in_=tab_scales[0].bitcast(I32))
        nc.sync.dma_start(out=table_w[:], in_=tab_words[0].rearrange("p t i -> p (t i)").bitcast(I32))
        dealt_s = tile([P, R], U8, "dealt_s")
        nc.vector.tensor_copy(
            dealt_s[:].rearrange("p (h t m) -> p h t m", h=2, t=4),
            wc_s[:].rearrange("p (h m t) -> p h t m", h=2, t=4),
        )
        carry_scale_rows(nc.sync, wcp_s, dealt_s)
        for q in range(2):
            nc.sync.dma_start(out=w_raw[q][:], in_=w_k[:, :, QUARTER * q : QUARTER * (q + 1)])
        nc.sync.dma_start(out=c_raw[0][:], in_=c_k[:, :, 0:QUARTER])

        gathered_s = tile([P, G * J], U8, "gathered_s")
        nc.vector.tensor_copy(gathered_s[:], table_s[:].indirect(offsets[:]))
        carry_scale_rows(nc.sync, picked_s, gathered_s)
        nc.sync.dma_start(out=wc_w[:].bitcast(I32), in_=wc_words[0].bitcast(I32))
        nc.sync.dma_start(out=w_raw[2][:], in_=w_k[:, :, QUARTER * 2 : QUARTER * 3])
        nc.sync.dma_start(out=c_raw[1][:], in_=c_k[:, :, QUARTER:J])
        nc.sync.dma_start(out=w_raw[3][:], in_=w_k[:, :, QUARTER * 3 : R])
        nc.sync.dma_start(out=wd8_w[:].bitcast(I32), in_=wd8_words[0].rearrange("p n i -> p (n i)").bitcast(I32))
        nc.sync.dma_start(out=wd4_w[:].bitcast(I32), in_=wd4_words[0].bitcast(I32))
        load_scale_rows(nc.sync, wd8_s, wd8_scales[0])
        load_scale_rows(nc.sync, wd4_s, wd4_scales[0])
        nc.sync.dma_start(out=res_sb[:], in_=res.rearrange("(a p) j -> p a j", p=P))

        w_bf = [tile([P, 4, P, 4], BF16, "w_bf0"), tile([P, 4, P, 4], BF16, "w_bf1", on_w_bf1, 0)]
        w_codes = [tile([P, HALF], U32, f"w_codes{h}") for h in range(2)]
        w_sc = [tile([P, HALF], U8, f"w_sc{h}") for h in range(2)]

        def cast_w(h, q):
            nc.scalar.copy(
                w_bf[h][:, :, 64 * q : 64 * (q + 1), :].rearrange("p t m i -> p m i t"),
                w_raw[2 * h + q][:].rearrange("p i (m t) -> p m i t", t=4),
            )

        def quantize_w(h):
            nc.vector.quantize_mx(
                out=w_codes[h][:].bitcast(E4), scales=w_sc[h][:], in_=w_bf[h][:].rearrange("p t m i -> p (t m i)")
            )

        picked_w, picked_pair = [], []

        def gather_words(first, n, dst):
            picked_w.extend(dst[:, P * k : P * (k + 1)] for k in range(n))
            picked_pair.extend(dst[:, 2 * P * k : 2 * P * (k + 1)] for k in range(n // 2))
            nc.vector.tensor_copy(
                dst[:].bitcast(U32),
                table_w[:].bitcast(U32).indirect(offsets[:, first * (P // 16) : (first + n) * (P // 16)]),
            )

        c_codes = tile([P, J], U32, "c_codes")
        c_sc = tile([P, J], U8, "c_sc")

        def quantize_c(q, c_bf):
            nc.vector.quantize_mx(
                out=c_codes[:, QUARTER * q : QUARTER * (q + 1)].bitcast(E4),
                scales=c_sc[:, QUARTER * q : QUARTER * (q + 1)],
                in_=c_bf[:].rearrange("p j i -> p (j i)"),
            )

        gather_words(0, EARLY, tile([P, EARLY * P], I32, "picked_early"))
        for q in range(2):
            cast_w(0, q)
            for t in range(4):
                cols = slice(P * t + 64 * q, P * t + 64 * (q + 1))
                nc.vector.quantize_mx(
                    out=w_codes[0][:, cols].bitcast(E4),
                    scales=w_sc[0][:, cols],
                    in_=w_bf[0][:, t, 64 * q : 64 * (q + 1), :].rearrange("p m i -> p (m i)"),
                )
        gather_words(EARLY, BLOCKS - EARLY, tile([P, (BLOCKS - EARLY) * P], I32, "picked_late", on_w_raw, 4096))
        wcp_w = tile([P, 2 * R], U8, "wcp_w")
        nc.vector.tensor_copy(
            wcp_w[:].bitcast(U16).rearrange("p (h t m) -> p h t m", h=2, t=4),
            wc_w[:].bitcast(U16).rearrange("p (h m t) -> p h t m", h=2, t=4),
        )
        c_bf0 = tile([P, QUARTER, 4], BF16, "c_bf0")
        nc.scalar.copy(
            c_bf0[:].rearrange("p (a b) i -> p a i b", b=4), c_raw[0][:].rearrange("p i (a b) -> p a i b", b=4)
        )
        quantize_c(0, c_bf0)
        c_bf1 = tile([P, QUARTER, 4], BF16, "c_bf1", on_wc, 0)
        nc.gpsimd.tensor_scalar(c_bf1[:], c_raw[1][:].rearrange("p i j -> p j i"), 1.0, 0.0, ALU.mult, ALU.add)

        free_banks = list(range(BANKS))

        def bank_tile(shape, k):
            return psum.tile(shape, F32, name="bank", tag=f"bank{k}")

        first = [None if u in (2, 3) else tile([P, P, 4], F32, f"first{u}") for u in range(FOLD)]
        best = [None if u < 2 else tile([P, P, 4], F32, f"best{u}") for u in range(FOLD) if u != 5]
        best = best[0:5] + [tile([P, P, 4], F32, "best5", on_add5, 4096), best[5]]
        last = [tile([P, P // 2, 4], F32, f"last{k}") for k in range(2)]
        best_pair = tile([P, 2, 2 * P, 2], F32, "best_pair")
        pre_ahead = tile([P, AHEAD, 4], BF16, "pre_ahead", on_c_raw1, 0)
        second2 = tile([P, P, 4], F32, "second2", on_w_raw3, 0)
        own = [tile([P, P, 4], F32, "own0", on_w_raw, 4096 * 2), tile([P, P, 4], F32, "own1", on_w_raw3, 4096)]
        own = own + [tile([P, P, 4], F32, f"own{u}") for u in range(2, 5)]
        own.append(tile([P, P, 4], F32, "own5", on_add5, 0))
        first[2] = tile([P, P, 4], F32, "first2", on_w_raw, 4096 * 2 + 2048)
        first[3] = tile([P, P, 4], F32, "first3", on_w_raw3, 2048)
        pre = [tile([P, P, 4], BF16, f"pre{u}", on_w_bf1, 1024 * u) for u in range(2)]
        pre = pre + [tile([P, P, 4], BF16, f"pre{u}") for u in range(2, 5)]
        pre_last = tile([P, 2, P, 4], BF16, "pre_last", on_h, 0)
        pre = pre + [pre_last[:, 0, :, :], pre_last[:, 1, :, :]]
        h_bf = [tile([P, 2, P, 4], BF16, "h_bf0", on_h, 0), tile([P, 6, P, 4], BF16, "h_bf1")]
        folded = tile([P, G, P, 4], BF16, "folded")
        pair_max = tile([P, 2, P, 4], BF16, "pair_max", on_add5, 4096)
        h_codes = [tile([P, QUARTER], U32, "h_codes0"), tile([P, 6 * P], U32, "h_codes1", on_add5, 0)]
        h_sc = tile([P, 2 * J], U8, "h_sc")

        def place(u):
            return (0, u) if u < 2 else (1, u - 2)

        def codes_of(u, n=1):
            part, k = place(u)
            return h_codes[part][:, k * P : (k + n) * P].bitcast(E4)

        def values_of(u, n=1):
            part, k = place(u)
            return h_bf[part][:, k : k + n, :, :]

        def own_pass(bank, u, t, start):
            h, cols = u // 4, slice(u % 4 * P, (u % 4 + 1) * P)
            r0 = HALF * h + P * t
            nc.tensor.matmul_mx(
                out=bank[:, t, :],
                lhsT=wcp_w[:, 2 * r0 : 2 * (r0 + P)].bitcast(E2),
                lhsT_scale=wcp_s[:, r0 : r0 + P],
                rhs=c_codes[:, cols].bitcast(E4),
                rhs_scale=c_sc[:, cols],
                start=start,
                stop=True,
            )

        filled = {}

        def fill(u, g):
            h, j0 = u // 4, u % 4 * P
            k = free_banks.pop(0)
            if u < 2 and g != OWN:
                bank = bank_tile([P, 2, 2 * P], k)
                for n in range(2):
                    t = 2 * u + n
                    nc.tensor.matmul_mx(
                        out=bank[:, n, :],
                        lhsT=w_codes[0][:, P * t : P * (t + 1)].bitcast(E4),
                        lhsT_scale=w_sc[0][:, P * t : P * (t + 1)],
                        rhs=picked_pair[2 * g].bitcast(E4),
                        rhs_scale=picked_s[:, g * J : g * J + 2 * P],
                        start=True,
                        stop=True,
                    )
                filled[u, g] = k, bank[:].rearrange("p t j -> p j t")
                return
            bank = bank_tile([P, 4, P], k)
            for t in range(4):
                if g != OWN:
                    nc.tensor.matmul_mx(
                        out=bank[:, t, :],
                        lhsT=w_codes[h][:, P * t : P * (t + 1)].bitcast(E4),
                        lhsT_scale=w_sc[h][:, P * t : P * (t + 1)],
                        rhs=picked_w[4 * g + u % 4].bitcast(E4),
                        rhs_scale=picked_s[:, g * J + j0 : g * J + j0 + P],
                        start=True,
                        stop=u != FOLD,
                    )
                if g == OWN or u == FOLD:
                    own_pass(bank, u, t, g == OWN)
            filled[u, g] = k, bank[:].rearrange("p t j -> p j t")

        w_halves, c_halves = {0}, {0}

        def ready(u, g):
            return u // 4 in w_halves and (u % 4 // 2 in c_halves or g != OWN)

        def refill():
            for u, g in [x for x in waiting if ready(*x)][: len(free_banks)]:
                waiting.remove((u, g))
                fill(u, g)

        def read(u, g):
            k, woven = filled[u, g]
            if u == FOLD:
                nc.scalar.activation(folded[:, g, :, :], woven, ACT.Relu)
            elif u == LAST and g > 1:
                for n, cols in enumerate(HALVES):
                    if g == OWN:
                        nc.vector.tensor_tensor(pre[u][:, cols, :], last[n][:], woven[:, cols, :], ALU.add)
                    else:
                        dst = best[u][:, cols, :] if g == 2 else last[n][:]
                        nc.vector.tensor_tensor(dst, best[u][:, cols, :], woven[:, cols, :], ALU.max)
            elif u < 2 and g != OWN:
                start = first[u][:].rearrange("p j (s t) -> p (j s) t", s=2)
                if g == 0:
                    nc.scalar.copy(start, woven)
                else:
                    mine = best_pair[:, u, :, :]
                    nc.vector.tensor_tensor(mine, start if g == 1 else mine, woven, ALU.max)
            elif g in (0, OWN):
                nc.scalar.copy((first if g == 0 else own)[u][:], woven)
            else:
                steps = [first[u], best[u], second2 if u == 2 else best[u], best[u]]
                nc.vector.tensor_tensor(steps[g][:], steps[g - 1][:], woven, ALU.max)
            free_banks.append(k)
            refill()

        def parts(u):
            if u == 0:
                return [(pre_ahead[:], slice(0, AHEAD)), (pre[0][:, AHEAD:P, :], slice(AHEAD, P))]
            return [(pre[u][:], slice(0, P))]

        def add_own(u, part=0):
            dst, points = parts(u)[part]
            if u < 2:
                split = "p j (s t) -> p j s t"
                pairs = best_pair[:].rearrange("p s j t -> p j s t")[:, P * u : P * (u + 1), :, :][:, points, :, :]
                nc.gpsimd.tensor_tensor(
                    dst.rearrange(split, s=2), pairs, own[u][:, points, :].rearrange(split, s=2), ALU.add
                )
            else:
                nc.gpsimd.tensor_tensor(dst, best[u][:, points, :], own[u][:, points, :], ALU.add)

        def relu(u):
            for src, points in parts(u):
                nc.scalar.activation(values_of(u)[:, 0, points, :], src, ACT.Relu)

        def quantize_h(u, n=1):
            nc.vector.quantize_mx(
                out=codes_of(u, n),
                scales=h_sc[:, u * P : (u + n) * P],
                in_=values_of(u, n).rearrange("p u j t -> p (u j t)"),
            )

        out_v = out.rearrange("(a p) j -> p a j", p=P)

        def open_layer(jt):
            cols = slice(jt * P, (jt + 1) * P)
            y = bank_tile([P, 2, P], filled[late_banks[jt]][0])
            for a in range(2):
                nc.tensor.matmul_mx(
                    out=y[:, a, :],
                    lhsT=wd8_w[:, 4 * P * a : 4 * P * (a + 1)].bitcast(E4),
                    lhsT_scale=wd8_s[:, P * a : P * (a + 1)],
                    rhs=codes_of(jt),
                    rhs_scale=h_sc[:, cols],
                    start=a == 0,
                    stop=False,
                )
            return y

        def close_layer(y, jt):
            for a in range(2):
                nc.tensor.matmul_mx(
                    out=y[:, a, :],
                    lhsT=wd4_w[:, 2 * P * a : 2 * P * (a + 1)].bitcast(E2),
                    lhsT_scale=wd4_s[:, P * a : P * (a + 1)],
                    rhs=codes_of(4 + jt),
                    rhs_scale=h_sc[:, J + jt * P : J + (jt + 1) * P],
                    start=False,
                    stop=a == 1,
                )

        def finish(y, jt):
            cols = slice(jt * P, (jt + 1) * P)
            o = tile([P, 2, P], F32, f"o{jt}")
            nc.vector.tensor_tensor(o[:], res_sb[:, :, cols], y[:], ALU.add)
            for a, queue in enumerate((nc.sync, nc.scalar)):
                queue.dma_start(out=out_v[:, a, cols], in_=o[:, a, :])

        waiting = [(u, g) for g in range(2) for u in range(2)] + [(0, 2), (1, 2), (2, 0), (0, 3), (1, 3), (0, OWN)]
        waiting.extend([(2, 1), (3, 0), (1, OWN), (3, 1), (2, 2), (2, OWN), (4, 0), (3, 2), (2, 3), (3, OWN)])
        for u in range(4, FOLD):
            waiting.extend([(u, 1), (u + 1, 0), (u - 1, 3)] + [(u, OWN)] * (u < LAST) + [(u, 2)])
        waiting.extend([(FOLD, 1), (LAST, 3), (LAST, OWN), (FOLD, 2), (FOLD, 3)])
        late_banks = [(LAST, 3), (LAST, OWN), (LAST, 2), (FOLD, 1)]

        refill()
        read(0, 0)
        read(1, 0)
        cast_w(1, 0)
        read(0, 1)
        read(1, 1)
        read(0, 2)
        read(2, 0)
        read(1, 2)
        read(0, 3)
        read(0, OWN)
        cast_w(1, 1)
        read(1, 3)
        add_own(0)
        read(2, 1)
        quantize_c(1, c_bf1)
        c_halves.add(1)
        quantize_w(1)
        w_halves.add(1)
        read(3, 0)
        read(1, OWN)
        add_own(0, 1)
        add_own(1)
        read(3, 1)
        read(2, OWN)
        read(2, 2)
        read(4, 0)
        read(3, 2)
        read(3, OWN)
        read(2, 3)
        add_own(2)
        read(5, 0)
        relu(0)
        for u in range(4, FOLD):
            read(u, 1)
            read(u - 1, 3)
            if u == LAST:
                quantize_h(0, 2)
            add_own(u - 1)
            if u < LAST:
                read(u, OWN)
            read(u, 2)
            read(min(u + 2, FOLD), max(u + 2 - FOLD, 0))
            relu(u - 3)
        relu(4)
        read(LAST, 3)
        read(LAST, OWN)
        read(FOLD, 2)
        read(FOLD, 3)

        quantize_h(2, 3)
        y = [open_layer(jt) for jt in range(4)]
        close_layer(y[0], 0)
        nc.vector.tensor_scalar_max(values_of(5, 2), pre_last[:], 0.0)
        nc.vector.tensor_tensor(pair_max[:], folded[:, 0:2, :, :], folded[:, 2:4, :, :], ALU.max)
        quantize_h(5, 2)
        close_layer(y[1], 1)
        close_layer(y[2], 2)
        nc.vector.tensor_tensor(values_of(FOLD)[:, 0, :, :], pair_max[:, 0, :, :], pair_max[:, 1, :, :], ALU.max)
        finish(y[0], 0)
        quantize_h(FOLD)
        close_layer(y[3], 3)
        for jt in (1, 2, 3):
            finish(y[jt], jt)
